import numpy as np
import ml_dtypes


def mxq(x, axis, fmt="e4m3"):
    dtype, down = {"e4m3": (ml_dtypes.float8_e4m3fn, 7), "e5m2": (ml_dtypes.float8_e5m2, 14)}[fmt]
    v = np.moveaxis(np.asarray(x, np.float32).astype(ml_dtypes.bfloat16).astype(np.float64), axis, -1)
    blocks = v.reshape(v.shape[:-1] + (-1, 32))
    amax = np.abs(blocks).max(-1, keepdims=True)
    byte = np.maximum(np.where(amax > 0, np.frexp(amax)[1] - 1 + 127, 0) - down, 1)
    scale = np.exp2(byte - 127.0)
    codes = (blocks / scale).astype(np.float32).astype(dtype).astype(np.float64)
    return np.moveaxis((codes * scale).reshape(v.shape), -1, axis)


WIDE = False


def mx_kscale(k):
    if not WIDE:
        return np.ones(k)
    levels = np.array([10, -10, 5, -5, 0])
    if k % 512:
        return np.exp2(np.random.permutation(np.resize(levels, k // 32))).repeat(32)
    a = np.empty((k // 512, 16))
    for p in range(k // 512):
        a[p, :8] = np.random.permutation(np.resize(levels, 8))
        for g in range(8):
            far = levels[np.abs(levels - a[p, g]) >= 10]
            a[p, g + 8] = far[np.random.randint(len(far))]
    return np.exp2(a.ravel()).repeat(32)


BF16 = ml_dtypes.bfloat16


def bf(x):
    return np.asarray(x, np.float32).astype(BF16)


def f64(x):
    return np.asarray(x).astype(np.float64)


E2M1 = np.array([0.0, 0.5, 1.0, 1.5, 2.0, 3.0, 4.0, 6.0, -0.0, -0.5, -1.0, -1.5, -2.0, -3.0, -4.0, -6.0])


def pack_weight(w, fmt):
    k, n = w.shape
    w = f64(bf(w)).reshape(k // 32, 32, n)
    amax = np.abs(w).max(1)
    if fmt == "e4m3":
        byte = np.frexp(amax)[1] - 1 + 127 - 7
    else:
        mant, ex = np.frexp(amax / 6.0)
        byte = np.where(mant > 0.5, ex, ex - 1) + 127
    byte = np.clip(np.where(amax > 0, byte, 1), 1, 254)
    scaled = (w * np.exp2(127.0 - byte)[:, None, :]).reshape(k, n).astype(np.float32)
    by_word = np.ascontiguousarray(scaled.reshape(k // 512, 128, 4, n).transpose(0, 1, 3, 2))
    if fmt == "e4m3":
        words = by_word.astype(ml_dtypes.float8_e4m3fn).view(np.uint8)
    else:
        c = by_word.astype(ml_dtypes.float4_e2m1fn).view(np.uint8) & 0xF
        words = c[..., 0::2] | (c[..., 1::2] << 4)
    return np.ascontiguousarray(words), np.ascontiguousarray(byte.astype(np.uint8).reshape(k // 512, 16, n))


def unpack_weight(words, scales, fmt):
    g, p, n, _ = words.shape
    if fmt == "e4m3":
        vals = np.ascontiguousarray(words).view(ml_dtypes.float8_e4m3fn).astype(np.float64)
    else:
        nib = np.empty((g, p, n, 4), np.uint8)
        nib[..., 0::2] = words & 0xF
        nib[..., 1::2] = words >> 4
        vals = E2M1[nib]
    vals = vals * np.repeat(np.exp2(scales.astype(np.float64) - 127.0), 8, axis=1)[..., None]
    return vals.transpose(0, 1, 3, 2).reshape(g * 512, n)
def pack4(w):
    words, scales = pack_weight(w, "e2m1")
    return words.reshape(words.shape[0], 128, -1), scales


def unpack4(words, scales):
    return unpack_weight(words.reshape(words.shape[0], 128, -1, 2), scales, "e2m1")


def planes(Y):
    n, m = Y.shape
    b = f64(bf(Y)).reshape(n // 32, 32, m)
    amax = np.abs(b).max(1)
    byte = np.clip(np.where(amax > 0, np.frexp(amax)[1] - 1 + 127 - 7, 1), 1, 254)
    codes = (b * np.exp2(127.0 - byte)[:, None, :]).reshape(n, m).astype(np.float32).astype(ml_dtypes.float8_e4m3fn).view(np.uint8)
    words = codes.reshape(n // 512, 128, 4, m).transpose(0, 1, 3, 2)
    return np.ascontiguousarray(words), np.ascontiguousarray(byte.astype(np.uint8).reshape(n // 512, 16, m))


U, K, R = 1024, 2560, 512
SPREAD, ADAPT, FRAME_STD = 0.8, 0.4, 0.5

def setup_inputs():
    s = mx_kscale(K)[:, None]
    size = np.exp(SPREAD * np.random.randn(R))
    F = np.random.randn(K, U) * s
    T = np.random.randn(K, R) / np.sqrt(K) * size / s
    A = ADAPT * np.random.randn(K, R) / np.sqrt(K) * size / s
    V = np.random.randn(K, R) / np.sqrt(K) / s
    f_words, f_scales = pack_weight(F, "e4m3")
    t_words, t_scales = pack4(T)
    a_words, a_scales = pack_weight(A, "e4m3")
    log_frames = FRAME_STD * np.random.randn(U)
    return {"f_words": f_words, "f_scales": f_scales, "t_words": t_words, "t_scales": t_scales,
            "a_words": a_words, "a_scales": a_scales, "v": bf(V), "log_frames": bf(log_frames)}

def reference(f_words, f_scales, t_words, t_scales, a_words, a_scales, v, log_frames):
    F = unpack_weight(f_words, f_scales, "e4m3")
    T = unpack4(t_words, t_scales)
    A = unpack_weight(a_words, a_scales, "e4m3")
    V = mxq(f64(v), 0, "e4m3")
    est = (F.T @ T) + (F.T @ A)
    z = (F.T @ V) + f64(log_frames)[:, None]
    y = est * (1.0 / (1.0 + np.exp(-z)))
    Y = y.T
    words, scales = planes(Y)
    return y, words, scales

@@ -1,0 +1,270 @@
+from contextlib import ExitStack
+
+import concourse.mybir as mybir
+from concourse.masks import make_identity
+
+U, K, R = 1024, 2560, 512
+FLOPS = 3 * 2 * U * K * R
+
+F32 = mybir.dt.float32
+BF16 = mybir.dt.bfloat16
+I32 = mybir.dt.int32
+U32 = mybir.dt.uint32
+U8 = mybir.dt.uint8
+FP8X4 = mybir.dt.float8_e4m3fn_x4
+FP4X4 = mybir.dt.float4_e2m1fn_x4
+SIGMOID = mybir.ActivationFunctionType.Sigmoid
+MULT = mybir.AluOpType.mult
+
+P = 128
+GROUPS = K // 512
+TILES = U // P
+LAST = TILES - 1
+EARLY_GROUPS = 2
+FIRST_TILES = 4
+A_PLANE = 4
+HELD_GROUPS = 2
+VECTOR_COLS = 320
+WARM_PASSES = 18
+EVACUATED = 2
+
+
+def tile_amortised_ivector_shrinkage_k3_kernel(
+    tc, f_words, f_scales, t_words, t_scales, a_words, a_scales, v, log_frames, out_0, out_1, out_2
+):
+    nc = tc.nc
+    with ExitStack() as ctx:
+        keep = ctx.enter_context(tc.tile_pool(name="keep", bufs=1))
+        ring = ctx.enter_context(tc.tile_pool(name="ring", bufs=3))
+        psum = ctx.enter_context(tc.psum_pool(name="psum", bufs=1))
+        ctx.enter_context(tc.manual_schedule())
+
+        f_codes = keep.tile([P, GROUPS, U], U32, align_bytes=256)
+        t_codes = keep.tile([P, GROUPS, 2 * R], U8, align_bytes=256)
+        a_codes = keep.tile([P, GROUPS, R], U32, align_bytes=256)
+        v_codes = keep.tile([P, GROUPS, R], U32, align_bytes=256)
+        f_plane = keep.tile([P, GROUPS, U], U8, align_bytes=256)
+        t_plane = keep.tile([P, GROUPS, R], U8, align_bytes=256)
+        a_plane = keep.tile([P, GROUPS, R], U8, align_bytes=256)
+        v_plane = keep.tile([P, GROUPS, R], U8, align_bytes=256)
+        v_rows = keep.tile([P, GROUPS, 4, R], BF16, align_bytes=256)
+        frames_rows = keep.tile([P, 32], BF16, align_bytes=64)
+        frames_cols = keep.tile([P, 32], BF16, align_bytes=64)
+        identity = keep.tile([P, P], F32, align_bytes=256)
+        warm_in = keep.tile([P, 4 * P], BF16, align_bytes=256)
+        warm_codes = keep.tile([P, P], U32, align_bytes=256)
+        warm_plane = keep.tile([P, P], U8, align_bytes=256)
+        warm_act = keep.tile([P, 1], F32)
+        est_sb = keep.tile([P, EVACUATED, R], F32, align_bytes=256)
+        y = keep.tile([P, TILES, R], F32, align_bytes=256)
+        y_pairs = keep.tile([P, TILES, 2, P, 2], BF16, align_bytes=256)
+        y_grouped = keep.tile([P, U, 4], BF16, align_bytes=256)
+        y_codes = keep.tile([P, U], U32, align_bytes=256)
+        y_plane = keep.tile([P, U], U8, align_bytes=256)
+
+        def bank(b, shape):
+            return psum.tile(shape, F32, name="bank%d" % b, tag="bank%d" % b)
+
+        def clear(plane, g0, g1):
+            nc.vector.memset(plane[:, g0:g1, :].rearrange("p g n -> p (g n)").bitcast(I32), 0)
+
+        def load_scales(plane, first, scales, g0, g1):
+            rows = scales.rearrange("g (q r) n -> r q g n", r=4)
+            for r in range(4):
+                nc.sync.dma_start(
+                    out=plane[first + r : P : 32, g0:g1, :].bitcast(I32),
+                    in_=rows[r][:, g0:g1, :].bitcast(I32),
+                )
+
+        def load_f(g, n0, n1):
+            src = f_words[g].rearrange("p n t -> p (n t)")[:, 4 * n0 : 4 * n1]
+            nc.sync.dma_start(out=f_codes[:, g, n0:n1].bitcast(I32), in_=src.bitcast(I32))
+
+        def load_t(g):
+            nc.sync.dma_start(out=t_codes[:, g, :].bitcast(I32), in_=t_words[g].bitcast(I32))
+
+        def load_a(g):
+            src = a_words[g].rearrange("p n t -> p (n t)")
+            nc.sync.dma_start(out=a_codes[:, g, :].bitcast(I32), in_=src.bitcast(I32))
+
+        def load_v(g):
+            src = v[512 * g : 512 * (g + 1), :].rearrange("(p t) n -> p t n", t=4)
+            nc.sync.dma_start(out=v_rows[:, g], in_=src)
+
+        def mx_pass(acc, n, g, codes, plane, start, stop):
+            cols = slice(P * n, P * (n + 1))
+            nc.tensor.matmul_mx(
+                out=acc,
+                lhsT=f_codes[:, g, cols].bitcast(FP8X4),
+                lhsT_scale=f_plane[:, g, cols],
+                rhs=codes,
+                rhs_scale=plane,
+                start=start,
+                stop=stop,
+            )
+
+        def t_pass(n, g):
+            mx_pass(est[n][:], n, g, t_codes[:, g, :].bitcast(FP4X4), t_plane[:, g, :], g == 0, False)
+
+        def a_pass(n, g):
+            mx_pass(est[n][:], n, g, a_codes[:, g, :].bitcast(FP8X4), a_plane[A_PLANE:P, g, :],
+                    False, g == GROUPS - 1)
+
+        def quantize_v(g):
+            grouped = ring.tile([P, R, 4], BF16, align_bytes=256, name="v_grouped")
+            src = v_rows[:, g].rearrange("p t n -> p n t")
+            nc.vector.tensor_copy(out=grouped[:, :VECTOR_COLS, :], in_=src[:, :VECTOR_COLS, :])
+            nc.scalar.copy(out=grouped[:, VECTOR_COLS:, :], in_=src[:, VECTOR_COLS:, :])
+            nc.vector.quantize_mx(
+                out=v_codes[:, g, :].bitcast(FP8X4),
+                scales=v_plane[:, g, :],
+                in_=grouped[:].rearrange("p n t -> p (n t)"),
+            )
+
+        def gate(n):
+            z = bank(n % EVACUATED, [P, R])
+            for g in range(GROUPS):
+                mx_pass(z[:], n, g, v_codes[:, g, :].bitcast(FP8X4), v_plane[:, g, :], g == 0, g == GROUPS - 1)
+            sig = ring.tile([P, R], F32, align_bytes=256, name="sig")
+            nc.scalar.activation(out=sig[:], in_=z[:], func=SIGMOID, bias=frames_cols[:, 4 * n : 4 * n + 1])
+            return sig
+
+        def product(n, sig):
+            src = est_sb[:, n, :] if n < EVACUATED else est[n][:]
+            nc.vector.tensor_tensor(out=y[:, n, :], in0=src, in1=sig[:], op=MULT)
+            nc.sync.dma_start(out=out_0[P * n : P * (n + 1), :], in_=y[:, n, :])
+
+        def by_pairs(ap):
+            return ap.rearrange("u (p h e) -> u h p e", h=2, e=2)
+
+        def round_to_pairs(n):
+            nc.vector.tensor_copy(out=y_pairs[:, n], in_=by_pairs(y[:, n, :]))
+
+        def turn(dst, n, h):
+            words = y_pairs[:, n, h].rearrange("u p e -> u (p e)").bitcast(F32)
+            nc.tensor.transpose(dst, words, identity[:])
+
+        def gather(turned, n0, count):
+            dst = y_grouped[:, P * n0 : P * (n0 + count), :].rearrange("p u t -> p (u t)").bitcast(F32)
+            nc.scalar.copy(
+                out=dst.rearrange("p (n u h) -> p n u h", n=count, h=2),
+                in_=turned.rearrange("p n h u -> p n u h"),
+            )
+
+        def quantize_y(n0, n1):
+            cols = slice(P * n0, P * n1)
+            nc.vector.quantize_mx(
+                out=y_codes[:, cols].bitcast(FP8X4),
+                scales=y_plane[:, cols],
+                in_=y_grouped[:, cols, :].rearrange("p u t -> p (u t)"),
+            )
+
+        def store_words(n0, n1):
+            dst = out_1[0].rearrange("p u t -> p (u t)")[:, 4 * P * n0 : 4 * P * n1]
+            nc.sync.dma_start(out=dst.bitcast(I32), in_=y_codes[:, P * n0 : P * n1].bitcast(I32))
+
+        def store_scales(n0, n1, queues):
+            rows = out_2[0].rearrange("(q r) u -> r q u", r=4)
+            for r in range(4):
+                queues[r].dma_start(
+                    out=rows[r][:, P * n0 : P * n1].bitcast(I32),
+                    in_=y_plane[r:P:32, P * n0 : P * n1].bitcast(I32),
+                )
+
+        clear(f_plane, 0, EARLY_GROUPS)
+        clear(t_plane, 0, EARLY_GROUPS)
+        nc.vector.memset(warm_in[:], 1.0)
+        clear(a_plane, 0, GROUPS)
+        nc.vector.quantize_mx(out=warm_codes[:].bitcast(FP8X4), scales=warm_plane[:], in_=warm_in[:])
+        clear(f_plane, EARLY_GROUPS, GROUPS)
+        clear(t_plane, EARLY_GROUPS, GROUPS)
+        nc.vector.memset(frames_rows[:], 0.0)
+        nc.vector.memset(identity[:], 0.0)
+        make_identity(nc, identity[:], nomemset=True)
+        nc.scalar.activation(out=warm_act[:], in_=warm_in[:, 0:1], func=SIGMOID)
+
+        warm = bank(LAST, [P, P])
+        for i in range(WARM_PASSES):
+            nc.tensor.matmul_mx(
+                out=warm[:], lhsT=warm_codes[:].bitcast(FP8X4), lhsT_scale=warm_plane[:],
+                rhs=warm_codes[:].bitcast(FP8X4), rhs_scale=warm_plane[:], start=True, stop=True,
+            )
+
+        load_f(0, 0, P * FIRST_TILES)
+        load_t(0)
+        load_scales(f_plane, 0, f_scales, 0, EARLY_GROUPS)
+        load_scales(t_plane, 0, t_scales, 0, EARLY_GROUPS)
+        load_f(0, P * FIRST_TILES, U)
+        load_a(0)
+        load_scales(a_plane, A_PLANE, a_scales, 0, GROUPS)
+        load_f(1, 0, U)
+        load_t(1)
+        load_a(1)
+        load_scales(f_plane, 0, f_scales, EARLY_GROUPS, GROUPS)
+        load_scales(t_plane, 0, t_scales, EARLY_GROUPS, GROUPS)
+        for g in range(2, GROUPS):
+            load_f(g, 0, U)
+            load_t(g)
+            load_a(g)
+            load_v(g - 2)
+        nc.sync.dma_start(out=frames_rows[0:P:4, :], in_=log_frames.rearrange("(n q j) -> q n j", q=4, j=32))
+        load_v(3)
+        load_v(4)
+
+        est = [bank(n, [P, R]) for n in range(TILES)]
+        for g in range(GROUPS - 1):
+            tiles = range(TILES if g < GROUPS - HELD_GROUPS else LAST)
+            for n in tiles:
+                t_pass(n, g)
+            for n in tiles:
+                a_pass(n, g)
+        for n in range(LAST):
+            t_pass(n, GROUPS - 1)
+            a_pass(n, GROUPS - 1)
+
+        for g in range(GROUPS - 1):
+            quantize_v(g)
+        nc.vector.transpose(frames_cols[:], frames_rows[:])
+        nc.scalar.copy(out=est_sb[:, 0, :], in_=est[0][:])
+        quantize_v(GROUPS - 1)
+        nc.scalar.copy(out=est_sb[:, 1, :], in_=est[1][:])
+
+        for n in range(LAST):
+            sig = gate(n)
+            if n > 0:
+                round_to_pairs(n - 1)
+            product(n, sig)
+        for pair in range(3):
+            turned = bank(EVACUATED + pair, [P, 2, 2, P])
+            for i in range(2):
+                for h in range(2):
+                    turn(turned[:, i, h, :], 2 * pair + i, h)
+            gather(turned[:], 2 * pair, 2)
+        round_to_pairs(LAST - 1)
+        quantize_y(0, 4)
+        store_words(0, 4)
+        quantize_y(4, 6)
+        store_words(4, 6)
+        store_scales(0, 6, [nc.sync] * 4)
+
+        sig = gate(LAST)
+        for g in range(GROUPS - HELD_GROUPS, GROUPS):
+            t_pass(LAST, g)
+            a_pass(LAST, g)
+
+        turned6 = bank(5, [P, 1, 2, P])
+        for h in range(2):
+            turn(turned6[:, 0, h, :], LAST - 1, h)
+        gather(turned6[:], LAST - 1, 1)
+        turned7 = bank(6, [P, 1, 2, P])
+        for h in range(2):
+            nc.vector.tensor_tensor(
+                out=y_pairs[:, LAST, h], in0=by_pairs(est[LAST][:])[:, h], in1=by_pairs(sig[:])[:, h], op=MULT
+            )
+            turn(turned7[:, 0, h, :], LAST, h)
+        product(LAST, sig)
+        gather(turned7[:], LAST, 1)
+        quantize_y(LAST - 1, LAST)
+        quantize_y(LAST, TILES)
+        store_words(LAST - 1, TILES)
+        store_scales(LAST - 1, TILES, [nc.scalar, nc.sync, nc.scalar, nc.sync])

@@ -43,8 +43,14 @@ def tile_amortised_ivector_shrinkage_k3_kernel(
         t_codes = keep.tile([P, GROUPS, 2 * R], U8, align_bytes=256)
         a_codes = keep.tile([P, GROUPS, R], U32, align_bytes=256)
         v_codes = keep.tile([P, GROUPS, R], U32, align_bytes=256)
-        f_plane = keep.tile([P, GROUPS, U], U8, align_bytes=256)
-        t_plane = keep.tile([P, GROUPS, R], U8, align_bytes=256)
+        f_early = keep.tile([P, EARLY_GROUPS, U], U8, align_bytes=256)
+        t_early = keep.tile([P, EARLY_GROUPS, R], U8, align_bytes=256)
+        f_late = keep.tile([P, GROUPS - EARLY_GROUPS, U], U8, align_bytes=256)
+        t_late = keep.tile([P, GROUPS - EARLY_GROUPS, R], U8, align_bytes=256)
+
+        def plane_of(early, late, g):
+            return early[:, g, :] if g < EARLY_GROUPS else late[:, g - EARLY_GROUPS, :]
+
         a_plane = keep.tile([P, GROUPS, R], U8, align_bytes=256)
         v_plane = keep.tile([P, GROUPS, R], U8, align_bytes=256)
         v_rows = keep.tile([P, GROUPS, 4, R], BF16, align_bytes=256)
@@ -60,19 +66,25 @@ def tile_amortised_ivector_shrinkage_k3_kernel(
         y_pairs = keep.tile([P, TILES, 2, P, 2], BF16, align_bytes=256)
         y_grouped = keep.tile([P, U, 4], BF16, align_bytes=256)
         y_codes = keep.tile([P, U], U32, align_bytes=256)
-        y_plane = keep.tile([P, U], U8, align_bytes=256)
+        y_plane_early = keep.tile([P, P * (LAST - 1)], U8, align_bytes=256)
+        y_plane_late = keep.tile([P, 2 * P], U8, align_bytes=256)
+
+        def y_plane(n0, n1):
+            if n0 < LAST - 1:
+                return y_plane_early[:, P * n0 : P * n1]
+            return y_plane_late[:, P * (n0 - LAST + 1) : P * (n1 - LAST + 1)]
 
         def bank(b, shape):
             return psum.tile(shape, F32, name="bank%d" % b, tag="bank%d" % b)
 
-        def clear(plane, g0, g1):
-            nc.vector.memset(plane[:, g0:g1, :].rearrange("p g n -> p (g n)").bitcast(I32), 0)
+        def clear(plane):
+            nc.vector.memset(plane[:].rearrange("p g n -> p (g n)").bitcast(I32), 0)
 
         def load_scales(plane, first, scales, g0, g1):
             rows = scales.rearrange("g (q r) n -> r q g n", r=4)
             for r in range(4):
                 nc.sync.dma_start(
-                    out=plane[first + r : P : 32, g0:g1, :].bitcast(I32),
+                    out=plane[first + r : P : 32, :, :].bitcast(I32),
                     in_=rows[r][:, g0:g1, :].bitcast(I32),
                 )
 
@@ -96,7 +108,7 @@ def tile_amortised_ivector_shrinkage_k3_kernel(
             nc.tensor.matmul_mx(
                 out=acc,
                 lhsT=f_codes[:, g, cols].bitcast(FP8X4),
-                lhsT_scale=f_plane[:, g, cols],
+                lhsT_scale=plane_of(f_early, f_late, g)[:, cols],
                 rhs=codes,
                 rhs_scale=plane,
                 start=start,
@@ -104,7 +116,7 @@ def tile_amortised_ivector_shrinkage_k3_kernel(
             )
 
         def t_pass(n, g):
-            mx_pass(est[n][:], n, g, t_codes[:, g, :].bitcast(FP4X4), t_plane[:, g, :], g == 0, False)
+            mx_pass(est[n][:], n, g, t_codes[:, g, :].bitcast(FP4X4), plane_of(t_early, t_late, g), g == 0, False)
 
         def a_pass(n, g):
             mx_pass(est[n][:], n, g, a_codes[:, g, :].bitcast(FP8X4), a_plane[A_PLANE:P, g, :],
@@ -155,7 +167,7 @@ def tile_amortised_ivector_shrinkage_k3_kernel(
             cols = slice(P * n0, P * n1)
             nc.vector.quantize_mx(
                 out=y_codes[:, cols].bitcast(FP8X4),
-                scales=y_plane[:, cols],
+                scales=y_plane(n0, n1),
                 in_=y_grouped[:, cols, :].rearrange("p u t -> p (u t)"),
             )
 
@@ -168,16 +180,16 @@ def tile_amortised_ivector_shrinkage_k3_kernel(
             for r in range(4):
                 queues[r].dma_start(
                     out=rows[r][:, P * n0 : P * n1].bitcast(I32),
-                    in_=y_plane[r:P:32, P * n0 : P * n1].bitcast(I32),
+                    in_=y_plane(n0, n1)[r:P:32, :].bitcast(I32),
                 )
 
-        clear(f_plane, 0, EARLY_GROUPS)
-        clear(t_plane, 0, EARLY_GROUPS)
+        clear(f_early)
         nc.vector.memset(warm_in[:], 1.0)
-        clear(a_plane, 0, GROUPS)
+        clear(t_early)
         nc.vector.quantize_mx(out=warm_codes[:].bitcast(FP8X4), scales=warm_plane[:], in_=warm_in[:])
-        clear(f_plane, EARLY_GROUPS, GROUPS)
-        clear(t_plane, EARLY_GROUPS, GROUPS)
+        clear(a_plane)
+        clear(f_late)
+        clear(t_late)
         nc.vector.memset(frames_rows[:], 0.0)
         nc.vector.memset(identity[:], 0.0)
         make_identity(nc, identity[:], nomemset=True)
@@ -192,16 +204,16 @@ def tile_amortised_ivector_shrinkage_k3_kernel(
 
         load_f(0, 0, P * FIRST_TILES)
         load_t(0)
-        load_scales(f_plane, 0, f_scales, 0, EARLY_GROUPS)
-        load_scales(t_plane, 0, t_scales, 0, EARLY_GROUPS)
+        load_scales(f_early, 0, f_scales, 0, EARLY_GROUPS)
+        load_scales(t_early, 0, t_scales, 0, EARLY_GROUPS)
         load_f(0, P * FIRST_TILES, U)
         load_a(0)
         load_scales(a_plane, A_PLANE, a_scales, 0, GROUPS)
         load_f(1, 0, U)
         load_t(1)
         load_a(1)
-        load_scales(f_plane, 0, f_scales, EARLY_GROUPS, GROUPS)
-        load_scales(t_plane, 0, t_scales, EARLY_GROUPS, GROUPS)
+        load_scales(f_late, 0, f_scales, EARLY_GROUPS, GROUPS)
+        load_scales(t_late, 0, t_scales, EARLY_GROUPS, GROUPS)
         for g in range(2, GROUPS):
             load_f(g, 0, U)
             load_t(g)

@@ -171,9 +171,9 @@ def tile_amortised_ivector_shrinkage_k3_kernel(
                 in_=y_grouped[:, cols, :].rearrange("p u t -> p (u t)"),
             )
 
-        def store_words(n0, n1):
+        def store_words(n0, n1, queue):
             dst = out_1[0].rearrange("p u t -> p (u t)")[:, 4 * P * n0 : 4 * P * n1]
-            nc.sync.dma_start(out=dst.bitcast(I32), in_=y_codes[:, P * n0 : P * n1].bitcast(I32))
+            queue.dma_start(out=dst.bitcast(I32), in_=y_codes[:, P * n0 : P * n1].bitcast(I32))
 
         def store_scales(n0, n1, queues):
             rows = out_2[0].rearrange("(q r) u -> r q u", r=4)
@@ -202,13 +202,13 @@ def tile_amortised_ivector_shrinkage_k3_kernel(
                 rhs=warm_codes[:].bitcast(FP8X4), rhs_scale=warm_plane[:], start=True, stop=True,
             )
 
-        load_f(0, 0, P * FIRST_TILES)
         load_t(0)
+        load_f(0, 0, P * FIRST_TILES)
         load_scales(f_early, 0, f_scales, 0, EARLY_GROUPS)
         load_scales(t_early, 0, t_scales, 0, EARLY_GROUPS)
+        load_scales(a_plane, A_PLANE, a_scales, 0, GROUPS)
         load_f(0, P * FIRST_TILES, U)
         load_a(0)
-        load_scales(a_plane, A_PLANE, a_scales, 0, GROUPS)
         load_f(1, 0, U)
         load_t(1)
         load_a(1)
@@ -254,9 +254,9 @@ def tile_amortised_ivector_shrinkage_k3_kernel(
             gather(turned[:], 2 * pair, 2)
         round_to_pairs(LAST - 1)
         quantize_y(0, 4)
-        store_words(0, 4)
+        store_words(0, 4, nc.sync)
         quantize_y(4, 6)
-        store_words(4, 6)
+        store_words(4, 6, nc.sync)
         store_scales(0, 6, [nc.sync] * 4)
 
         sig = gate(LAST)
@@ -277,6 +277,7 @@ def tile_amortised_ivector_shrinkage_k3_kernel(
         product(LAST, sig)
         gather(turned7[:], LAST, 1)
         quantize_y(LAST - 1, LAST)
+        store_words(LAST - 1, LAST, nc.sync)
         quantize_y(LAST, TILES)
-        store_words(LAST - 1, TILES)
-        store_scales(LAST - 1, TILES, [nc.scalar, nc.sync, nc.scalar, nc.sync])
+        store_words(LAST, TILES, nc.scalar)
+        store_scales(LAST - 1, TILES, [nc.sync, nc.sync, nc.scalar, nc.sync])

@@ -25,8 +25,9 @@ FIRST_TILES = 4
 A_PLANE = 4
 HELD_GROUPS = 2
 VECTOR_COLS = 320
-WARM_PASSES = 18
-EVACUATED = 2
+WARM_PASSES = 16
+BRIDGE_PASSES = 10
+EVACUATED = 3
 
 
 def tile_amortised_ivector_shrinkage_k3_kernel(
@@ -80,9 +81,9 @@ def tile_amortised_ivector_shrinkage_k3_kernel(
         def clear(plane):
             nc.vector.memset(plane[:].rearrange("p g n -> p (g n)").bitcast(I32), 0)
 
-        def load_scales(plane, first, scales, g0, g1):
+        def load_scales(plane, first, scales, g0, g1, which=range(4)):
             rows = scales.rearrange("g (q r) n -> r q g n", r=4)
-            for r in range(4):
+            for r in which:
                 nc.sync.dma_start(
                     out=plane[first + r : P : 32, :, :].bitcast(I32),
                     in_=rows[r][:, g0:g1, :].bitcast(I32),
@@ -133,10 +134,11 @@ def tile_amortised_ivector_shrinkage_k3_kernel(
                 in_=grouped[:].rearrange("p n t -> p (n t)"),
             )
 
-        def gate(n):
-            z = bank(n % EVACUATED, [P, R])
-            for g in range(GROUPS):
+        def z_passes(z, n, groups):
+            for g in groups:
                 mx_pass(z[:], n, g, v_codes[:, g, :].bitcast(FP8X4), v_plane[:, g, :], g == 0, g == GROUPS - 1)
+
+        def gate(z, n):
             sig = ring.tile([P, R], F32, align_bytes=256, name="sig")
             nc.scalar.activation(out=sig[:], in_=z[:], func=SIGMOID, bias=frames_cols[:, 4 * n : 4 * n + 1])
             return sig
@@ -183,9 +185,9 @@ def tile_amortised_ivector_shrinkage_k3_kernel(
                     in_=y_plane(n0, n1)[r:P:32, :].bitcast(I32),
                 )
 
-        clear(f_early)
-        nc.vector.memset(warm_in[:], 1.0)
         clear(t_early)
+        nc.vector.memset(warm_in[:], 1.0)
+        clear(f_early)
         nc.vector.quantize_mx(out=warm_codes[:].bitcast(FP8X4), scales=warm_plane[:], in_=warm_in[:])
         clear(a_plane)
         clear(f_late)
@@ -203,9 +205,10 @@ def tile_amortised_ivector_shrinkage_k3_kernel(
             )
 
         load_t(0)
+        load_scales(t_early, 0, t_scales, 0, EARLY_GROUPS, range(1))
         load_f(0, 0, P * FIRST_TILES)
+        load_scales(t_early, 0, t_scales, 0, EARLY_GROUPS, range(1, 4))
         load_scales(f_early, 0, f_scales, 0, EARLY_GROUPS)
-        load_scales(t_early, 0, t_scales, 0, EARLY_GROUPS)
         load_scales(a_plane, A_PLANE, a_scales, 0, GROUPS)
         load_f(0, P * FIRST_TILES, U)
         load_a(0)
@@ -223,6 +226,12 @@ def tile_amortised_ivector_shrinkage_k3_kernel(
         load_v(3)
         load_v(4)
 
+        for i in range(BRIDGE_PASSES):
+            nc.tensor.matmul_mx(
+                out=warm[:], lhsT=warm_codes[:].bitcast(FP8X4), lhsT_scale=warm_plane[:],
+                rhs=f_codes[:, 0, 0:P].bitcast(FP8X4), rhs_scale=warm_plane[:], start=True, stop=True,
+            )
+
         est = [bank(n, [P, R]) for n in range(TILES)]
         for g in range(GROUPS - 1):
             tiles = range(TILES if g < GROUPS - HELD_GROUPS else LAST)
@@ -239,13 +248,18 @@ def tile_amortised_ivector_shrinkage_k3_kernel(
         nc.vector.transpose(frames_cols[:], frames_rows[:])
         nc.scalar.copy(out=est_sb[:, 0, :], in_=est[0][:])
         quantize_v(GROUPS - 1)
-        nc.scalar.copy(out=est_sb[:, 1, :], in_=est[1][:])
+        for n in range(1, EVACUATED):
+            nc.scalar.copy(out=est_sb[:, n, :], in_=est[n][:])
 
         for n in range(LAST):
-            sig = gate(n)
+            z = bank(n % EVACUATED, [P, R])
+            z_passes(z, n, range(GROUPS))
+            sig = gate(z, n)
             if n > 0:
                 round_to_pairs(n - 1)
             product(n, sig)
+        z = bank(LAST % EVACUATED, [P, R])
+        z_passes(z, LAST, range(2))
         for pair in range(3):
             turned = bank(EVACUATED + pair, [P, 2, 2, P])
             for i in range(2):
@@ -259,12 +273,13 @@ def tile_amortised_ivector_shrinkage_k3_kernel(
         store_words(4, 6, nc.sync)
         store_scales(0, 6, [nc.sync] * 4)
 
-        sig = gate(LAST)
+        z_passes(z, LAST, range(2, GROUPS))
+        sig = gate(z, LAST)
         for g in range(GROUPS - HELD_GROUPS, GROUPS):
             t_pass(LAST, g)
             a_pass(LAST, g)
 
-        turned6 = bank(5, [P, 1, 2, P])
+        turned6 = bank(2, [P, 1, 2, P])
         for h in range(2):
             turn(turned6[:, 0, h, :], LAST - 1, h)
         gather(turned6[:], LAST - 1, 1)

@@ -22,12 +22,14 @@ TILES = U // P
 LAST = TILES - 1
 EARLY_GROUPS = 2
 FIRST_TILES = 4
-A_PLANE = 4
 HELD_GROUPS = 2
 VECTOR_COLS = 320
 WARM_PASSES = 16
 BRIDGE_PASSES = 10
-EVACUATED = 3
+EVACUATED = 4
+WOVEN = 3
+PACKED = 4
+PAIR_BANKS = (0, 4, 1)
 
 
 def tile_amortised_ivector_shrinkage_k3_kernel(
@@ -52,7 +54,8 @@ def tile_amortised_ivector_shrinkage_k3_kernel(
         def plane_of(early, late, g):
             return early[:, g, :] if g < EARLY_GROUPS else late[:, g - EARLY_GROUPS, :]
 
-        a_plane = keep.tile([P, GROUPS, R], U8, align_bytes=256)
+        a_packed = keep.tile([P, 1, R], U8, align_bytes=256)
+        a_last = keep.tile([P, 1, R], U8, align_bytes=256)
         v_plane = keep.tile([P, GROUPS, R], U8, align_bytes=256)
         v_rows = keep.tile([P, GROUPS, 4, R], BF16, align_bytes=256)
         frames_rows = keep.tile([P, 32], BF16, align_bytes=64)
@@ -67,13 +70,7 @@ def tile_amortised_ivector_shrinkage_k3_kernel(
         y_pairs = keep.tile([P, TILES, 2, P, 2], BF16, align_bytes=256)
         y_grouped = keep.tile([P, U, 4], BF16, align_bytes=256)
         y_codes = keep.tile([P, U], U32, align_bytes=256)
-        y_plane_early = keep.tile([P, P * (LAST - 1)], U8, align_bytes=256)
-        y_plane_late = keep.tile([P, 2 * P], U8, align_bytes=256)
-
-        def y_plane(n0, n1):
-            if n0 < LAST - 1:
-                return y_plane_early[:, P * n0 : P * n1]
-            return y_plane_late[:, P * (n0 - LAST + 1) : P * (n1 - LAST + 1)]
+        y_plane = keep.tile([P, U], U8, align_bytes=256)
 
         def bank(b, shape):
             return psum.tile(shape, F32, name="bank%d" % b, tag="bank%d" % b)
@@ -81,11 +78,11 @@ def tile_amortised_ivector_shrinkage_k3_kernel(
         def clear(plane):
             nc.vector.memset(plane[:].rearrange("p g n -> p (g n)").bitcast(I32), 0)
 
-        def load_scales(plane, first, scales, g0, g1, which=range(4)):
+        def load_scales(plane, scales, g0, g1, which=range(4)):
             rows = scales.rearrange("g (q r) n -> r q g n", r=4)
             for r in which:
                 nc.sync.dma_start(
-                    out=plane[first + r : P : 32, :, :].bitcast(I32),
+                    out=plane[r:P:32, :, :].bitcast(I32),
                     in_=rows[r][:, g0:g1, :].bitcast(I32),
                 )
 
@@ -120,14 +117,15 @@ def tile_amortised_ivector_shrinkage_k3_kernel(
             mx_pass(est[n][:], n, g, t_codes[:, g, :].bitcast(FP4X4), plane_of(t_early, t_late, g), g == 0, False)
 
         def a_pass(n, g):
-            mx_pass(est[n][:], n, g, a_codes[:, g, :].bitcast(FP8X4), a_plane[A_PLANE:P, g, :],
-                    False, g == GROUPS - 1)
+            plane = a_packed[4 * g : P, 0, :] if g < PACKED else a_last[:, 0, :]
+            mx_pass(est[n][:], n, g, a_codes[:, g, :].bitcast(FP8X4), plane, False, g == GROUPS - 1)
 
-        def quantize_v(g):
+        def quantize_v(g, split):
             grouped = ring.tile([P, R, 4], BF16, align_bytes=256, name="v_grouped")
             src = v_rows[:, g].rearrange("p t n -> p n t")
-            nc.vector.tensor_copy(out=grouped[:, :VECTOR_COLS, :], in_=src[:, :VECTOR_COLS, :])
-            nc.scalar.copy(out=grouped[:, VECTOR_COLS:, :], in_=src[:, VECTOR_COLS:, :])
+            nc.vector.tensor_copy(out=grouped[:, :split, :], in_=src[:, :split, :])
+            if split < R:
+                nc.scalar.copy(out=grouped[:, split:, :], in_=src[:, split:, :])
             nc.vector.quantize_mx(
                 out=v_codes[:, g, :].bitcast(FP8X4),
                 scales=v_plane[:, g, :],
@@ -169,7 +167,7 @@ def tile_amortised_ivector_shrinkage_k3_kernel(
             cols = slice(P * n0, P * n1)
             nc.vector.quantize_mx(
                 out=y_codes[:, cols].bitcast(FP8X4),
-                scales=y_plane(n0, n1),
+                scales=y_plane[:, cols],
                 in_=y_grouped[:, cols, :].rearrange("p u t -> p (u t)"),
             )
 
@@ -182,16 +180,17 @@ def tile_amortised_ivector_shrinkage_k3_kernel(
             for r in range(4):
                 queues[r].dma_start(
                     out=rows[r][:, P * n0 : P * n1].bitcast(I32),
-                    in_=y_plane(n0, n1)[r:P:32, :].bitcast(I32),
+                    in_=y_plane[r:P:32, P * n0 : P * n1].bitcast(I32),
                 )
 
         clear(t_early)
         nc.vector.memset(warm_in[:], 1.0)
         clear(f_early)
         nc.vector.quantize_mx(out=warm_codes[:].bitcast(FP8X4), scales=warm_plane[:], in_=warm_in[:])
-        clear(a_plane)
+        clear(a_packed)
         clear(f_late)
         clear(t_late)
+        clear(a_last)
         nc.vector.memset(frames_rows[:], 0.0)
         nc.vector.memset(identity[:], 0.0)
         make_identity(nc, identity[:], nomemset=True)
@@ -205,24 +204,32 @@ def tile_amortised_ivector_shrinkage_k3_kernel(
             )
 
         load_t(0)
-        load_scales(t_early, 0, t_scales, 0, EARLY_GROUPS, range(1))
+        load_scales(t_early, t_scales, 0, EARLY_GROUPS, range(1))
         load_f(0, 0, P * FIRST_TILES)
-        load_scales(t_early, 0, t_scales, 0, EARLY_GROUPS, range(1, 4))
-        load_scales(f_early, 0, f_scales, 0, EARLY_GROUPS)
-        load_scales(a_plane, A_PLANE, a_scales, 0, GROUPS)
+        load_scales(t_early, t_scales, 0, EARLY_GROUPS, range(1, 4))
+        load_scales(f_early, f_scales, 0, EARLY_GROUPS)
         load_f(0, P * FIRST_TILES, U)
         load_a(0)
+        for q in range(4):
+            nc.sync.dma_start(
+                out=a_packed[32 * q : 32 * q + 4 * PACKED, 0, :].bitcast(I32),
+                in_=a_scales[0:PACKED, 4 * q : 4 * q + 4, :].bitcast(I32),
+            )
         load_f(1, 0, U)
         load_t(1)
         load_a(1)
-        load_scales(f_late, 0, f_scales, EARLY_GROUPS, GROUPS)
-        load_scales(t_late, 0, t_scales, EARLY_GROUPS, GROUPS)
+        load_scales(f_late, f_scales, EARLY_GROUPS, GROUPS)
+        load_scales(t_late, t_scales, EARLY_GROUPS, GROUPS)
         for g in range(2, GROUPS):
+            if g == GROUPS - 1:
+                load_scales(a_last, a_scales, PACKED, GROUPS)
+                nc.sync.dma_start(
+                    out=frames_rows[0:P:4, :], in_=log_frames.rearrange("(n q j) -> q n j", q=4, j=32)
+                )
             load_f(g, 0, U)
             load_t(g)
             load_a(g)
             load_v(g - 2)
-        nc.sync.dma_start(out=frames_rows[0:P:4, :], in_=log_frames.rearrange("(n q j) -> q n j", q=4, j=32))
         load_v(3)
         load_v(4)
 
@@ -243,35 +250,45 @@ def tile_amortised_ivector_shrinkage_k3_kernel(
             t_pass(n, GROUPS - 1)
             a_pass(n, GROUPS - 1)
 
-        for g in range(GROUPS - 1):
-            quantize_v(g)
+        quantize_v(0, VECTOR_COLS)
+        quantize_v(1, VECTOR_COLS)
+        quantize_v(2, R)
+        for n in range(WOVEN):
+            nc.scalar.copy(out=est_sb[:, n, :], in_=est[n][:])
         nc.vector.transpose(frames_cols[:], frames_rows[:])
-        nc.scalar.copy(out=est_sb[:, 0, :], in_=est[0][:])
-        quantize_v(GROUPS - 1)
-        for n in range(1, EVACUATED):
+        for g in range(3, GROUPS):
+            quantize_v(g, VECTOR_COLS)
+        for n in range(WOVEN, EVACUATED):
             nc.scalar.copy(out=est_sb[:, n, :], in_=est[n][:])
 
+        woven = [bank(n, [P, R]) for n in range(WOVEN)]
+        for g in range(GROUPS):
+            for n in range(WOVEN):
+                z_passes(woven[n], n, [g])
+        rounded = 0
         for n in range(LAST):
-            z = bank(n % EVACUATED, [P, R])
-            z_passes(z, n, range(GROUPS))
-            sig = gate(z, n)
-            if n > 0:
-                round_to_pairs(n - 1)
-            product(n, sig)
+            if n < WOVEN:
+                z = woven[n]
+            else:
+                z = bank(n % EVACUATED, [P, R])
+                z_passes(z, n, range(GROUPS))
+            product(n, gate(z, n))
+            upto = n if n >= EVACUATED else n - 1
+            for i in range(rounded, upto + 1):
+                round_to_pairs(i)
+            rounded = upto + 1
         z = bank(LAST % EVACUATED, [P, R])
         z_passes(z, LAST, range(2))
         for pair in range(3):
-            turned = bank(EVACUATED + pair, [P, 2, 2, P])
+            turned = bank(PAIR_BANKS[pair], [P, 2, 2, P])
             for i in range(2):
                 for h in range(2):
                     turn(turned[:, i, h, :], 2 * pair + i, h)
             gather(turned[:], 2 * pair, 2)
-        round_to_pairs(LAST - 1)
         quantize_y(0, 4)
         store_words(0, 4, nc.sync)
         quantize_y(4, 6)
         store_words(4, 6, nc.sync)
-        store_scales(0, 6, [nc.sync] * 4)
 
         z_passes(z, LAST, range(2, GROUPS))
         sig = gate(z, LAST)
@@ -279,7 +296,7 @@ def tile_amortised_ivector_shrinkage_k3_kernel(
             t_pass(LAST, g)
             a_pass(LAST, g)
 
-        turned6 = bank(2, [P, 1, 2, P])
+        turned6 = bank(5, [P, 1, 2, P])
         for h in range(2):
             turn(turned6[:, 0, h, :], LAST - 1, h)
         gather(turned6[:], LAST - 1, 1)
@@ -295,4 +312,4 @@ def tile_amortised_ivector_shrinkage_k3_kernel(
         store_words(LAST - 1, LAST, nc.sync)
         quantize_y(LAST, TILES)
         store_words(LAST, TILES, nc.scalar)
-        store_scales(LAST - 1, TILES, [nc.sync, nc.sync, nc.scalar, nc.sync])
+        store_scales(0, TILES, [nc.sync, nc.sync, nc.scalar, nc.sync])

@@ -24,8 +24,6 @@ EARLY_GROUPS = 2
 FIRST_TILES = 4
 HELD_GROUPS = 2
 VECTOR_COLS = 320
-WARM_PASSES = 16
-BRIDGE_PASSES = 10
 EVACUATED = 4
 WOVEN = 3
 PACKED = 4
@@ -61,10 +59,6 @@ def tile_amortised_ivector_shrinkage_k3_kernel(
         frames_rows = keep.tile([P, 32], BF16, align_bytes=64)
         frames_cols = keep.tile([P, 32], BF16, align_bytes=64)
         identity = keep.tile([P, P], F32, align_bytes=256)
-        warm_in = keep.tile([P, 4 * P], BF16, align_bytes=256)
-        warm_codes = keep.tile([P, P], U32, align_bytes=256)
-        warm_plane = keep.tile([P, P], U8, align_bytes=256)
-        warm_act = keep.tile([P, 1], F32)
         est_sb = keep.tile([P, EVACUATED, R], F32, align_bytes=256)
         y = keep.tile([P, TILES, R], F32, align_bytes=256)
         y_pairs = keep.tile([P, TILES, 2, P, 2], BF16, align_bytes=256)
@@ -184,9 +178,7 @@ def tile_amortised_ivector_shrinkage_k3_kernel(
                 )
 
         clear(t_early)
-        nc.vector.memset(warm_in[:], 1.0)
         clear(f_early)
-        nc.vector.quantize_mx(out=warm_codes[:].bitcast(FP8X4), scales=warm_plane[:], in_=warm_in[:])
         clear(a_packed)
         clear(f_late)
         clear(t_late)
@@ -194,14 +186,6 @@ def tile_amortised_ivector_shrinkage_k3_kernel(
         nc.vector.memset(frames_rows[:], 0.0)
         nc.vector.memset(identity[:], 0.0)
         make_identity(nc, identity[:], nomemset=True)
-        nc.scalar.activation(out=warm_act[:], in_=warm_in[:, 0:1], func=SIGMOID)
-
-        warm = bank(LAST, [P, P])
-        for i in range(WARM_PASSES):
-            nc.tensor.matmul_mx(
-                out=warm[:], lhsT=warm_codes[:].bitcast(FP8X4), lhsT_scale=warm_plane[:],
-                rhs=warm_codes[:].bitcast(FP8X4), rhs_scale=warm_plane[:], start=True, stop=True,
-            )
 
         load_t(0)
         load_scales(t_early, t_scales, 0, EARLY_GROUPS, range(1))
@@ -232,12 +216,6 @@ def tile_amortised_ivector_shrinkage_k3_kernel(
             load_v(g - 2)
         load_v(3)
         load_v(4)
-
-        for i in range(BRIDGE_PASSES):
-            nc.tensor.matmul_mx(
-                out=warm[:], lhsT=warm_codes[:].bitcast(FP8X4), lhsT_scale=warm_plane[:],
-                rhs=f_codes[:, 0, 0:P].bitcast(FP8X4), rhs_scale=warm_plane[:], start=True, stop=True,
-            )
 
         est = [bank(n, [P, R]) for n in range(TILES)]
         for g in range(GROUPS - 1):

@@ -19,15 +19,15 @@ MULT = mybir.AluOpType.mult
 P = 128
 GROUPS = K // 512
 TILES = U // P
-LAST = TILES - 1
 EARLY_GROUPS = 2
-FIRST_TILES = 4
-HELD_GROUPS = 2
-VECTOR_COLS = 320
-EVACUATED = 4
-WOVEN = 3
 PACKED = 4
-PAIR_BANKS = (0, 4, 1)
+FRONT = 6
+TURNED = 5
+FIRST_TILES = 3
+VECTOR_COLS = 256
+WARM_N = 256
+WARM_FREE = 3
+WARM_TIED = 4
 
 
 def tile_amortised_ivector_shrinkage_k3_kernel(
@@ -40,7 +40,8 @@ def tile_amortised_ivector_shrinkage_k3_kernel(
         psum = ctx.enter_context(tc.psum_pool(name="psum", bufs=1))
         ctx.enter_context(tc.manual_schedule())
 
-        f_codes = keep.tile([P, GROUPS, U], U32, align_bytes=256)
+        f_front = keep.tile([P, GROUPS, P * FRONT], U32, align_bytes=256)
+        f_back = keep.tile([P, GROUPS, U - P * FRONT], U32, align_bytes=256)
         t_codes = keep.tile([P, GROUPS, 2 * R], U8, align_bytes=256)
         a_codes = keep.tile([P, GROUPS, R], U32, align_bytes=256)
         v_codes = keep.tile([P, GROUPS, R], U32, align_bytes=256)
@@ -48,44 +49,43 @@ def tile_amortised_ivector_shrinkage_k3_kernel(
         t_early = keep.tile([P, EARLY_GROUPS, R], U8, align_bytes=256)
         f_late = keep.tile([P, GROUPS - EARLY_GROUPS, U], U8, align_bytes=256)
         t_late = keep.tile([P, GROUPS - EARLY_GROUPS, R], U8, align_bytes=256)
-
-        def plane_of(early, late, g):
-            return early[:, g, :] if g < EARLY_GROUPS else late[:, g - EARLY_GROUPS, :]
-
         a_packed = keep.tile([P, 1, R], U8, align_bytes=256)
         a_last = keep.tile([P, 1, R], U8, align_bytes=256)
         v_plane = keep.tile([P, GROUPS, R], U8, align_bytes=256)
-        v_rows = keep.tile([P, GROUPS, 4, R], BF16, align_bytes=256)
+        v_rows = [keep.tile([P, 4, R], BF16, align_bytes=256, name="v_rows%d" % g) for g in range(GROUPS)]
         frames_rows = keep.tile([P, 32], BF16, align_bytes=64)
         frames_cols = keep.tile([P, 32], BF16, align_bytes=64)
         identity = keep.tile([P, P], F32, align_bytes=256)
-        est_sb = keep.tile([P, EVACUATED, R], F32, align_bytes=256)
+        warm_codes = keep.tile([P, WARM_N], U32, align_bytes=256)
+        warm_plane = keep.tile([P, WARM_N], U8, align_bytes=256)
+        warm_act = keep.tile([P, 1], F32)
         y = keep.tile([P, TILES, R], F32, align_bytes=256)
-        y_pairs = keep.tile([P, TILES, 2, P, 2], BF16, align_bytes=256)
-        y_grouped = keep.tile([P, U, 4], BF16, align_bytes=256)
+        staged = keep.tile([P, 4, TURNED, 64], F32, align_bytes=256)
+        landed = keep.tile([P, TURNED, 4, 64], F32, align_bytes=256)
         y_codes = keep.tile([P, U], U32, align_bytes=256)
         y_plane = keep.tile([P, U], U8, align_bytes=256)
 
         def bank(b, shape):
             return psum.tile(shape, F32, name="bank%d" % b, tag="bank%d" % b)
 
+        def plane_of(early, late, g):
+            return early[:, g, :] if g < EARLY_GROUPS else late[:, g - EARLY_GROUPS, :]
+
         def clear(plane):
             nc.vector.memset(plane[:].rearrange("p g n -> p (g n)").bitcast(I32), 0)
 
-        def load_scales(plane, scales, g0, g1, which=range(4)):
+        def load_scales(plane, scales, g0, g1, queue, which=range(4)):
             rows = scales.rearrange("g (q r) n -> r q g n", r=4)
             for r in which:
-                nc.sync.dma_start(
-                    out=plane[r:P:32, :, :].bitcast(I32),
-                    in_=rows[r][:, g0:g1, :].bitcast(I32),
-                )
+                queue.dma_start(out=plane[r:P:32, :, :].bitcast(I32), in_=rows[r][:, g0:g1, :].bitcast(I32))
 
         def load_f(g, n0, n1):
-            src = f_words[g].rearrange("p n t -> p (n t)")[:, 4 * n0 : 4 * n1]
-            nc.sync.dma_start(out=f_codes[:, g, n0:n1].bitcast(I32), in_=src.bitcast(I32))
+            src = f_words[g].rearrange("p n t -> p (n t)")[:, 4 * P * n0 : 4 * P * n1]
+            nc.sync.dma_start(out=f_front[:, g, P * n0 : P * n1].bitcast(I32), in_=src.bitcast(I32))
 
-        def load_t(g):
-            nc.sync.dma_start(out=t_codes[:, g, :].bitcast(I32), in_=t_words[g].bitcast(I32))
+        def load_t(g0, g1):
+            src = t_words[g0:g1].rearrange("g p n -> p g n")
+            nc.sync.dma_start(out=t_codes[:, g0:g1, :].bitcast(I32), in_=src.bitcast(I32))
 
         def load_a(g):
             src = a_words[g].rearrange("p n t -> p (n t)")
@@ -93,201 +93,218 @@ def tile_amortised_ivector_shrinkage_k3_kernel(
 
         def load_v(g):
             src = v[512 * g : 512 * (g + 1), :].rearrange("(p t) n -> p t n", t=4)
-            nc.sync.dma_start(out=v_rows[:, g], in_=src)
+            nc.sync.dma_start(out=v_rows[g][:], in_=src)
 
         def mx_pass(acc, n, g, codes, plane, start, stop):
-            cols = slice(P * n, P * (n + 1))
+            if n < FRONT:
+                held = f_front[:, g, P * n : P * (n + 1)]
+            else:
+                held = f_back[:, g, P * (n - FRONT) : P * (n - FRONT + 1)]
             nc.tensor.matmul_mx(
-                out=acc,
-                lhsT=f_codes[:, g, cols].bitcast(FP8X4),
-                lhsT_scale=plane_of(f_early, f_late, g)[:, cols],
+                out=acc[:],
+                lhsT=held.bitcast(FP8X4),
+                lhsT_scale=plane_of(f_early, f_late, g)[:, P * n : P * (n + 1)],
                 rhs=codes,
                 rhs_scale=plane,
                 start=start,
                 stop=stop,
             )
 
-        def t_pass(n, g):
-            mx_pass(est[n][:], n, g, t_codes[:, g, :].bitcast(FP4X4), plane_of(t_early, t_late, g), g == 0, False)
+        def t_pass(est, n, g):
+            mx_pass(est, n, g, t_codes[:, g, :].bitcast(FP4X4), plane_of(t_early, t_late, g), g == 0, False)
 
-        def a_pass(n, g):
+        def a_pass(est, n, g):
             plane = a_packed[4 * g : P, 0, :] if g < PACKED else a_last[:, 0, :]
-            mx_pass(est[n][:], n, g, a_codes[:, g, :].bitcast(FP8X4), plane, False, g == GROUPS - 1)
+            mx_pass(est, n, g, a_codes[:, g, :].bitcast(FP8X4), plane, False, g == GROUPS - 1)
 
-        def quantize_v(g, split):
+        def interleave_v(g):
             grouped = ring.tile([P, R, 4], BF16, align_bytes=256, name="v_grouped")
-            src = v_rows[:, g].rearrange("p t n -> p n t")
-            nc.vector.tensor_copy(out=grouped[:, :split, :], in_=src[:, :split, :])
-            if split < R:
-                nc.scalar.copy(out=grouped[:, split:, :], in_=src[:, split:, :])
+            src = v_rows[g][:].rearrange("p t (c i) -> p c t i", i=4)
+            dst = grouped[:].rearrange("p (c i) t -> p c t i", i=4)
+            split = VECTOR_COLS // 4
+            nc.vector.tensor_copy(out=dst[:, :split], in_=src[:, :split])
+            nc.scalar.copy(out=dst[:, split:], in_=src[:, split:])
+            return grouped
+
+        def quantize_v(g, grouped):
             nc.vector.quantize_mx(
                 out=v_codes[:, g, :].bitcast(FP8X4),
                 scales=v_plane[:, g, :],
                 in_=grouped[:].rearrange("p n t -> p (n t)"),
             )
 
-        def z_passes(z, n, groups):
-            for g in groups:
-                mx_pass(z[:], n, g, v_codes[:, g, :].bitcast(FP8X4), v_plane[:, g, :], g == 0, g == GROUPS - 1)
-
-        def gate(z, n):
+        def logits(n):
+            z = bank(FRONT + n % 2, [P, R])
+            for g in range(GROUPS):
+                mx_pass(z, n, g, v_codes[:, g, :].bitcast(FP8X4), v_plane[:, g, :], g == 0, g == GROUPS - 1)
             sig = ring.tile([P, R], F32, align_bytes=256, name="sig")
             nc.scalar.activation(out=sig[:], in_=z[:], func=SIGMOID, bias=frames_cols[:, 4 * n : 4 * n + 1])
             return sig
 
-        def product(n, sig):
-            src = est_sb[:, n, :] if n < EVACUATED else est[n][:]
-            nc.vector.tensor_tensor(out=y[:, n, :], in0=src, in1=sig[:], op=MULT)
+        def product(n, est, sig):
+            nc.vector.tensor_tensor(out=y[:, n, :], in0=est[:], in1=sig[:], op=MULT)
+
+        def store_y(n):
             nc.sync.dma_start(out=out_0[P * n : P * (n + 1), :], in_=y[:, n, :])
 
         def by_pairs(ap):
             return ap.rearrange("u (p h e) -> u h p e", h=2, e=2)
 
         def round_to_pairs(n):
-            nc.vector.tensor_copy(out=y_pairs[:, n], in_=by_pairs(y[:, n, :]))
+            pairs = ring.tile([P, 2, P, 2], BF16, align_bytes=256, name="pairs")
+            nc.scalar.copy(out=pairs[:], in_=by_pairs(y[:, n, :]))
+            return pairs
 
-        def turn(dst, n, h):
-            words = y_pairs[:, n, h].rearrange("u p e -> u (p e)").bitcast(F32)
-            nc.tensor.transpose(dst, words, identity[:])
-
-        def gather(turned, n0, count):
-            dst = y_grouped[:, P * n0 : P * (n0 + count), :].rearrange("p u t -> p (u t)").bitcast(F32)
-            nc.scalar.copy(
-                out=dst.rearrange("p (n u h) -> p n u h", n=count, h=2),
-                in_=turned.rearrange("p n h u -> p n u h"),
+        def turn_blocks(n, pairs):
+            blocks = ring.tile([P, 2 * P], F32, align_bytes=256, name="blocks")
+            nc.vector.transpose(blocks[:], pairs[:].rearrange("u h p e -> u (h p e)").bitcast(F32))
+            nc.vector.tensor_copy(
+                out=staged[:, :, n, :].rearrange("p q (i h) -> p q i h", h=2),
+                in_=blocks[:].rearrange("p (h q i) -> p q i h", h=2, q=4),
             )
 
-        def quantize_y(n0, n1):
+        def turn(dst, pairs, h):
+            nc.tensor.transpose(dst[:, h, :], pairs[:, h].rearrange("u p e -> u (p e)").bitcast(F32), identity[:])
+
+        def gather(turned):
+            joined = ring.tile([P, P, 2], F32, align_bytes=256, name="joined")
+            nc.scalar.copy(out=joined[:], in_=turned[:].rearrange("p h u -> p u h"))
+            return joined[:].rearrange("p u h -> p (u h)")
+
+        def quantize_y(n0, n1, words):
             cols = slice(P * n0, P * n1)
-            nc.vector.quantize_mx(
-                out=y_codes[:, cols].bitcast(FP8X4),
-                scales=y_plane[:, cols],
-                in_=y_grouped[:, cols, :].rearrange("p u t -> p (u t)"),
-            )
+            nc.vector.quantize_mx(out=y_codes[:, cols].bitcast(FP8X4), scales=y_plane[:, cols], in_=words.bitcast(BF16))
 
         def store_words(n0, n1, queue):
             dst = out_1[0].rearrange("p u t -> p (u t)")[:, 4 * P * n0 : 4 * P * n1]
             queue.dma_start(out=dst.bitcast(I32), in_=y_codes[:, P * n0 : P * n1].bitcast(I32))
 
-        def store_scales(n0, n1, queues):
+        def store_scales(queues):
             rows = out_2[0].rearrange("(q r) u -> r q u", r=4)
             for r in range(4):
-                queues[r].dma_start(
-                    out=rows[r][:, P * n0 : P * n1].bitcast(I32),
-                    in_=y_plane[r:P:32, P * n0 : P * n1].bitcast(I32),
+                queues[r].dma_start(out=rows[r].bitcast(I32), in_=y_plane[r:P:32, :].bitcast(I32))
+
+        def warm_passes(count, moving):
+            for i in range(count):
+                nc.tensor.matmul_mx(
+                    out=warm[:], lhsT=warm_codes[:, 0:P].bitcast(FP8X4), lhsT_scale=warm_plane[:, 0:P],
+                    rhs=moving.bitcast(FP8X4), rhs_scale=warm_plane[:], start=True, stop=True,
                 )
 
         clear(t_early)
-        clear(f_early)
-        clear(a_packed)
         clear(f_late)
+        clear(f_early)
+        zeros = f_late[:].rearrange("p g n -> p (g n)").bitcast(BF16)
+        nc.vector.quantize_mx(out=warm_codes[:].bitcast(FP8X4), scales=warm_plane[:], in_=zeros[:, : 4 * WARM_N])
+        clear(a_packed)
         clear(t_late)
         clear(a_last)
         nc.vector.memset(frames_rows[:], 0.0)
         nc.vector.memset(identity[:], 0.0)
+        nc.scalar.activation(out=warm_act[:], in_=t_late[:, 0, :].bitcast(BF16)[:, 0:1], func=SIGMOID)
+
+        load_scales(f_late, f_scales, EARLY_GROUPS, GROUPS, nc.gpsimd)
+        load_scales(a_last, a_scales, PACKED, GROUPS, nc.gpsimd)
         make_identity(nc, identity[:], nomemset=True)
 
-        load_t(0)
-        load_scales(t_early, t_scales, 0, EARLY_GROUPS, range(1))
-        load_f(0, 0, P * FIRST_TILES)
-        load_scales(t_early, t_scales, 0, EARLY_GROUPS, range(1, 4))
-        load_scales(f_early, f_scales, 0, EARLY_GROUPS)
-        load_f(0, P * FIRST_TILES, U)
+        load_t(0, 1)
+        load_scales(t_early, t_scales, 0, EARLY_GROUPS, nc.sync, range(1))
+        load_f(0, 0, FIRST_TILES)
+        load_scales(t_early, t_scales, 0, EARLY_GROUPS, nc.sync, range(1, 4))
+        load_scales(f_early, f_scales, 0, EARLY_GROUPS, nc.sync)
+        load_f(0, FIRST_TILES, FRONT)
         load_a(0)
         for q in range(4):
             nc.sync.dma_start(
                 out=a_packed[32 * q : 32 * q + 4 * PACKED, 0, :].bitcast(I32),
                 in_=a_scales[0:PACKED, 4 * q : 4 * q + 4, :].bitcast(I32),
             )
-        load_f(1, 0, U)
-        load_t(1)
+        load_f(1, 0, FRONT)
+        load_t(1, 3)
         load_a(1)
-        load_scales(f_late, f_scales, EARLY_GROUPS, GROUPS)
-        load_scales(t_late, t_scales, EARLY_GROUPS, GROUPS)
+        load_scales(t_late, t_scales, EARLY_GROUPS, GROUPS, nc.sync)
+        load_f(2, 0, FRONT)
+        load_a(2)
+        load_v(0)
+        load_f(3, 0, FRONT)
+        load_t(3, 5)
+        load_a(3)
+        load_v(1)
+        nc.sync.dma_start(out=frames_rows[0:P:4, :], in_=log_frames.rearrange("(n q j) -> q n j", q=4, j=32))
+        load_f(4, 0, FRONT)
+        load_a(4)
         for g in range(2, GROUPS):
-            if g == GROUPS - 1:
-                load_scales(a_last, a_scales, PACKED, GROUPS)
-                nc.sync.dma_start(
-                    out=frames_rows[0:P:4, :], in_=log_frames.rearrange("(n q j) -> q n j", q=4, j=32)
-                )
-            load_f(g, 0, U)
-            load_t(g)
-            load_a(g)
-            load_v(g - 2)
-        load_v(3)
-        load_v(4)
+            load_v(g)
+        back = f_words.rearrange("g p n t -> p g (n t)")[:, :, 4 * P * FRONT :]
+        nc.sync.dma_start(out=f_back[:].bitcast(I32), in_=back.bitcast(I32))
 
-        est = [bank(n, [P, R]) for n in range(TILES)]
-        for g in range(GROUPS - 1):
-            tiles = range(TILES if g < GROUPS - HELD_GROUPS else LAST)
-            for n in tiles:
-                t_pass(n, g)
-            for n in tiles:
-                a_pass(n, g)
-        for n in range(LAST):
-            t_pass(n, GROUPS - 1)
-            a_pass(n, GROUPS - 1)
+        warm = bank(TILES - 1, [P, WARM_N])
+        warm_passes(WARM_FREE, warm_codes[:])
+        warm_passes(WARM_TIED, f_front[:, 0, 0:WARM_N])
 
-        quantize_v(0, VECTOR_COLS)
-        quantize_v(1, VECTOR_COLS)
-        quantize_v(2, R)
-        for n in range(WOVEN):
-            nc.scalar.copy(out=est_sb[:, n, :], in_=est[n][:])
-        nc.vector.transpose(frames_cols[:], frames_rows[:])
-        for g in range(3, GROUPS):
-            quantize_v(g, VECTOR_COLS)
-        for n in range(WOVEN, EVACUATED):
-            nc.scalar.copy(out=est_sb[:, n, :], in_=est[n][:])
-
-        woven = [bank(n, [P, R]) for n in range(WOVEN)]
+        est = [bank(n, [P, R]) for n in range(FRONT)]
         for g in range(GROUPS):
-            for n in range(WOVEN):
-                z_passes(woven[n], n, [g])
-        rounded = 0
-        for n in range(LAST):
-            if n < WOVEN:
-                z = woven[n]
-            else:
-                z = bank(n % EVACUATED, [P, R])
-                z_passes(z, n, range(GROUPS))
-            product(n, gate(z, n))
-            upto = n if n >= EVACUATED else n - 1
-            for i in range(rounded, upto + 1):
-                round_to_pairs(i)
-            rounded = upto + 1
-        z = bank(LAST % EVACUATED, [P, R])
-        z_passes(z, LAST, range(2))
-        for pair in range(3):
-            turned = bank(PAIR_BANKS[pair], [P, 2, 2, P])
-            for i in range(2):
-                for h in range(2):
-                    turn(turned[:, i, h, :], 2 * pair + i, h)
-            gather(turned[:], 2 * pair, 2)
-        quantize_y(0, 4)
-        store_words(0, 4, nc.sync)
-        quantize_y(4, 6)
-        store_words(4, 6, nc.sync)
+            for n in range(FRONT):
+                t_pass(est[n], n, g)
+            for n in range(FRONT):
+                a_pass(est[n], n, g)
 
-        z_passes(z, LAST, range(2, GROUPS))
-        sig = gate(z, LAST)
-        for g in range(GROUPS - HELD_GROUPS, GROUPS):
-            t_pass(LAST, g)
-            a_pass(LAST, g)
+        for g in range(GROUPS):
+            quantize_v(g, interleave_v(g))
+            if g == 1:
+                nc.vector.transpose(frames_cols[:], frames_rows[:])
 
-        turned6 = bank(5, [P, 1, 2, P])
+        for n in range(FRONT):
+            sig = logits(n)
+            product(n, est[n], sig)
+            if n > 0:
+                turn_blocks(n - 1, round_to_pairs(n - 1))
+            if n < TURNED - 1:
+                store_y(n)
+        for a in range(4):
+            for q in range(4):
+                nc.sync.dma_start(out=landed[32 * q : 32 * q + 32, :, a, :], in_=staged[32 * a : 32 * a + 32, q])
+        for n in range(TURNED - 1, FRONT):
+            store_y(n)
+
+        n = TILES - 2
+        pairs5 = round_to_pairs(n - 1)
+        sig = logits(n)
+        est6 = bank(0, [P, R])
+        for g in range(GROUPS):
+            t_pass(est6, n, g)
+            a_pass(est6, n, g)
+        product(n, est6, sig)
+        store_y(n)
+        pairs6 = round_to_pairs(n)
+
+        n = TILES - 1
+        sig = logits(n)
+        est7 = bank(1, [P, R])
+        for g in range(GROUPS):
+            t_pass(est7, n, g)
+            a_pass(est7, n, g)
+        flat = landed[:].rearrange("p n a w -> p (n a w)")
+        quantize_y(0, 4, flat[:, : 4 * 2 * P])
+        quantize_y(4, 5, flat[:, 4 * 2 * P :])
+        store_words(0, 5, nc.sync)
+
+        turned = bank(2, [P, 2, 2, P])
+        for i, pairs in enumerate((pairs5, pairs6)):
+            for h in range(2):
+                turn(turned[:, i], pairs, h)
+        joined = keep.tile([P, 2, P, 2], F32, align_bytes=256)
+        nc.scalar.copy(out=joined[:], in_=turned[:].rearrange("p n h u -> p n u h"))
+        pairs7 = ring.tile([P, 2, P, 2], BF16, align_bytes=256, name="pairs")
+        turned7 = bank(3, [P, 2, P])
         for h in range(2):
-            turn(turned6[:, 0, h, :], LAST - 1, h)
-        gather(turned6[:], LAST - 1, 1)
-        turned7 = bank(6, [P, 1, 2, P])
-        for h in range(2):
-            nc.vector.tensor_tensor(
-                out=y_pairs[:, LAST, h], in0=by_pairs(est[LAST][:])[:, h], in1=by_pairs(sig[:])[:, h], op=MULT
-            )
-            turn(turned7[:, 0, h, :], LAST, h)
-        product(LAST, sig)
-        gather(turned7[:], LAST, 1)
-        quantize_y(LAST - 1, LAST)
-        store_words(LAST - 1, LAST, nc.sync)
-        quantize_y(LAST, TILES)
-        store_words(LAST, TILES, nc.scalar)
-        store_scales(0, TILES, [nc.sync, nc.sync, nc.scalar, nc.sync])
+            nc.vector.tensor_tensor(out=pairs7[:, h], in0=by_pairs(est7[:])[:, h], in1=by_pairs(sig[:])[:, h], op=MULT)
+            turn(turned7, pairs7, h)
+        product(n, est7, sig)
+        store_y(n)
+        joined7 = gather(turned7)
+        quantize_y(5, 7, joined[:].rearrange("p n u h -> p (n u h)"))
+        store_words(5, 7, nc.sync)
+        quantize_y(7, 8, joined7)
+        store_words(7, 8, nc.scalar)
+        store_scales([nc.sync, nc.sync, nc.scalar, nc.sync])

@@ -46,9 +46,8 @@ def tile_amortised_ivector_shrinkage_k3_kernel(
         a_codes = keep.tile([P, GROUPS, R], U32, align_bytes=256)
         v_codes = keep.tile([P, GROUPS, R], U32, align_bytes=256)
         f_early = keep.tile([P, EARLY_GROUPS, U], U8, align_bytes=256)
-        t_early = keep.tile([P, EARLY_GROUPS, R], U8, align_bytes=256)
+        t_plane = keep.tile([P, GROUPS, R], U8, align_bytes=256)
         f_late = keep.tile([P, GROUPS - EARLY_GROUPS, U], U8, align_bytes=256)
-        t_late = keep.tile([P, GROUPS - EARLY_GROUPS, R], U8, align_bytes=256)
         a_packed = keep.tile([P, 1, R], U8, align_bytes=256)
         a_last = keep.tile([P, 1, R], U8, align_bytes=256)
         v_plane = keep.tile([P, GROUPS, R], U8, align_bytes=256)
@@ -68,8 +67,8 @@ def tile_amortised_ivector_shrinkage_k3_kernel(
         def bank(b, shape):
             return psum.tile(shape, F32, name="bank%d" % b, tag="bank%d" % b)
 
-        def plane_of(early, late, g):
-            return early[:, g, :] if g < EARLY_GROUPS else late[:, g - EARLY_GROUPS, :]
+        def f_plane(g):
+            return f_early[:, g, :] if g < EARLY_GROUPS else f_late[:, g - EARLY_GROUPS, :]
 
         def clear(plane):
             nc.vector.memset(plane[:].rearrange("p g n -> p (g n)").bitcast(I32), 0)
@@ -103,7 +102,7 @@ def tile_amortised_ivector_shrinkage_k3_kernel(
             nc.tensor.matmul_mx(
                 out=acc[:],
                 lhsT=held.bitcast(FP8X4),
-                lhsT_scale=plane_of(f_early, f_late, g)[:, P * n : P * (n + 1)],
+                lhsT_scale=f_plane(g)[:, P * n : P * (n + 1)],
                 rhs=codes,
                 rhs_scale=plane,
                 start=start,
@@ -111,7 +110,7 @@ def tile_amortised_ivector_shrinkage_k3_kernel(
             )
 
         def t_pass(est, n, g):
-            mx_pass(est, n, g, t_codes[:, g, :].bitcast(FP4X4), plane_of(t_early, t_late, g), g == 0, False)
+            mx_pass(est, n, g, t_codes[:, g, :].bitcast(FP4X4), t_plane[:, g, :], g == 0, False)
 
         def a_pass(est, n, g):
             plane = a_packed[4 * g : P, 0, :] if g < PACKED else a_last[:, 0, :]
@@ -191,27 +190,24 @@ def tile_amortised_ivector_shrinkage_k3_kernel(
                     rhs=moving.bitcast(FP8X4), rhs_scale=warm_plane[:], start=True, stop=True,
                 )
 
-        clear(t_early)
-        clear(f_late)
         clear(f_early)
+        clear(t_plane)
+        clear(f_late)
+        clear(a_packed)
         zeros = f_late[:].rearrange("p g n -> p (g n)").bitcast(BF16)
         nc.vector.quantize_mx(out=warm_codes[:].bitcast(FP8X4), scales=warm_plane[:], in_=zeros[:, : 4 * WARM_N])
-        clear(a_packed)
-        clear(t_late)
         clear(a_last)
         nc.vector.memset(frames_rows[:], 0.0)
         nc.vector.memset(identity[:], 0.0)
-        nc.scalar.activation(out=warm_act[:], in_=t_late[:, 0, :].bitcast(BF16)[:, 0:1], func=SIGMOID)
+        nc.scalar.activation(out=warm_act[:], in_=a_last[:, 0, :].bitcast(BF16)[:, 0:1], func=SIGMOID)
 
-        load_scales(f_late, f_scales, EARLY_GROUPS, GROUPS, nc.gpsimd)
-        load_scales(a_last, a_scales, PACKED, GROUPS, nc.gpsimd)
         make_identity(nc, identity[:], nomemset=True)
 
         load_t(0, 1)
-        load_scales(t_early, t_scales, 0, EARLY_GROUPS, nc.sync, range(1))
+        load_scales(f_early, f_scales, 0, EARLY_GROUPS, nc.sync, range(1))
         load_f(0, 0, FIRST_TILES)
-        load_scales(t_early, t_scales, 0, EARLY_GROUPS, nc.sync, range(1, 4))
-        load_scales(f_early, f_scales, 0, EARLY_GROUPS, nc.sync)
+        load_scales(t_plane, t_scales, 0, GROUPS, nc.sync)
+        load_scales(f_early, f_scales, 0, EARLY_GROUPS, nc.sync, range(1, 4))
         load_f(0, FIRST_TILES, FRONT)
         load_a(0)
         for q in range(4):
@@ -222,7 +218,7 @@ def tile_amortised_ivector_shrinkage_k3_kernel(
         load_f(1, 0, FRONT)
         load_t(1, 3)
         load_a(1)
-        load_scales(t_late, t_scales, EARLY_GROUPS, GROUPS, nc.sync)
+        load_scales(f_late, f_scales, EARLY_GROUPS, GROUPS, nc.sync)
         load_f(2, 0, FRONT)
         load_a(2)
         load_v(0)
@@ -230,6 +226,7 @@ def tile_amortised_ivector_shrinkage_k3_kernel(
         load_t(3, 5)
         load_a(3)
         load_v(1)
+        load_scales(a_last, a_scales, PACKED, GROUPS, nc.sync)
         nc.sync.dma_start(out=frames_rows[0:P:4, :], in_=log_frames.rearrange("(n q j) -> q n j", q=4, j=32))
         load_f(4, 0, FRONT)
         load_a(4)
@@ -254,18 +251,20 @@ def tile_amortised_ivector_shrinkage_k3_kernel(
             if g == 1:
                 nc.vector.transpose(frames_cols[:], frames_rows[:])
 
-        for n in range(FRONT):
+        for n in range(TURNED):
             sig = logits(n)
             product(n, est[n], sig)
             if n > 0:
                 turn_blocks(n - 1, round_to_pairs(n - 1))
             if n < TURNED - 1:
                 store_y(n)
+        turn_blocks(TURNED - 1, round_to_pairs(TURNED - 1))
         for a in range(4):
             for q in range(4):
                 nc.sync.dma_start(out=landed[32 * q : 32 * q + 32, :, a, :], in_=staged[32 * a : 32 * a + 32, q])
-        for n in range(TURNED - 1, FRONT):
-            store_y(n)
+        store_y(TURNED - 1)
+        product(TURNED, est[TURNED], logits(TURNED))
+        store_y(TURNED)
 
         n = TILES - 2
         pairs5 = round_to_pairs(n - 1)

@@ -22,11 +22,12 @@ TILES = U // P
 EARLY_GROUPS = 2
 PACKED = 4
 FRONT = 6
-TURNED = 5
-FIRST_TILES = 3
+TURNED = 4
+COPIED = 2
+FIRST_TILES = 4
 VECTOR_COLS = 256
 WARM_N = 256
-WARM_FREE = 3
+WARM_FREE = 4
 WARM_TIED = 4
 
 
@@ -40,14 +41,16 @@ def tile_amortised_ivector_shrinkage_k3_kernel(
         psum = ctx.enter_context(tc.psum_pool(name="psum", bufs=1))
         ctx.enter_context(tc.manual_schedule())
 
-        f_front = keep.tile([P, GROUPS, P * FRONT], U32, align_bytes=256)
-        f_back = keep.tile([P, GROUPS, U - P * FRONT], U32, align_bytes=256)
+        f_first = keep.tile([P, U], U32, align_bytes=256)
+        f_front = keep.tile([P, GROUPS - 1, P * FRONT], U32, align_bytes=256)
+        f_back = keep.tile([P, GROUPS - 1, U - P * FRONT], U32, align_bytes=256)
         t_codes = keep.tile([P, GROUPS, 2 * R], U8, align_bytes=256)
         a_codes = keep.tile([P, GROUPS, R], U32, align_bytes=256)
         v_codes = keep.tile([P, GROUPS, R], U32, align_bytes=256)
         f_early = keep.tile([P, EARLY_GROUPS, U], U8, align_bytes=256)
-        t_plane = keep.tile([P, GROUPS, R], U8, align_bytes=256)
+        t_early = keep.tile([P, EARLY_GROUPS, R], U8, align_bytes=256)
         f_late = keep.tile([P, GROUPS - EARLY_GROUPS, U], U8, align_bytes=256)
+        t_late = keep.tile([P, GROUPS - EARLY_GROUPS, R], U8, align_bytes=256)
         a_packed = keep.tile([P, 1, R], U8, align_bytes=256)
         a_last = keep.tile([P, 1, R], U8, align_bytes=256)
         v_plane = keep.tile([P, GROUPS, R], U8, align_bytes=256)
@@ -58,6 +61,8 @@ def tile_amortised_ivector_shrinkage_k3_kernel(
         warm_codes = keep.tile([P, WARM_N], U32, align_bytes=256)
         warm_plane = keep.tile([P, WARM_N], U8, align_bytes=256)
         warm_act = keep.tile([P, 1], F32)
+        est_sb = keep.tile([P, COPIED, R], F32, align_bytes=256)
+        pairs = keep.tile([P, TILES, 2, P, 2], BF16, align_bytes=256)
         y = keep.tile([P, TILES, R], F32, align_bytes=256)
         staged = keep.tile([P, 4, TURNED, 64], F32, align_bytes=256)
         landed = keep.tile([P, TURNED, 4, 64], F32, align_bytes=256)
@@ -67,8 +72,8 @@ def tile_amortised_ivector_shrinkage_k3_kernel(
         def bank(b, shape):
             return psum.tile(shape, F32, name="bank%d" % b, tag="bank%d" % b)
 
-        def f_plane(g):
-            return f_early[:, g, :] if g < EARLY_GROUPS else f_late[:, g - EARLY_GROUPS, :]
+        def plane_of(early, late, g):
+            return early[:, g, :] if g < EARLY_GROUPS else late[:, g - EARLY_GROUPS, :]
 
         def clear(plane):
             nc.vector.memset(plane[:].rearrange("p g n -> p (g n)").bitcast(I32), 0)
@@ -80,7 +85,8 @@ def tile_amortised_ivector_shrinkage_k3_kernel(
 
         def load_f(g, n0, n1):
             src = f_words[g].rearrange("p n t -> p (n t)")[:, 4 * P * n0 : 4 * P * n1]
-            nc.sync.dma_start(out=f_front[:, g, P * n0 : P * n1].bitcast(I32), in_=src.bitcast(I32))
+            dst = f_first[:, P * n0 : P * n1] if g == 0 else f_front[:, g - 1, P * n0 : P * n1]
+            nc.sync.dma_start(out=dst.bitcast(I32), in_=src.bitcast(I32))
 
         def load_t(g0, g1):
             src = t_words[g0:g1].rearrange("g p n -> p g n")
@@ -95,14 +101,16 @@ def tile_amortised_ivector_shrinkage_k3_kernel(
             nc.sync.dma_start(out=v_rows[g][:], in_=src)
 
         def mx_pass(acc, n, g, codes, plane, start, stop):
-            if n < FRONT:
-                held = f_front[:, g, P * n : P * (n + 1)]
+            if g == 0:
+                held = f_first[:, P * n : P * (n + 1)]
+            elif n < FRONT:
+                held = f_front[:, g - 1, P * n : P * (n + 1)]
             else:
-                held = f_back[:, g, P * (n - FRONT) : P * (n - FRONT + 1)]
+                held = f_back[:, g - 1, P * (n - FRONT) : P * (n - FRONT + 1)]
             nc.tensor.matmul_mx(
                 out=acc[:],
                 lhsT=held.bitcast(FP8X4),
-                lhsT_scale=f_plane(g)[:, P * n : P * (n + 1)],
+                lhsT_scale=plane_of(f_early, f_late, g)[:, P * n : P * (n + 1)],
                 rhs=codes,
                 rhs_scale=plane,
                 start=start,
@@ -110,7 +118,7 @@ def tile_amortised_ivector_shrinkage_k3_kernel(
             )
 
         def t_pass(est, n, g):
-            mx_pass(est, n, g, t_codes[:, g, :].bitcast(FP4X4), t_plane[:, g, :], g == 0, False)
+            mx_pass(est, n, g, t_codes[:, g, :].bitcast(FP4X4), plane_of(t_early, t_late, g), g == 0, False)
 
         def a_pass(est, n, g):
             plane = a_packed[4 * g : P, 0, :] if g < PACKED else a_last[:, 0, :]
@@ -132,16 +140,23 @@ def tile_amortised_ivector_shrinkage_k3_kernel(
                 in_=grouped[:].rearrange("p n t -> p (n t)"),
             )
 
+        def z_pass(z, n, g):
+            mx_pass(z, n, g, v_codes[:, g, :].bitcast(FP8X4), v_plane[:, g, :], g == 0, g == GROUPS - 1)
+
         def logits(n):
-            z = bank(FRONT + n % 2, [P, R])
+            z = bank(n % COPIED, [P, R])
             for g in range(GROUPS):
-                mx_pass(z, n, g, v_codes[:, g, :].bitcast(FP8X4), v_plane[:, g, :], g == 0, g == GROUPS - 1)
+                z_pass(z, n, g)
+            return gate(z, n)
+
+        def gate(z, n):
             sig = ring.tile([P, R], F32, align_bytes=256, name="sig")
             nc.scalar.activation(out=sig[:], in_=z[:], func=SIGMOID, bias=frames_cols[:, 4 * n : 4 * n + 1])
             return sig
 
-        def product(n, est, sig):
-            nc.vector.tensor_tensor(out=y[:, n, :], in0=est[:], in1=sig[:], op=MULT)
+        def product(n, sig):
+            src = est_sb[:, n, :] if n < COPIED else est[n][:]
+            nc.vector.tensor_tensor(out=y[:, n, :], in0=src, in1=sig[:], op=MULT)
 
         def store_y(n):
             nc.sync.dma_start(out=out_0[P * n : P * (n + 1), :], in_=y[:, n, :])
@@ -150,25 +165,24 @@ def tile_amortised_ivector_shrinkage_k3_kernel(
             return ap.rearrange("u (p h e) -> u h p e", h=2, e=2)
 
         def round_to_pairs(n):
-            pairs = ring.tile([P, 2, P, 2], BF16, align_bytes=256, name="pairs")
-            nc.scalar.copy(out=pairs[:], in_=by_pairs(y[:, n, :]))
-            return pairs
+            nc.vector.tensor_copy(out=pairs[:, n], in_=by_pairs(y[:, n, :]))
 
-        def turn_blocks(n, pairs):
+        def turn_blocks(n):
             blocks = ring.tile([P, 2 * P], F32, align_bytes=256, name="blocks")
-            nc.vector.transpose(blocks[:], pairs[:].rearrange("u h p e -> u (h p e)").bitcast(F32))
-            nc.vector.tensor_copy(
+            nc.vector.transpose(blocks[:], pairs[:, n].rearrange("u h p e -> u (h p e)").bitcast(F32))
+            return blocks
+
+        def stage(n, blocks):
+            nc.scalar.copy(
                 out=staged[:, :, n, :].rearrange("p q (i h) -> p q i h", h=2),
                 in_=blocks[:].rearrange("p (h q i) -> p q i h", h=2, q=4),
             )
 
-        def turn(dst, pairs, h):
-            nc.tensor.transpose(dst[:, h, :], pairs[:, h].rearrange("u p e -> u (p e)").bitcast(F32), identity[:])
+        def turn(dst, n, h):
+            nc.tensor.transpose(dst[:, h, :], pairs[:, n, h].rearrange("u p e -> u (p e)").bitcast(F32), identity[:])
 
-        def gather(turned):
-            joined = ring.tile([P, P, 2], F32, align_bytes=256, name="joined")
-            nc.scalar.copy(out=joined[:], in_=turned[:].rearrange("p h u -> p u h"))
-            return joined[:].rearrange("p u h -> p (u h)")
+        def gather(turned, dst):
+            nc.scalar.copy(out=dst, in_=turned.rearrange("p n h u -> p n u h"))
 
         def quantize_y(n0, n1, words):
             cols = slice(P * n0, P * n1)
@@ -190,25 +204,26 @@ def tile_amortised_ivector_shrinkage_k3_kernel(
                     rhs=moving.bitcast(FP8X4), rhs_scale=warm_plane[:], start=True, stop=True,
                 )
 
-        clear(f_early)
-        clear(t_plane)
+        clear(t_early)
         clear(f_late)
-        clear(a_packed)
+        clear(f_early)
         zeros = f_late[:].rearrange("p g n -> p (g n)").bitcast(BF16)
         nc.vector.quantize_mx(out=warm_codes[:].bitcast(FP8X4), scales=warm_plane[:], in_=zeros[:, : 4 * WARM_N])
+        clear(a_packed)
+        clear(t_late)
         clear(a_last)
         nc.vector.memset(frames_rows[:], 0.0)
         nc.vector.memset(identity[:], 0.0)
-        nc.scalar.activation(out=warm_act[:], in_=a_last[:, 0, :].bitcast(BF16)[:, 0:1], func=SIGMOID)
+        nc.scalar.activation(out=warm_act[:], in_=t_late[:, 0, :].bitcast(BF16)[:, 0:1], func=SIGMOID)
 
         make_identity(nc, identity[:], nomemset=True)
 
         load_t(0, 1)
-        load_scales(f_early, f_scales, 0, EARLY_GROUPS, nc.sync, range(1))
+        load_scales(t_early, t_scales, 0, EARLY_GROUPS, nc.sync, range(1))
         load_f(0, 0, FIRST_TILES)
-        load_scales(t_plane, t_scales, 0, GROUPS, nc.sync)
-        load_scales(f_early, f_scales, 0, EARLY_GROUPS, nc.sync, range(1, 4))
-        load_f(0, FIRST_TILES, FRONT)
+        load_scales(t_early, t_scales, 0, EARLY_GROUPS, nc.sync, range(1, 4))
+        load_scales(f_early, f_scales, 0, EARLY_GROUPS, nc.sync)
+        load_f(0, FIRST_TILES, TILES)
         load_a(0)
         for q in range(4):
             nc.sync.dma_start(
@@ -220,6 +235,7 @@ def tile_amortised_ivector_shrinkage_k3_kernel(
         load_a(1)
         load_scales(f_late, f_scales, EARLY_GROUPS, GROUPS, nc.sync)
         load_f(2, 0, FRONT)
+        load_scales(t_late, t_scales, EARLY_GROUPS, GROUPS, nc.sync)
         load_a(2)
         load_v(0)
         load_f(3, 0, FRONT)
@@ -232,78 +248,87 @@ def tile_amortised_ivector_shrinkage_k3_kernel(
         load_a(4)
         for g in range(2, GROUPS):
             load_v(g)
-        back = f_words.rearrange("g p n t -> p g (n t)")[:, :, 4 * P * FRONT :]
+        back = f_words[1:GROUPS].rearrange("g p n t -> p g (n t)")[:, :, 4 * P * FRONT :]
         nc.sync.dma_start(out=f_back[:].bitcast(I32), in_=back.bitcast(I32))
 
         warm = bank(TILES - 1, [P, WARM_N])
         warm_passes(WARM_FREE, warm_codes[:])
-        warm_passes(WARM_TIED, f_front[:, 0, 0:WARM_N])
+        warm_passes(WARM_TIED, f_first[:, 0:WARM_N])
 
-        est = [bank(n, [P, R]) for n in range(FRONT)]
-        for g in range(GROUPS):
-            for n in range(FRONT):
+        est = [bank(n, [P, R]) for n in range(TILES)]
+        for g in range(GROUPS - 1):
+            tiles = range(TILES if g == 0 else FRONT)
+            for n in tiles:
                 t_pass(est[n], n, g)
-            for n in range(FRONT):
+            for n in tiles:
                 a_pass(est[n], n, g)
+        for n in range(FRONT - 1):
+            t_pass(est[n], n, GROUPS - 1)
+            a_pass(est[n], n, GROUPS - 1)
 
         for g in range(GROUPS):
+            if g == GROUPS - 1:
+                for n in range(COPIED):
+                    nc.scalar.copy(out=est_sb[:, n, :], in_=est[n][:])
             quantize_v(g, interleave_v(g))
-            if g == 1:
+            if g == 2:
                 nc.vector.transpose(frames_cols[:], frames_rows[:])
 
+        woven = [bank(n, [P, R]) for n in range(COPIED)]
+        for groups in (range(GROUPS - 1), range(GROUPS - 1, GROUPS)):
+            for n in range(COPIED):
+                for g in groups:
+                    z_pass(woven[n], n, g)
+        t_pass(est[FRONT - 1], FRONT - 1, GROUPS - 1)
+        a_pass(est[FRONT - 1], FRONT - 1, GROUPS - 1)
+        blocks = {}
         for n in range(TURNED):
-            sig = logits(n)
-            product(n, est[n], sig)
+            product(n, gate(woven[n], n) if n < COPIED else logits(n))
+            if n > 1:
+                stage(n - 2, blocks[n - 2])
             if n > 0:
-                turn_blocks(n - 1, round_to_pairs(n - 1))
-            if n < TURNED - 1:
-                store_y(n)
-        turn_blocks(TURNED - 1, round_to_pairs(TURNED - 1))
+                blocks[n - 1] = turn_blocks(n - 1)
+                store_y(n - 1)
+            round_to_pairs(n)
+        sig = logits(TURNED)
+        stage(TURNED - 2, blocks[TURNED - 2])
+        stage(TURNED - 1, turn_blocks(TURNED - 1))
         for a in range(4):
             for q in range(4):
                 nc.sync.dma_start(out=landed[32 * q : 32 * q + 32, :, a, :], in_=staged[32 * a : 32 * a + 32, q])
         store_y(TURNED - 1)
-        product(TURNED, est[TURNED], logits(TURNED))
-        store_y(TURNED)
 
-        n = TILES - 2
-        pairs5 = round_to_pairs(n - 1)
-        sig = logits(n)
-        est6 = bank(0, [P, R])
-        for g in range(GROUPS):
-            t_pass(est6, n, g)
-            a_pass(est6, n, g)
-        product(n, est6, sig)
-        store_y(n)
-        pairs6 = round_to_pairs(n)
+        last = TILES - 1
+        for n in range(TURNED, TILES):
+            if n > TURNED:
+                sig = logits(n)
+            if n >= FRONT:
+                for g in range(1, GROUPS):
+                    t_pass(est[n], n, g)
+                    a_pass(est[n], n, g)
+            if n < last:
+                product(n, sig)
+                store_y(n)
+                round_to_pairs(n)
+        quantize_y(0, TURNED, landed[:].rearrange("p n a w -> p (n a w)"))
+        store_words(0, TURNED, nc.sync)
 
-        n = TILES - 1
-        sig = logits(n)
-        est7 = bank(1, [P, R])
-        for g in range(GROUPS):
-            t_pass(est7, n, g)
-            a_pass(est7, n, g)
-        flat = landed[:].rearrange("p n a w -> p (n a w)")
-        quantize_y(0, 4, flat[:, : 4 * 2 * P])
-        quantize_y(4, 5, flat[:, 4 * 2 * P :])
-        store_words(0, 5, nc.sync)
-
-        turned = bank(2, [P, 2, 2, P])
-        for i, pairs in enumerate((pairs5, pairs6)):
+        joined = [keep.tile([P, 2, P, 2], F32, align_bytes=256, name="joined%d" % i) for i in range(2)]
+        turned = [bank(b, [P, 2, 2, P]) for b in (2, 3, 4)]
+        for n in (6, 4, 5):
             for h in range(2):
-                turn(turned[:, i], pairs, h)
-        joined = keep.tile([P, 2, P, 2], F32, align_bytes=256)
-        nc.scalar.copy(out=joined[:], in_=turned[:].rearrange("p n h u -> p n u h"))
-        pairs7 = ring.tile([P, 2, P, 2], BF16, align_bytes=256, name="pairs")
-        turned7 = bank(3, [P, 2, P])
+                turn(turned[(n - TURNED) // 2][:, n % 2], n, h)
+        gather(turned[1][:, 0:1], joined[1][:, 0:1])
+        gather(turned[0][:], joined[0][:])
         for h in range(2):
-            nc.vector.tensor_tensor(out=pairs7[:, h], in0=by_pairs(est7[:])[:, h], in1=by_pairs(sig[:])[:, h], op=MULT)
-            turn(turned7, pairs7, h)
-        product(n, est7, sig)
-        store_y(n)
-        joined7 = gather(turned7)
-        quantize_y(5, 7, joined[:].rearrange("p n u h -> p (n u h)"))
-        store_words(5, 7, nc.sync)
-        quantize_y(7, 8, joined7)
-        store_words(7, 8, nc.scalar)
+            nc.vector.tensor_tensor(
+                out=pairs[:, last, h], in0=by_pairs(est[last][:])[:, h], in1=by_pairs(sig[:])[:, h], op=MULT
+            )
+            turn(turned[2][:, 0], last, h)
+        product(last, sig)
+        store_y(last)
+        gather(turned[2][:, 0:1], joined[1][:, 1:2])
+        for i in range(2):
+            quantize_y(TURNED + 2 * i, TURNED + 2 * i + 2, joined[i][:].rearrange("p n u h -> p (n u h)"))
+            store_words(TURNED + 2 * i, TURNED + 2 * i + 2, (nc.sync, nc.scalar)[i])
         store_scales([nc.sync, nc.sync, nc.scalar, nc.sync])

@@ -24,11 +24,12 @@ PACKED = 4
 FRONT = 6
 TURNED = 4
 COPIED = 2
+FULL = 2
 FIRST_TILES = 4
 VECTOR_COLS = 256
 WARM_N = 256
-WARM_FREE = 4
-WARM_TIED = 4
+WARM_FREE = 7
+WARM_TIED = 5
 
 
 def tile_amortised_ivector_shrinkage_k3_kernel(
@@ -41,9 +42,9 @@ def tile_amortised_ivector_shrinkage_k3_kernel(
         psum = ctx.enter_context(tc.psum_pool(name="psum", bufs=1))
         ctx.enter_context(tc.manual_schedule())
 
-        f_first = keep.tile([P, U], U32, align_bytes=256)
-        f_front = keep.tile([P, GROUPS - 1, P * FRONT], U32, align_bytes=256)
-        f_back = keep.tile([P, GROUPS - 1, U - P * FRONT], U32, align_bytes=256)
+        f_first = keep.tile([P, FULL, U], U32, align_bytes=256)
+        f_front = keep.tile([P, GROUPS - FULL, P * FRONT], U32, align_bytes=256)
+        f_back = keep.tile([P, GROUPS - FULL, U - P * FRONT], U32, align_bytes=256)
         t_codes = keep.tile([P, GROUPS, 2 * R], U8, align_bytes=256)
         a_codes = keep.tile([P, GROUPS, R], U32, align_bytes=256)
         v_codes = keep.tile([P, GROUPS, R], U32, align_bytes=256)
@@ -58,6 +59,7 @@ def tile_amortised_ivector_shrinkage_k3_kernel(
         frames_rows = keep.tile([P, 32], BF16, align_bytes=64)
         frames_cols = keep.tile([P, 32], BF16, align_bytes=64)
         identity = keep.tile([P, P], F32, align_bytes=256)
+        warm_in = keep.tile([P, 4 * WARM_N], BF16, align_bytes=256)
         warm_codes = keep.tile([P, WARM_N], U32, align_bytes=256)
         warm_plane = keep.tile([P, WARM_N], U8, align_bytes=256)
         warm_act = keep.tile([P, 1], F32)
@@ -85,7 +87,7 @@ def tile_amortised_ivector_shrinkage_k3_kernel(
 
         def load_f(g, n0, n1):
             src = f_words[g].rearrange("p n t -> p (n t)")[:, 4 * P * n0 : 4 * P * n1]
-            dst = f_first[:, P * n0 : P * n1] if g == 0 else f_front[:, g - 1, P * n0 : P * n1]
+            dst = f_first[:, g, P * n0 : P * n1] if g < FULL else f_front[:, g - FULL, P * n0 : P * n1]
             nc.sync.dma_start(out=dst.bitcast(I32), in_=src.bitcast(I32))
 
         def load_t(g0, g1):
@@ -101,12 +103,12 @@ def tile_amortised_ivector_shrinkage_k3_kernel(
             nc.sync.dma_start(out=v_rows[g][:], in_=src)
 
         def mx_pass(acc, n, g, codes, plane, start, stop):
-            if g == 0:
-                held = f_first[:, P * n : P * (n + 1)]
+            if g < FULL:
+                held = f_first[:, g, P * n : P * (n + 1)]
             elif n < FRONT:
-                held = f_front[:, g - 1, P * n : P * (n + 1)]
+                held = f_front[:, g - FULL, P * n : P * (n + 1)]
             else:
-                held = f_back[:, g - 1, P * (n - FRONT) : P * (n - FRONT + 1)]
+                held = f_back[:, g - FULL, P * (n - FRONT) : P * (n - FRONT + 1)]
             nc.tensor.matmul_mx(
                 out=acc[:],
                 lhsT=held.bitcast(FP8X4),
@@ -124,13 +126,14 @@ def tile_amortised_ivector_shrinkage_k3_kernel(
             plane = a_packed[4 * g : P, 0, :] if g < PACKED else a_last[:, 0, :]
             mx_pass(est, n, g, a_codes[:, g, :].bitcast(FP8X4), plane, False, g == GROUPS - 1)
 
-        def interleave_v(g):
+        def interleave_v(g, vector_cols):
             grouped = ring.tile([P, R, 4], BF16, align_bytes=256, name="v_grouped")
             src = v_rows[g][:].rearrange("p t (c i) -> p c t i", i=4)
             dst = grouped[:].rearrange("p (c i) t -> p c t i", i=4)
-            split = VECTOR_COLS // 4
+            split = vector_cols // 4
             nc.vector.tensor_copy(out=dst[:, :split], in_=src[:, :split])
-            nc.scalar.copy(out=dst[:, split:], in_=src[:, split:])
+            if vector_cols < R:
+                nc.scalar.copy(out=dst[:, split:], in_=src[:, split:])
             return grouped
 
         def quantize_v(g, grouped):
@@ -205,16 +208,16 @@ def tile_amortised_ivector_shrinkage_k3_kernel(
                 )
 
         clear(t_early)
-        clear(f_late)
+        nc.vector.memset(warm_in[:].bitcast(I32), 0x3F803F80)
         clear(f_early)
-        zeros = f_late[:].rearrange("p g n -> p (g n)").bitcast(BF16)
-        nc.vector.quantize_mx(out=warm_codes[:].bitcast(FP8X4), scales=warm_plane[:], in_=zeros[:, : 4 * WARM_N])
+        nc.vector.quantize_mx(out=warm_codes[:].bitcast(FP8X4), scales=warm_plane[:], in_=warm_in[:])
         clear(a_packed)
+        clear(f_late)
         clear(t_late)
         clear(a_last)
         nc.vector.memset(frames_rows[:], 0.0)
         nc.vector.memset(identity[:], 0.0)
-        nc.scalar.activation(out=warm_act[:], in_=t_late[:, 0, :].bitcast(BF16)[:, 0:1], func=SIGMOID)
+        nc.scalar.activation(out=warm_act[:], in_=warm_in[:, 0:1], func=SIGMOID)
 
         make_identity(nc, identity[:], nomemset=True)
 
@@ -230,7 +233,7 @@ def tile_amortised_ivector_shrinkage_k3_kernel(
                 out=a_packed[32 * q : 32 * q + 4 * PACKED, 0, :].bitcast(I32),
                 in_=a_scales[0:PACKED, 4 * q : 4 * q + 4, :].bitcast(I32),
             )
-        load_f(1, 0, FRONT)
+        load_f(1, 0, TILES)
         load_t(1, 3)
         load_a(1)
         load_scales(f_late, f_scales, EARLY_GROUPS, GROUPS, nc.sync)
@@ -244,33 +247,35 @@ def tile_amortised_ivector_shrinkage_k3_kernel(
         load_v(1)
         load_scales(a_last, a_scales, PACKED, GROUPS, nc.sync)
         nc.sync.dma_start(out=frames_rows[0:P:4, :], in_=log_frames.rearrange("(n q j) -> q n j", q=4, j=32))
+        load_v(2)
         load_f(4, 0, FRONT)
         load_a(4)
-        for g in range(2, GROUPS):
-            load_v(g)
-        back = f_words[1:GROUPS].rearrange("g p n t -> p g (n t)")[:, :, 4 * P * FRONT :]
+        load_v(3)
+        load_v(4)
+        back = f_words[FULL:GROUPS].rearrange("g p n t -> p g (n t)")[:, :, 4 * P * FRONT :]
         nc.sync.dma_start(out=f_back[:].bitcast(I32), in_=back.bitcast(I32))
 
         warm = bank(TILES - 1, [P, WARM_N])
         warm_passes(WARM_FREE, warm_codes[:])
-        warm_passes(WARM_TIED, f_first[:, 0:WARM_N])
+        warm_passes(WARM_TIED, f_first[:, 0, 0:WARM_N])
 
         est = [bank(n, [P, R]) for n in range(TILES)]
         for g in range(GROUPS - 1):
-            tiles = range(TILES if g == 0 else FRONT)
+            tiles = range(TILES if g < FULL else FRONT)
             for n in tiles:
                 t_pass(est[n], n, g)
             for n in tiles:
                 a_pass(est[n], n, g)
-        for n in range(FRONT - 1):
+        for n in range(FRONT - 2):
             t_pass(est[n], n, GROUPS - 1)
             a_pass(est[n], n, GROUPS - 1)
+        t_pass(est[FRONT - 2], FRONT - 2, GROUPS - 1)
 
         for g in range(GROUPS):
-            if g == GROUPS - 1:
+            if g == GROUPS - 2:
                 for n in range(COPIED):
                     nc.scalar.copy(out=est_sb[:, n, :], in_=est[n][:])
-            quantize_v(g, interleave_v(g))
+            quantize_v(g, interleave_v(g, R if g == GROUPS - 2 else VECTOR_COLS))
             if g == 2:
                 nc.vector.transpose(frames_cols[:], frames_rows[:])
 
@@ -279,10 +284,11 @@ def tile_amortised_ivector_shrinkage_k3_kernel(
             for n in range(COPIED):
                 for g in groups:
                     z_pass(woven[n], n, g)
+        a_pass(est[FRONT - 2], FRONT - 2, GROUPS - 1)
         t_pass(est[FRONT - 1], FRONT - 1, GROUPS - 1)
         a_pass(est[FRONT - 1], FRONT - 1, GROUPS - 1)
         blocks = {}
-        for n in range(TURNED):
+        for n in range(TURNED - 1):
             product(n, gate(woven[n], n) if n < COPIED else logits(n))
             if n > 1:
                 stage(n - 2, blocks[n - 2])
@@ -290,12 +296,20 @@ def tile_amortised_ivector_shrinkage_k3_kernel(
                 blocks[n - 1] = turn_blocks(n - 1)
                 store_y(n - 1)
             round_to_pairs(n)
+        n = TURNED - 1
+        sig = logits(n)
+        blocks[n - 1] = turn_blocks(n - 1)
+        nc.vector.tensor_tensor(out=pairs[:, n], in0=by_pairs(est[n][:]), in1=by_pairs(sig[:]), op=MULT)
+        blocks[n] = turn_blocks(n)
+        product(n, sig)
+        stage(n - 2, blocks[n - 2])
+        stage(n - 1, blocks[n - 1])
         sig = logits(TURNED)
-        stage(TURNED - 2, blocks[TURNED - 2])
-        stage(TURNED - 1, turn_blocks(TURNED - 1))
+        stage(n, blocks[n])
         for a in range(4):
             for q in range(4):
                 nc.sync.dma_start(out=landed[32 * q : 32 * q + 32, :, a, :], in_=staged[32 * a : 32 * a + 32, q])
+        store_y(TURNED - 2)
         store_y(TURNED - 1)
 
         last = TILES - 1
@@ -303,7 +317,7 @@ def tile_amortised_ivector_shrinkage_k3_kernel(
             if n > TURNED:
                 sig = logits(n)
             if n >= FRONT:
-                for g in range(1, GROUPS):
+                for g in range(FULL, GROUPS):
                     t_pass(est[n], n, g)
                     a_pass(est[n], n, g)
             if n < last:

@@ -26,7 +26,8 @@ TURNED = 4
 COPIED = 2
 FULL = 2
 FIRST_TILES = 4
-VECTOR_COLS = 256
+VECTOR_COLS = 320
+HALF = R // 2
 WARM_N = 256
 WARM_FREE = 7
 WARM_TIED = 5
@@ -50,7 +51,8 @@ def tile_amortised_ivector_shrinkage_k3_kernel(
         v_codes = keep.tile([P, GROUPS, R], U32, align_bytes=256)
         f_early = keep.tile([P, EARLY_GROUPS, U], U8, align_bytes=256)
         t_early = keep.tile([P, EARLY_GROUPS, R], U8, align_bytes=256)
-        f_late = keep.tile([P, GROUPS - EARLY_GROUPS, U], U8, align_bytes=256)
+        f_late = keep.tile([P, GROUPS - EARLY_GROUPS, P * FRONT], U8, align_bytes=256)
+        f_late_back = keep.tile([P, GROUPS - EARLY_GROUPS, U - P * FRONT], U8, align_bytes=256)
         t_late = keep.tile([P, GROUPS - EARLY_GROUPS, R], U8, align_bytes=256)
         a_packed = keep.tile([P, 1, R], U8, align_bytes=256)
         a_last = keep.tile([P, 1, R], U8, align_bytes=256)
@@ -80,10 +82,10 @@ def tile_amortised_ivector_shrinkage_k3_kernel(
         def clear(plane):
             nc.vector.memset(plane[:].rearrange("p g n -> p (g n)").bitcast(I32), 0)
 
-        def load_scales(plane, scales, g0, g1, queue, which=range(4)):
+        def load_scales(plane, scales, g0, g1, queue, which=range(4), first=0):
             rows = scales.rearrange("g (q r) n -> r q g n", r=4)
             for r in which:
-                queue.dma_start(out=plane[r:P:32, :, :].bitcast(I32), in_=rows[r][:, g0:g1, :].bitcast(I32))
+                queue.dma_start(out=plane[first + r : P : 32, :, :].bitcast(I32), in_=rows[r][:, g0:g1, :].bitcast(I32))
 
         def load_f(g, n0, n1):
             src = f_words[g].rearrange("p n t -> p (n t)")[:, 4 * P * n0 : 4 * P * n1]
@@ -105,26 +107,45 @@ def tile_amortised_ivector_shrinkage_k3_kernel(
         def mx_pass(acc, n, g, codes, plane, start, stop):
             if g < FULL:
                 held = f_first[:, g, P * n : P * (n + 1)]
+                held_plane = f_early[:, g, P * n : P * (n + 1)]
             elif n < FRONT:
                 held = f_front[:, g - FULL, P * n : P * (n + 1)]
+                held_plane = f_late[:, g - FULL, P * n : P * (n + 1)]
             else:
                 held = f_back[:, g - FULL, P * (n - FRONT) : P * (n - FRONT + 1)]
+                held_plane = f_late_back[:, g - FULL, P * (n - FRONT) : P * (n - FRONT + 1)]
             nc.tensor.matmul_mx(
-                out=acc[:],
+                out=acc,
                 lhsT=held.bitcast(FP8X4),
-                lhsT_scale=plane_of(f_early, f_late, g)[:, P * n : P * (n + 1)],
+                lhsT_scale=held_plane,
                 rhs=codes,
                 rhs_scale=plane,
                 start=start,
                 stop=stop,
             )
 
+        def t_part(acc, n, g, start, c0, c1):
+            codes = t_codes[:, g, 2 * c0 : 2 * c1].bitcast(FP4X4)
+            mx_pass(acc, n, g, codes, plane_of(t_early, t_late, g)[:, c0:c1], start, False)
+
+        def a_part(acc, n, g, start, c0, c1):
+            plane = a_packed[4 * g : P, 0, c0:c1] if g < PACKED else a_last[4:P, 0, c0:c1]
+            mx_pass(acc, n, g, a_codes[:, g, c0:c1].bitcast(FP8X4), plane, start, g == GROUPS - 1)
+
         def t_pass(est, n, g):
-            mx_pass(est, n, g, t_codes[:, g, :].bitcast(FP4X4), plane_of(t_early, t_late, g), g == 0, False)
+            t_part(est[:], n, g, g == 0, 0, R)
 
         def a_pass(est, n, g):
-            plane = a_packed[4 * g : P, 0, :] if g < PACKED else a_last[:, 0, :]
-            mx_pass(est, n, g, a_codes[:, g, :].bitcast(FP8X4), plane, False, g == GROUPS - 1)
+            a_part(est[:], n, g, False, 0, R)
+
+        def half_passes(acc, k, g):
+            c0 = HALF * k
+            if g == 0:
+                a_part(acc[:], TILES - 1, g, True, c0, c0 + HALF)
+            for c in range(0, HALF, P):
+                t_part(acc[:, c : c + P], TILES - 1, g, False, c0 + c, c0 + c + P)
+            if g > 0:
+                a_part(acc[:], TILES - 1, g, False, c0, c0 + HALF)
 
         def interleave_v(g, vector_cols):
             grouped = ring.tile([P, R, 4], BF16, align_bytes=256, name="v_grouped")
@@ -144,7 +165,7 @@ def tile_amortised_ivector_shrinkage_k3_kernel(
             )
 
         def z_pass(z, n, g):
-            mx_pass(z, n, g, v_codes[:, g, :].bitcast(FP8X4), v_plane[:, g, :], g == 0, g == GROUPS - 1)
+            mx_pass(z[:], n, g, v_codes[:, g, :].bitcast(FP8X4), v_plane[:, g, :], g == 0, g == GROUPS - 1)
 
         def logits(n):
             z = bank(n % COPIED, [P, R])
@@ -184,8 +205,8 @@ def tile_amortised_ivector_shrinkage_k3_kernel(
         def turn(dst, n, h):
             nc.tensor.transpose(dst[:, h, :], pairs[:, n, h].rearrange("u p e -> u (p e)").bitcast(F32), identity[:])
 
-        def gather(turned, dst):
-            nc.scalar.copy(out=dst, in_=turned.rearrange("p n h u -> p n u h"))
+        def gather(turned, dst, copy):
+            copy(out=dst, in_=turned.rearrange("p h u -> p u h"))
 
         def quantize_y(n0, n1, words):
             cols = slice(P * n0, P * n1)
@@ -215,6 +236,7 @@ def tile_amortised_ivector_shrinkage_k3_kernel(
         clear(f_late)
         clear(t_late)
         clear(a_last)
+        clear(f_late_back)
         nc.vector.memset(frames_rows[:], 0.0)
         nc.vector.memset(identity[:], 0.0)
         nc.scalar.activation(out=warm_act[:], in_=warm_in[:, 0:1], func=SIGMOID)
@@ -236,7 +258,7 @@ def tile_amortised_ivector_shrinkage_k3_kernel(
         load_f(1, 0, TILES)
         load_t(1, 3)
         load_a(1)
-        load_scales(f_late, f_scales, EARLY_GROUPS, GROUPS, nc.sync)
+        load_scales(f_late, f_scales[:, :, 0 : P * FRONT], EARLY_GROUPS, GROUPS, nc.sync)
         load_f(2, 0, FRONT)
         load_scales(t_late, t_scales, EARLY_GROUPS, GROUPS, nc.sync)
         load_a(2)
@@ -245,7 +267,7 @@ def tile_amortised_ivector_shrinkage_k3_kernel(
         load_t(3, 5)
         load_a(3)
         load_v(1)
-        load_scales(a_last, a_scales, PACKED, GROUPS, nc.sync)
+        load_scales(a_last, a_scales, PACKED, GROUPS, nc.sync, first=4)
         nc.sync.dma_start(out=frames_rows[0:P:4, :], in_=log_frames.rearrange("(n q j) -> q n j", q=4, j=32))
         load_v(2)
         load_f(4, 0, FRONT)
@@ -254,18 +276,22 @@ def tile_amortised_ivector_shrinkage_k3_kernel(
         load_v(4)
         back = f_words[FULL:GROUPS].rearrange("g p n t -> p g (n t)")[:, :, 4 * P * FRONT :]
         nc.sync.dma_start(out=f_back[:].bitcast(I32), in_=back.bitcast(I32))
+        load_scales(f_late_back, f_scales[:, :, P * FRONT :], EARLY_GROUPS, GROUPS, nc.sync)
 
         warm = bank(TILES - 1, [P, WARM_N])
         warm_passes(WARM_FREE, warm_codes[:])
         warm_passes(WARM_TIED, f_first[:, 0, 0:WARM_N])
 
-        est = [bank(n, [P, R]) for n in range(TILES)]
+        est = [bank(n, [P, R]) for n in range(TILES - 1)]
+        halves = [bank(TILES - 1, [P, HALF])]
         for g in range(GROUPS - 1):
-            tiles = range(TILES if g < FULL else FRONT)
+            tiles = range(TILES - 1 if g < FULL else FRONT)
             for n in tiles:
                 t_pass(est[n], n, g)
             for n in tiles:
                 a_pass(est[n], n, g)
+            if g < FULL:
+                half_passes(halves[0], 0, g)
         for n in range(FRONT - 2):
             t_pass(est[n], n, GROUPS - 1)
             a_pass(est[n], n, GROUPS - 1)
@@ -306,17 +332,18 @@ def tile_amortised_ivector_shrinkage_k3_kernel(
         stage(n - 1, blocks[n - 1])
         sig = logits(TURNED)
         stage(n, blocks[n])
+        store_y(TURNED - 2)
         for a in range(4):
             for q in range(4):
-                nc.sync.dma_start(out=landed[32 * q : 32 * q + 32, :, a, :], in_=staged[32 * a : 32 * a + 32, q])
-        store_y(TURNED - 2)
+                if a != q:
+                    nc.sync.dma_start(out=landed[32 * q : 32 * q + 32, :, a, :], in_=staged[32 * a : 32 * a + 32, q])
         store_y(TURNED - 1)
 
         last = TILES - 1
         for n in range(TURNED, TILES):
             if n > TURNED:
                 sig = logits(n)
-            if n >= FRONT:
+            if FRONT <= n < last:
                 for g in range(FULL, GROUPS):
                     t_pass(est[n], n, g)
                     a_pass(est[n], n, g)
@@ -324,25 +351,40 @@ def tile_amortised_ivector_shrinkage_k3_kernel(
                 product(n, sig)
                 store_y(n)
                 round_to_pairs(n)
+            if n == FRONT - 1:
+                for q in range(4):
+                    nc.scalar.copy(out=landed[32 * q : 32 * q + 32, :, q, :], in_=staged[32 * q : 32 * q + 32, q])
+        halves.append(bank(6, [P, HALF]))
+        for k in range(2):
+            for g in range(FULL if k == 0 else 0, GROUPS):
+                half_passes(halves[k], k, g)
+
+        def half_products(k):
+            cols = slice(HALF * k, HALF * (k + 1))
+            dst = pairs[:, last, :, P // 2 * k : P // 2 * (k + 1), :]
+            nc.vector.tensor_tensor(out=dst, in0=by_pairs(halves[k][:]), in1=by_pairs(sig[:, cols]), op=MULT)
+            nc.vector.tensor_tensor(out=y[:, last, cols], in0=halves[k][:], in1=sig[:, cols], op=MULT)
+
+        half_products(0)
         quantize_y(0, TURNED, landed[:].rearrange("p n a w -> p (n a w)"))
         store_words(0, TURNED, nc.sync)
 
-        joined = [keep.tile([P, 2, P, 2], F32, align_bytes=256, name="joined%d" % i) for i in range(2)]
-        turned = [bank(b, [P, 2, 2, P]) for b in (2, 3, 4)]
-        for n in (6, 4, 5):
-            for h in range(2):
-                turn(turned[(n - TURNED) // 2][:, n % 2], n, h)
-        gather(turned[1][:, 0:1], joined[1][:, 0:1])
-        gather(turned[0][:], joined[0][:])
-        for h in range(2):
-            nc.vector.tensor_tensor(
-                out=pairs[:, last, h], in0=by_pairs(est[last][:])[:, h], in1=by_pairs(sig[:])[:, h], op=MULT
-            )
-            turn(turned[2][:, 0], last, h)
-        product(last, sig)
+        joined45 = keep.tile([P, 2, P, 2], F32, align_bytes=256)
+        joined6 = keep.tile([P, P, 2], F32, align_bytes=256)
+        joined7 = keep.tile([P, P, 2], F32, align_bytes=256)
+        turned = {n: bank(n - 2, [P, 2, P]) for n in range(TURNED, TILES)}
+        half_products(1)
         store_y(last)
-        gather(turned[2][:, 0:1], joined[1][:, 1:2])
-        for i in range(2):
-            quantize_y(TURNED + 2 * i, TURNED + 2 * i + 2, joined[i][:].rearrange("p n u h -> p (n u h)"))
-            store_words(TURNED + 2 * i, TURNED + 2 * i + 2, (nc.sync, nc.scalar)[i])
+        for n in range(TURNED, TILES):
+            for h in range(2):
+                turn(turned[n], n, h)
+        gather(turned[4][:], joined45[:, 0], nc.scalar.copy)
+        gather(turned[5][:], joined45[:, 1], nc.vector.tensor_copy)
+        gather(turned[6][:], joined6[:], nc.scalar.copy)
+        gather(turned[last][:], joined7[:], nc.scalar.copy)
+        quantize_y(4, 6, joined45[:].rearrange("p n u h -> p (n u h)"))
+        store_words(4, 6, nc.sync)
+        quantize_y(6, 7, joined6[:].rearrange("p u h -> p (u h)"))
+        quantize_y(last, TILES, joined7[:].rearrange("p u h -> p (u h)"))
+        store_words(6, TILES, nc.scalar)
         store_scales([nc.sync, nc.sync, nc.scalar, nc.sync])

@@ -262,18 +262,18 @@ def tile_amortised_ivector_shrinkage_k3_kernel(
         load_f(2, 0, FRONT)
         load_scales(t_late, t_scales, EARLY_GROUPS, GROUPS, nc.sync)
         load_a(2)
-        load_v(0)
         load_f(3, 0, FRONT)
         load_t(3, 5)
+        load_v(0)
         load_a(3)
         load_v(1)
-        load_scales(a_last, a_scales, PACKED, GROUPS, nc.sync, first=4)
-        nc.sync.dma_start(out=frames_rows[0:P:4, :], in_=log_frames.rearrange("(n q j) -> q n j", q=4, j=32))
         load_v(2)
         load_f(4, 0, FRONT)
+        load_scales(a_last, a_scales, PACKED, GROUPS, nc.sync, first=4)
         load_a(4)
         load_v(3)
         load_v(4)
+        nc.sync.dma_start(out=frames_rows[0:P:4, :], in_=log_frames.rearrange("(n q j) -> q n j", q=4, j=32))
         back = f_words[FULL:GROUPS].rearrange("g p n t -> p g (n t)")[:, :, 4 * P * FRONT :]
         nc.sync.dma_start(out=f_back[:].bitcast(I32), in_=back.bitcast(I32))
         load_scales(f_late_back, f_scales[:, :, P * FRONT :], EARLY_GROUPS, GROUPS, nc.sync)
@@ -302,11 +302,10 @@ def tile_amortised_ivector_shrinkage_k3_kernel(
                 for n in range(COPIED):
                     nc.scalar.copy(out=est_sb[:, n, :], in_=est[n][:])
             quantize_v(g, interleave_v(g, R if g == GROUPS - 2 else VECTOR_COLS))
-            if g == 2:
-                nc.vector.transpose(frames_cols[:], frames_rows[:])
+        nc.vector.transpose(frames_cols[:], frames_rows[:])
 
         woven = [bank(n, [P, R]) for n in range(COPIED)]
-        for groups in (range(GROUPS - 1), range(GROUPS - 1, GROUPS)):
+        for groups in (range(GROUPS - 2), (GROUPS - 2,), (GROUPS - 1,)):
             for n in range(COPIED):
                 for g in groups:
                     z_pass(woven[n], n, g)

@@ -19,15 +19,15 @@ MULT = mybir.AluOpType.mult
 P = 128
 GROUPS = K // 512
 TILES = U // P
-EARLY_GROUPS = 2
-PACKED = 4
+LAST = TILES - 1
+HALF = R // 2
+EARLY = 2
 FRONT = 6
-TURNED = 4
 COPIED = 2
-FULL = 2
+TURNED = 4
+PACKED = 4
 FIRST_TILES = 4
 VECTOR_COLS = 320
-HALF = R // 2
 WARM_N = 256
 WARM_FREE = 7
 WARM_TIED = 5
@@ -43,20 +43,20 @@ def tile_amortised_ivector_shrinkage_k3_kernel(
         psum = ctx.enter_context(tc.psum_pool(name="psum", bufs=1))
         ctx.enter_context(tc.manual_schedule())
 
-        f_first = keep.tile([P, FULL, U], U32, align_bytes=256)
-        f_front = keep.tile([P, GROUPS - FULL, P * FRONT], U32, align_bytes=256)
-        f_back = keep.tile([P, GROUPS - FULL, U - P * FRONT], U32, align_bytes=256)
+        f_first = keep.tile([P, EARLY, U], U32, align_bytes=256)
+        f_front = keep.tile([P, GROUPS - EARLY, P * FRONT], U32, align_bytes=256)
+        f_back = keep.tile([P, GROUPS - EARLY, U - P * FRONT], U32, align_bytes=256)
         t_codes = keep.tile([P, GROUPS, 2 * R], U8, align_bytes=256)
         a_codes = keep.tile([P, GROUPS, R], U32, align_bytes=256)
         v_codes = keep.tile([P, GROUPS, R], U32, align_bytes=256)
-        f_early = keep.tile([P, EARLY_GROUPS, U], U8, align_bytes=256)
-        t_early = keep.tile([P, EARLY_GROUPS, R], U8, align_bytes=256)
-        f_late = keep.tile([P, GROUPS - EARLY_GROUPS, P * FRONT], U8, align_bytes=256)
-        f_late_back = keep.tile([P, GROUPS - EARLY_GROUPS, U - P * FRONT], U8, align_bytes=256)
-        t_late = keep.tile([P, GROUPS - EARLY_GROUPS, R], U8, align_bytes=256)
-        a_packed = keep.tile([P, 1, R], U8, align_bytes=256)
-        a_last = keep.tile([P, 1, R], U8, align_bytes=256)
-        v_plane = keep.tile([P, GROUPS, R], U8, align_bytes=256)
+        f_first_planes = keep.tile([P, EARLY, U], U8, align_bytes=256)
+        t_early_planes = keep.tile([P, EARLY, R], U8, align_bytes=256)
+        f_front_planes = keep.tile([P, GROUPS - EARLY, P * FRONT], U8, align_bytes=256)
+        f_back_planes = keep.tile([P, GROUPS - EARLY, U - P * FRONT], U8, align_bytes=256)
+        t_late_planes = keep.tile([P, GROUPS - EARLY, R], U8, align_bytes=256)
+        a_packed_planes = keep.tile([P, 1, R], U8, align_bytes=256)
+        a_last_plane = keep.tile([P, 1, R], U8, align_bytes=256)
+        v_planes = keep.tile([P, GROUPS, R], U8, align_bytes=256)
         v_rows = [keep.tile([P, 4, R], BF16, align_bytes=256, name="v_rows%d" % g) for g in range(GROUPS)]
         frames_rows = keep.tile([P, 32], BF16, align_bytes=64)
         frames_cols = keep.tile([P, 32], BF16, align_bytes=64)
@@ -76,20 +76,18 @@ def tile_amortised_ivector_shrinkage_k3_kernel(
         def bank(b, shape):
             return psum.tile(shape, F32, name="bank%d" % b, tag="bank%d" % b)
 
-        def plane_of(early, late, g):
-            return early[:, g, :] if g < EARLY_GROUPS else late[:, g - EARLY_GROUPS, :]
+        def clear(planes):
+            nc.vector.memset(planes[:].rearrange("p g n -> p (g n)").bitcast(I32), 0)
 
-        def clear(plane):
-            nc.vector.memset(plane[:].rearrange("p g n -> p (g n)").bitcast(I32), 0)
-
-        def load_scales(plane, scales, g0, g1, queue, which=range(4), first=0):
+        def load_scales(planes, scales, g0, g1, which=range(4), first=0):
             rows = scales.rearrange("g (q r) n -> r q g n", r=4)
             for r in which:
-                queue.dma_start(out=plane[first + r : P : 32, :, :].bitcast(I32), in_=rows[r][:, g0:g1, :].bitcast(I32))
+                dst = planes[first + r : P : 32, :, :]
+                nc.sync.dma_start(out=dst.bitcast(I32), in_=rows[r][:, g0:g1, :].bitcast(I32))
 
         def load_f(g, n0, n1):
             src = f_words[g].rearrange("p n t -> p (n t)")[:, 4 * P * n0 : 4 * P * n1]
-            dst = f_first[:, g, P * n0 : P * n1] if g < FULL else f_front[:, g - FULL, P * n0 : P * n1]
+            dst = f_first[:, g, P * n0 : P * n1] if g < EARLY else f_front[:, g - EARLY, P * n0 : P * n1]
             nc.sync.dma_start(out=dst.bitcast(I32), in_=src.bitcast(I32))
 
         def load_t(g0, g1):
@@ -105,19 +103,16 @@ def tile_amortised_ivector_shrinkage_k3_kernel(
             nc.sync.dma_start(out=v_rows[g][:], in_=src)
 
         def mx_pass(acc, n, g, codes, plane, start, stop):
-            if g < FULL:
-                held = f_first[:, g, P * n : P * (n + 1)]
-                held_plane = f_early[:, g, P * n : P * (n + 1)]
+            if g < EARLY:
+                held, held_plane, col = f_first[:, g, :], f_first_planes[:, g, :], P * n
             elif n < FRONT:
-                held = f_front[:, g - FULL, P * n : P * (n + 1)]
-                held_plane = f_late[:, g - FULL, P * n : P * (n + 1)]
+                held, held_plane, col = f_front[:, g - EARLY, :], f_front_planes[:, g - EARLY, :], P * n
             else:
-                held = f_back[:, g - FULL, P * (n - FRONT) : P * (n - FRONT + 1)]
-                held_plane = f_late_back[:, g - FULL, P * (n - FRONT) : P * (n - FRONT + 1)]
+                held, held_plane, col = f_back[:, g - EARLY, :], f_back_planes[:, g - EARLY, :], P * (n - FRONT)
             nc.tensor.matmul_mx(
                 out=acc,
-                lhsT=held.bitcast(FP8X4),
-                lhsT_scale=held_plane,
+                lhsT=held[:, col : col + P].bitcast(FP8X4),
+                lhsT_scale=held_plane[:, col : col + P],
                 rhs=codes,
                 rhs_scale=plane,
                 start=start,
@@ -125,27 +120,25 @@ def tile_amortised_ivector_shrinkage_k3_kernel(
             )
 
         def t_part(acc, n, g, start, c0, c1):
-            codes = t_codes[:, g, 2 * c0 : 2 * c1].bitcast(FP4X4)
-            mx_pass(acc, n, g, codes, plane_of(t_early, t_late, g)[:, c0:c1], start, False)
+            plane = t_early_planes[:, g, c0:c1] if g < EARLY else t_late_planes[:, g - EARLY, c0:c1]
+            mx_pass(acc, n, g, t_codes[:, g, 2 * c0 : 2 * c1].bitcast(FP4X4), plane, start, False)
 
-        def a_part(acc, n, g, start, c0, c1):
-            plane = a_packed[4 * g : P, 0, c0:c1] if g < PACKED else a_last[4:P, 0, c0:c1]
-            mx_pass(acc, n, g, a_codes[:, g, c0:c1].bitcast(FP8X4), plane, start, g == GROUPS - 1)
+        def a_part(acc, n, g, c0, c1):
+            plane = a_packed_planes[4 * g : P, 0, c0:c1] if g < PACKED else a_last_plane[4:P, 0, c0:c1]
+            mx_pass(acc, n, g, a_codes[:, g, c0:c1].bitcast(FP8X4), plane, False, g == GROUPS - 1)
 
-        def t_pass(est, n, g):
-            t_part(est[:], n, g, g == 0, 0, R)
+        def t_pass(n, g):
+            t_part(est[n][:], n, g, g == 0, 0, R)
 
-        def a_pass(est, n, g):
-            a_part(est[:], n, g, False, 0, R)
+        def a_pass(n, g):
+            a_part(est[n][:], n, g, 0, R)
 
-        def half_passes(acc, k, g):
-            c0 = HALF * k
-            if g == 0:
-                a_part(acc[:], TILES - 1, g, True, c0, c0 + HALF)
+        def t_half(k, g):
             for c in range(0, HALF, P):
-                t_part(acc[:, c : c + P], TILES - 1, g, False, c0 + c, c0 + c + P)
-            if g > 0:
-                a_part(acc[:], TILES - 1, g, False, c0, c0 + HALF)
+                t_part(halves[k][:, c : c + P], LAST, g, g == 0 and c == 0, HALF * k + c, HALF * k + c + P)
+
+        def a_half(k, g):
+            a_part(halves[k][:], LAST, g, HALF * k, HALF * (k + 1))
 
         def interleave_v(g, vector_cols):
             grouped = ring.tile([P, R, 4], BF16, align_bytes=256, name="v_grouped")
@@ -160,30 +153,31 @@ def tile_amortised_ivector_shrinkage_k3_kernel(
         def quantize_v(g, grouped):
             nc.vector.quantize_mx(
                 out=v_codes[:, g, :].bitcast(FP8X4),
-                scales=v_plane[:, g, :],
+                scales=v_planes[:, g, :],
                 in_=grouped[:].rearrange("p n t -> p (n t)"),
             )
 
         def z_pass(z, n, g):
-            mx_pass(z[:], n, g, v_codes[:, g, :].bitcast(FP8X4), v_plane[:, g, :], g == 0, g == GROUPS - 1)
-
-        def logits(n):
-            z = bank(n % COPIED, [P, R])
-            for g in range(GROUPS):
-                z_pass(z, n, g)
-            return gate(z, n)
+            mx_pass(z[:], n, g, v_codes[:, g, :].bitcast(FP8X4), v_planes[:, g, :], g == 0, g == GROUPS - 1)
 
         def gate(z, n):
             sig = ring.tile([P, R], F32, align_bytes=256, name="sig")
             nc.scalar.activation(out=sig[:], in_=z[:], func=SIGMOID, bias=frames_cols[:, 4 * n : 4 * n + 1])
             return sig
 
+        def logits_and_gate(n):
+            z = bank(n % COPIED, [P, R])
+            for g in range(GROUPS):
+                z_pass(z, n, g)
+            return gate(z, n)
+
         def product(n, sig):
             src = est_sb[:, n, :] if n < COPIED else est[n][:]
             nc.vector.tensor_tensor(out=y[:, n, :], in0=src, in1=sig[:], op=MULT)
 
-        def store_y(n):
-            nc.sync.dma_start(out=out_0[P * n : P * (n + 1), :], in_=y[:, n, :])
+        def store_y(n0, n1):
+            rows = out_0[P * n0 : P * n1, :].rearrange("(n p) r -> p n r", p=P)
+            nc.sync.dma_start(out=rows, in_=y[:, n0:n1, :])
 
         def by_pairs(ap):
             return ap.rearrange("u (p h e) -> u h p e", h=2, e=2)
@@ -198,14 +192,11 @@ def tile_amortised_ivector_shrinkage_k3_kernel(
 
         def stage(n, blocks):
             nc.scalar.copy(
-                out=staged[:, :, n, :].rearrange("p q (i h) -> p q i h", h=2),
-                in_=blocks[:].rearrange("p (h q i) -> p q i h", h=2, q=4),
+                out=staged[:, :, n, :].rearrange("p q (j h) -> p q j h", h=2),
+                in_=blocks[:].rearrange("p (h q j) -> p q j h", h=2, q=4),
             )
 
-        def turn(dst, n, h):
-            nc.tensor.transpose(dst[:, h, :], pairs[:, n, h].rearrange("u p e -> u (p e)").bitcast(F32), identity[:])
-
-        def gather(turned, dst, copy):
+        def join(turned, dst, copy):
             copy(out=dst, in_=turned.rearrange("p h u -> p u h"))
 
         def quantize_y(n0, n1, words):
@@ -216,11 +207,6 @@ def tile_amortised_ivector_shrinkage_k3_kernel(
             dst = out_1[0].rearrange("p u t -> p (u t)")[:, 4 * P * n0 : 4 * P * n1]
             queue.dma_start(out=dst.bitcast(I32), in_=y_codes[:, P * n0 : P * n1].bitcast(I32))
 
-        def store_scales(queues):
-            rows = out_2[0].rearrange("(q r) u -> r q u", r=4)
-            for r in range(4):
-                queues[r].dma_start(out=rows[r].bitcast(I32), in_=y_plane[r:P:32, :].bitcast(I32))
-
         def warm_passes(count, moving):
             for i in range(count):
                 nc.tensor.matmul_mx(
@@ -228,74 +214,75 @@ def tile_amortised_ivector_shrinkage_k3_kernel(
                     rhs=moving.bitcast(FP8X4), rhs_scale=warm_plane[:], start=True, stop=True,
                 )
 
-        clear(t_early)
+        clear(t_early_planes)
         nc.vector.memset(warm_in[:].bitcast(I32), 0x3F803F80)
-        clear(f_early)
+        clear(f_first_planes)
         nc.vector.quantize_mx(out=warm_codes[:].bitcast(FP8X4), scales=warm_plane[:], in_=warm_in[:])
-        clear(a_packed)
-        clear(f_late)
-        clear(t_late)
-        clear(a_last)
-        clear(f_late_back)
+        clear(a_packed_planes)
+        clear(f_front_planes)
+        clear(t_late_planes)
+        clear(a_last_plane)
+        clear(f_back_planes)
         nc.vector.memset(frames_rows[:], 0.0)
         nc.vector.memset(identity[:], 0.0)
         nc.scalar.activation(out=warm_act[:], in_=warm_in[:, 0:1], func=SIGMOID)
-
         make_identity(nc, identity[:], nomemset=True)
 
         load_t(0, 1)
-        load_scales(t_early, t_scales, 0, EARLY_GROUPS, nc.sync, range(1))
+        load_scales(t_early_planes, t_scales, 0, EARLY, range(1))
         load_f(0, 0, FIRST_TILES)
-        load_scales(t_early, t_scales, 0, EARLY_GROUPS, nc.sync, range(1, 4))
-        load_scales(f_early, f_scales, 0, EARLY_GROUPS, nc.sync)
+        load_scales(t_early_planes, t_scales, 0, EARLY, range(1, 4))
+        load_scales(f_first_planes, f_scales, 0, EARLY)
         load_f(0, FIRST_TILES, TILES)
         load_a(0)
         for q in range(4):
             nc.sync.dma_start(
-                out=a_packed[32 * q : 32 * q + 4 * PACKED, 0, :].bitcast(I32),
+                out=a_packed_planes[32 * q : 32 * q + 4 * PACKED, 0, :].bitcast(I32),
                 in_=a_scales[0:PACKED, 4 * q : 4 * q + 4, :].bitcast(I32),
             )
+        load_t(1, 2)
         load_f(1, 0, TILES)
-        load_t(1, 3)
         load_a(1)
-        load_scales(f_late, f_scales[:, :, 0 : P * FRONT], EARLY_GROUPS, GROUPS, nc.sync)
+        load_scales(f_front_planes, f_scales[:, :, 0 : P * FRONT], EARLY, GROUPS)
         load_f(2, 0, FRONT)
-        load_scales(t_late, t_scales, EARLY_GROUPS, GROUPS, nc.sync)
         load_a(2)
+        load_scales(t_late_planes, t_scales, EARLY, GROUPS)
+        load_t(2, GROUPS)
         load_f(3, 0, FRONT)
-        load_t(3, 5)
         load_v(0)
         load_a(3)
         load_v(1)
         load_v(2)
         load_f(4, 0, FRONT)
-        load_scales(a_last, a_scales, PACKED, GROUPS, nc.sync, first=4)
+        load_scales(a_last_plane, a_scales, PACKED, GROUPS, first=4)
         load_a(4)
         load_v(3)
         load_v(4)
         nc.sync.dma_start(out=frames_rows[0:P:4, :], in_=log_frames.rearrange("(n q j) -> q n j", q=4, j=32))
-        back = f_words[FULL:GROUPS].rearrange("g p n t -> p g (n t)")[:, :, 4 * P * FRONT :]
+        back = f_words[EARLY:GROUPS].rearrange("g p n t -> p g (n t)")[:, :, 4 * P * FRONT :]
         nc.sync.dma_start(out=f_back[:].bitcast(I32), in_=back.bitcast(I32))
-        load_scales(f_late_back, f_scales[:, :, P * FRONT :], EARLY_GROUPS, GROUPS, nc.sync)
+        load_scales(f_back_planes, f_scales[:, :, P * FRONT :], EARLY, GROUPS)
 
-        warm = bank(TILES - 1, [P, WARM_N])
+        warm = bank(LAST, [P, WARM_N])
         warm_passes(WARM_FREE, warm_codes[:])
         warm_passes(WARM_TIED, f_first[:, 0, 0:WARM_N])
 
-        est = [bank(n, [P, R]) for n in range(TILES - 1)]
-        halves = [bank(TILES - 1, [P, HALF])]
-        for g in range(GROUPS - 1):
-            tiles = range(TILES - 1 if g < FULL else FRONT)
-            for n in tiles:
-                t_pass(est[n], n, g)
-            for n in tiles:
-                a_pass(est[n], n, g)
-            if g < FULL:
-                half_passes(halves[0], 0, g)
-        for n in range(FRONT - 2):
-            t_pass(est[n], n, GROUPS - 1)
-            a_pass(est[n], n, GROUPS - 1)
-        t_pass(est[FRONT - 2], FRONT - 2, GROUPS - 1)
+        est = [bank(n, [P, R]) for n in range(LAST)]
+        halves = [bank(LAST, [P, HALF])]
+        for g in range(EARLY):
+            for n in range(LAST):
+                t_pass(n, g)
+            t_half(0, g)
+            for n in range(LAST):
+                a_pass(n, g)
+            a_half(0, g)
+        for g in range(EARLY, GROUPS - 1):
+            for weight_pass in (a_pass, t_pass) if g == EARLY else (t_pass, a_pass):
+                for n in range(FRONT):
+                    weight_pass(n, g)
+        last_group = [(weight_pass, n) for n in range(FRONT) for weight_pass in (t_pass, a_pass)]
+        for weight_pass, n in last_group[:-3]:
+            weight_pass(n, GROUPS - 1)
 
         for g in range(GROUPS):
             if g == GROUPS - 2:
@@ -309,81 +296,88 @@ def tile_amortised_ivector_shrinkage_k3_kernel(
             for n in range(COPIED):
                 for g in groups:
                     z_pass(woven[n], n, g)
-        a_pass(est[FRONT - 2], FRONT - 2, GROUPS - 1)
-        t_pass(est[FRONT - 1], FRONT - 1, GROUPS - 1)
-        a_pass(est[FRONT - 1], FRONT - 1, GROUPS - 1)
-        blocks = {}
-        for n in range(TURNED - 1):
-            product(n, gate(woven[n], n) if n < COPIED else logits(n))
-            if n > 1:
-                stage(n - 2, blocks[n - 2])
+        for weight_pass, n in last_group[-3:]:
+            weight_pass(n, GROUPS - 1)
+
+        blocks, gates = {}, {}
+        for n in range(COPIED):
+            product(n, gate(woven[n], n))
             if n > 0:
                 blocks[n - 1] = turn_blocks(n - 1)
-                store_y(n - 1)
             round_to_pairs(n)
-        n = TURNED - 1
-        sig = logits(n)
-        blocks[n - 1] = turn_blocks(n - 1)
-        nc.vector.tensor_tensor(out=pairs[:, n], in0=by_pairs(est[n][:]), in1=by_pairs(sig[:]), op=MULT)
-        blocks[n] = turn_blocks(n)
-        product(n, sig)
-        stage(n - 2, blocks[n - 2])
-        stage(n - 1, blocks[n - 1])
-        sig = logits(TURNED)
-        stage(n, blocks[n])
-        store_y(TURNED - 2)
+            store_y(n, n + 1)
+        for n in range(COPIED, TURNED):
+            gates[n] = logits_and_gate(n)
+            stage(n - 2, blocks[n - 2])
+            if n == COPIED:
+                blocks[n - 1] = turn_blocks(n - 1)
+            nc.vector.tensor_tensor(out=pairs[:, n], in0=by_pairs(est[n][:]), in1=by_pairs(gates[n][:]), op=MULT)
+            blocks[n] = turn_blocks(n)
+        stage(TURNED - 2, blocks[TURNED - 2])
+        gates[TURNED] = logits_and_gate(TURNED)
+        stage(TURNED - 1, blocks[TURNED - 1])
         for a in range(4):
             for q in range(4):
                 if a != q:
                     nc.sync.dma_start(out=landed[32 * q : 32 * q + 32, :, a, :], in_=staged[32 * a : 32 * a + 32, q])
-        store_y(TURNED - 1)
+        for n in range(COPIED, TURNED):
+            product(n, gates[n])
+        store_y(COPIED, TURNED)
 
-        last = TILES - 1
-        for n in range(TURNED, TILES):
-            if n > TURNED:
-                sig = logits(n)
-            if FRONT <= n < last:
-                for g in range(FULL, GROUPS):
-                    t_pass(est[n], n, g)
-                    a_pass(est[n], n, g)
-            if n < last:
-                product(n, sig)
-                store_y(n)
-                round_to_pairs(n)
-            if n == FRONT - 1:
-                for q in range(4):
-                    nc.scalar.copy(out=landed[32 * q : 32 * q + 32, :, q, :], in_=staged[32 * q : 32 * q + 32, q])
-        halves.append(bank(6, [P, HALF]))
+        product(TURNED, gates[TURNED])
+        round_to_pairs(TURNED)
+        gates[FRONT - 1] = logits_and_gate(FRONT - 1)
+        product(FRONT - 1, gates[FRONT - 1])
+        store_y(TURNED, FRONT)
+        round_to_pairs(FRONT - 1)
+        for q in range(4):
+            nc.scalar.copy(out=landed[32 * q : 32 * q + 32, :, q, :], in_=staged[32 * q : 32 * q + 32, q])
+        gates[FRONT] = logits_and_gate(FRONT)
+        for g in range(EARLY, GROUPS):
+            t_pass(FRONT, g)
+            a_pass(FRONT, g)
+        product(FRONT, gates[FRONT])
+        store_y(FRONT, LAST)
+        round_to_pairs(FRONT)
+
+        gates[LAST] = logits_and_gate(LAST)
+        halves.append(bank(FRONT, [P, HALF]))
         for k in range(2):
-            for g in range(FULL if k == 0 else 0, GROUPS):
-                half_passes(halves[k], k, g)
+            for g in range(EARLY if k == 0 else 0, GROUPS):
+                t_half(k, g)
+                a_half(k, g)
 
-        def half_products(k):
+        def half_products(k, parts):
             cols = slice(HALF * k, HALF * (k + 1))
-            dst = pairs[:, last, :, P // 2 * k : P // 2 * (k + 1), :]
-            nc.vector.tensor_tensor(out=dst, in0=by_pairs(halves[k][:]), in1=by_pairs(sig[:, cols]), op=MULT)
-            nc.vector.tensor_tensor(out=y[:, last, cols], in0=halves[k][:], in1=sig[:, cols], op=MULT)
+            dst = pairs[:, LAST, :, P // 2 * k : P // 2 * (k + 1), :]
+            for h in parts:
+                nc.vector.tensor_tensor(
+                    out=dst[:, h], in0=by_pairs(halves[k][:])[:, h], in1=by_pairs(gates[LAST][:, cols])[:, h], op=MULT
+                )
+            nc.vector.tensor_tensor(out=y[:, LAST, cols], in0=halves[k][:], in1=gates[LAST][:, cols], op=MULT)
 
-        half_products(0)
+        half_products(0, [slice(0, 2)])
         quantize_y(0, TURNED, landed[:].rearrange("p n a w -> p (n a w)"))
         store_words(0, TURNED, nc.sync)
 
-        joined45 = keep.tile([P, 2, P, 2], F32, align_bytes=256)
-        joined6 = keep.tile([P, P, 2], F32, align_bytes=256)
-        joined7 = keep.tile([P, P, 2], F32, align_bytes=256)
+        joined_pair = keep.tile([P, 2, P, 2], F32, align_bytes=256)
+        joined = {n: keep.tile([P, P, 2], F32, align_bytes=256, name="joined%d" % n) for n in (FRONT, LAST)}
         turned = {n: bank(n - 2, [P, 2, P]) for n in range(TURNED, TILES)}
-        half_products(1)
-        store_y(last)
+        half_products(1, [slice(0, 1), slice(1, 2)])
+        store_y(LAST, TILES)
         for n in range(TURNED, TILES):
             for h in range(2):
-                turn(turned[n], n, h)
-        gather(turned[4][:], joined45[:, 0], nc.scalar.copy)
-        gather(turned[5][:], joined45[:, 1], nc.vector.tensor_copy)
-        gather(turned[6][:], joined6[:], nc.scalar.copy)
-        gather(turned[last][:], joined7[:], nc.scalar.copy)
-        quantize_y(4, 6, joined45[:].rearrange("p n u h -> p (n u h)"))
-        store_words(4, 6, nc.sync)
-        quantize_y(6, 7, joined6[:].rearrange("p u h -> p (u h)"))
-        quantize_y(last, TILES, joined7[:].rearrange("p u h -> p (u h)"))
-        store_words(6, TILES, nc.scalar)
-        store_scales([nc.sync, nc.sync, nc.scalar, nc.sync])
+                words = pairs[:, n, h].rearrange("u p e -> u (p e)").bitcast(F32)
+                nc.tensor.transpose(turned[n][:, h, :], words, identity[:])
+        join(turned[TURNED][:], joined_pair[:, 0], nc.scalar.copy)
+        join(turned[TURNED + 1][:], joined_pair[:, 1], nc.vector.tensor_copy)
+        for n in (FRONT, LAST):
+            join(turned[n][:], joined[n][:], nc.scalar.copy)
+        quantize_y(TURNED, FRONT, joined_pair[:].rearrange("p n u h -> p (n u h)"))
+        store_words(TURNED, FRONT, nc.sync)
+        for n in (FRONT, LAST):
+            quantize_y(n, n + 1, joined[n][:].rearrange("p u h -> p (u h)"))
+        store_words(FRONT, TILES, nc.scalar)
+        scale_rows = out_2[0].rearrange("(q r) u -> r q u", r=4)
+        for r, queue in enumerate((nc.sync, nc.sync, nc.scalar, nc.sync)):
+            queue.dma_start(out=scale_rows[r].bitcast(I32), in_=y_plane[r:P:32, :].bitcast(I32))

@@ -22,15 +22,15 @@ TILES = U // P
 LAST = TILES - 1
 HALF = R // 2
 EARLY = 2
+FULL = 3
 FRONT = 6
 COPIED = 2
-TURNED = 4
+TURNED = 6
 PACKED = 4
 FIRST_TILES = 4
 VECTOR_COLS = 320
 WARM_N = 256
-WARM_FREE = 7
-WARM_TIED = 5
+WARM_PASSES = 10
 
 
 def tile_amortised_ivector_shrinkage_k3_kernel(
@@ -43,16 +43,15 @@ def tile_amortised_ivector_shrinkage_k3_kernel(
         psum = ctx.enter_context(tc.psum_pool(name="psum", bufs=1))
         ctx.enter_context(tc.manual_schedule())
 
-        f_first = keep.tile([P, EARLY, U], U32, align_bytes=256)
-        f_front = keep.tile([P, GROUPS - EARLY, P * FRONT], U32, align_bytes=256)
-        f_back = keep.tile([P, GROUPS - EARLY, U - P * FRONT], U32, align_bytes=256)
+        f_full = [keep.tile([P, U], U32, align_bytes=256, name="f_full%d" % g) for g in range(FULL)]
+        f_front = keep.tile([P, GROUPS - FULL, P * FRONT], U32, align_bytes=256)
+        f_back = keep.tile([P, GROUPS - FULL, U - P * FRONT], U32, align_bytes=256)
         t_codes = keep.tile([P, GROUPS, 2 * R], U8, align_bytes=256)
         a_codes = keep.tile([P, GROUPS, R], U32, align_bytes=256)
         v_codes = keep.tile([P, GROUPS, R], U32, align_bytes=256)
         f_first_planes = keep.tile([P, EARLY, U], U8, align_bytes=256)
         t_early_planes = keep.tile([P, EARLY, R], U8, align_bytes=256)
-        f_front_planes = keep.tile([P, GROUPS - EARLY, P * FRONT], U8, align_bytes=256)
-        f_back_planes = keep.tile([P, GROUPS - EARLY, U - P * FRONT], U8, align_bytes=256)
+        f_late_planes = keep.tile([P, GROUPS - EARLY, U], U8, align_bytes=256)
         t_late_planes = keep.tile([P, GROUPS - EARLY, R], U8, align_bytes=256)
         a_packed_planes = keep.tile([P, 1, R], U8, align_bytes=256)
         a_last_plane = keep.tile([P, 1, R], U8, align_bytes=256)
@@ -68,7 +67,7 @@ def tile_amortised_ivector_shrinkage_k3_kernel(
         est_sb = keep.tile([P, COPIED, R], F32, align_bytes=256)
         pairs = keep.tile([P, TILES, 2, P, 2], BF16, align_bytes=256)
         y = keep.tile([P, TILES, R], F32, align_bytes=256)
-        staged = keep.tile([P, 4, TURNED, 64], F32, align_bytes=256)
+        staged = keep.tile([P, TURNED // 2, 4, 2, 64], F32, align_bytes=256)
         landed = keep.tile([P, TURNED, 4, 64], F32, align_bytes=256)
         y_codes = keep.tile([P, U], U32, align_bytes=256)
         y_plane = keep.tile([P, U], U8, align_bytes=256)
@@ -79,15 +78,15 @@ def tile_amortised_ivector_shrinkage_k3_kernel(
         def clear(planes):
             nc.vector.memset(planes[:].rearrange("p g n -> p (g n)").bitcast(I32), 0)
 
-        def load_scales(planes, scales, g0, g1, which=range(4), first=0):
+        def load_scales(planes, scales, g0, g1, first=0):
             rows = scales.rearrange("g (q r) n -> r q g n", r=4)
-            for r in which:
+            for r in range(4):
                 dst = planes[first + r : P : 32, :, :]
                 nc.sync.dma_start(out=dst.bitcast(I32), in_=rows[r][:, g0:g1, :].bitcast(I32))
 
         def load_f(g, n0, n1):
             src = f_words[g].rearrange("p n t -> p (n t)")[:, 4 * P * n0 : 4 * P * n1]
-            dst = f_first[:, g, P * n0 : P * n1] if g < EARLY else f_front[:, g - EARLY, P * n0 : P * n1]
+            dst = f_full[g][:, P * n0 : P * n1] if g < FULL else f_front[:, g - FULL, P * n0 : P * n1]
             nc.sync.dma_start(out=dst.bitcast(I32), in_=src.bitcast(I32))
 
         def load_t(g0, g1):
@@ -103,16 +102,17 @@ def tile_amortised_ivector_shrinkage_k3_kernel(
             nc.sync.dma_start(out=v_rows[g][:], in_=src)
 
         def mx_pass(acc, n, g, codes, plane, start, stop):
-            if g < EARLY:
-                held, held_plane, col = f_first[:, g, :], f_first_planes[:, g, :], P * n
+            if g < FULL:
+                held = f_full[g][:, P * n : P * (n + 1)]
             elif n < FRONT:
-                held, held_plane, col = f_front[:, g - EARLY, :], f_front_planes[:, g - EARLY, :], P * n
+                held = f_front[:, g - FULL, P * n : P * (n + 1)]
             else:
-                held, held_plane, col = f_back[:, g - EARLY, :], f_back_planes[:, g - EARLY, :], P * (n - FRONT)
+                held = f_back[:, g - FULL, P * (n - FRONT) : P * (n - FRONT + 1)]
+            held_plane = f_first_planes[:, g, :] if g < EARLY else f_late_planes[:, g - EARLY, :]
             nc.tensor.matmul_mx(
                 out=acc,
-                lhsT=held[:, col : col + P].bitcast(FP8X4),
-                lhsT_scale=held_plane[:, col : col + P],
+                lhsT=held.bitcast(FP8X4),
+                lhsT_scale=held_plane[:, P * n : P * (n + 1)],
                 rhs=codes,
                 rhs_scale=plane,
                 start=start,
@@ -134,8 +134,7 @@ def tile_amortised_ivector_shrinkage_k3_kernel(
             a_part(est[n][:], n, g, 0, R)
 
         def t_half(k, g):
-            for c in range(0, HALF, P):
-                t_part(halves[k][:, c : c + P], LAST, g, g == 0 and c == 0, HALF * k + c, HALF * k + c + P)
+            t_part(halves[k][:], LAST, g, g == 0, HALF * k, HALF * (k + 1))
 
         def a_half(k, g):
             a_part(halves[k][:], LAST, g, HALF * k, HALF * (k + 1))
@@ -161,15 +160,15 @@ def tile_amortised_ivector_shrinkage_k3_kernel(
             mx_pass(z[:], n, g, v_codes[:, g, :].bitcast(FP8X4), v_planes[:, g, :], g == 0, g == GROUPS - 1)
 
         def gate(z, n):
-            sig = ring.tile([P, R], F32, align_bytes=256, name="sig")
-            nc.scalar.activation(out=sig[:], in_=z[:], func=SIGMOID, bias=frames_cols[:, 4 * n : 4 * n + 1])
+            sig = ring.tile(list(z.shape), F32, align_bytes=256, name="sig")
+            nc.scalar.activation(out=sig[:], in_=z, func=SIGMOID, bias=frames_cols[:, 4 * n : 4 * n + 1])
             return sig
 
-        def logits_and_gate(n):
+        def logits(n):
             z = bank(n % COPIED, [P, R])
             for g in range(GROUPS):
                 z_pass(z, n, g)
-            return gate(z, n)
+            return z
 
         def product(n, sig):
             src = est_sb[:, n, :] if n < COPIED else est[n][:]
@@ -183,7 +182,17 @@ def tile_amortised_ivector_shrinkage_k3_kernel(
             return ap.rearrange("u (p h e) -> u h p e", h=2, e=2)
 
         def round_to_pairs(n):
-            nc.vector.tensor_copy(out=pairs[:, n], in_=by_pairs(y[:, n, :]))
+            nc.scalar.copy(out=pairs[:, n], in_=by_pairs(y[:, n, :]))
+
+        def by_blocks(ap):
+            return ap.rearrange("u (i b e) -> u b i e", b=8, e=2)
+
+        def block_words(n):
+            return pairs[:, n].rearrange("u h p e -> u (h p e)").rearrange("u (b i e) -> u b i e", b=8, e=2)
+
+        def round_to_blocks(n):
+            copy = nc.scalar.copy if n < COPIED else nc.vector.tensor_copy
+            copy(out=block_words(n), in_=by_blocks(y[:, n, :]))
 
         def turn_blocks(n):
             blocks = ring.tile([P, 2 * P], F32, align_bytes=256, name="blocks")
@@ -192,9 +201,15 @@ def tile_amortised_ivector_shrinkage_k3_kernel(
 
         def stage(n, blocks):
             nc.scalar.copy(
-                out=staged[:, :, n, :].rearrange("p q (j h) -> p q j h", h=2),
-                in_=blocks[:].rearrange("p (h q j) -> p q j h", h=2, q=4),
+                out=staged[:, n // 2, :, n % 2, :].rearrange("p q (j h) -> p q j h", h=2),
+                in_=blocks[:].rearrange("p (q h j) -> p q j h", h=2, q=4),
             )
+            if n % 2 == 1:
+                for a in (0, 2, 1, 3):
+                    nc.sync.dma_start(out=landed[:, n - 1 : n + 1, a, :], in_=staged[32 * a : 32 * a + 32, n // 2])
+
+        def quantize_landed(n0, n1):
+            quantize_y(n0, n1, landed[:, n0:n1].rearrange("p n a w -> p (n a w)"))
 
         def join(turned, dst, copy):
             copy(out=dst, in_=turned.rearrange("p h u -> p u h"))
@@ -207,31 +222,22 @@ def tile_amortised_ivector_shrinkage_k3_kernel(
             dst = out_1[0].rearrange("p u t -> p (u t)")[:, 4 * P * n0 : 4 * P * n1]
             queue.dma_start(out=dst.bitcast(I32), in_=y_codes[:, P * n0 : P * n1].bitcast(I32))
 
-        def warm_passes(count, moving):
-            for i in range(count):
-                nc.tensor.matmul_mx(
-                    out=warm[:], lhsT=warm_codes[:, 0:P].bitcast(FP8X4), lhsT_scale=warm_plane[:, 0:P],
-                    rhs=moving.bitcast(FP8X4), rhs_scale=warm_plane[:], start=True, stop=True,
-                )
-
         clear(t_early_planes)
         nc.vector.memset(warm_in[:].bitcast(I32), 0x3F803F80)
         clear(f_first_planes)
         nc.vector.quantize_mx(out=warm_codes[:].bitcast(FP8X4), scales=warm_plane[:], in_=warm_in[:])
         clear(a_packed_planes)
-        clear(f_front_planes)
+        clear(f_late_planes)
         clear(t_late_planes)
         clear(a_last_plane)
-        clear(f_back_planes)
         nc.vector.memset(frames_rows[:], 0.0)
         nc.vector.memset(identity[:], 0.0)
         nc.scalar.activation(out=warm_act[:], in_=warm_in[:, 0:1], func=SIGMOID)
         make_identity(nc, identity[:], nomemset=True)
 
         load_t(0, 1)
-        load_scales(t_early_planes, t_scales, 0, EARLY, range(1))
+        load_scales(t_early_planes, t_scales, 0, EARLY)
         load_f(0, 0, FIRST_TILES)
-        load_scales(t_early_planes, t_scales, 0, EARLY, range(1, 4))
         load_scales(f_first_planes, f_scales, 0, EARLY)
         load_f(0, FIRST_TILES, TILES)
         load_a(0)
@@ -243,14 +249,15 @@ def tile_amortised_ivector_shrinkage_k3_kernel(
         load_t(1, 2)
         load_f(1, 0, TILES)
         load_a(1)
-        load_scales(f_front_planes, f_scales[:, :, 0 : P * FRONT], EARLY, GROUPS)
-        load_f(2, 0, FRONT)
+        load_scales(f_late_planes, f_scales, EARLY, GROUPS)
+        load_f(2, 0, TILES)
         load_a(2)
         load_scales(t_late_planes, t_scales, EARLY, GROUPS)
-        load_t(2, GROUPS)
+        load_t(2, 3)
         load_f(3, 0, FRONT)
-        load_v(0)
         load_a(3)
+        load_v(0)
+        load_t(3, GROUPS)
         load_v(1)
         load_v(2)
         load_f(4, 0, FRONT)
@@ -259,27 +266,27 @@ def tile_amortised_ivector_shrinkage_k3_kernel(
         load_v(3)
         load_v(4)
         nc.sync.dma_start(out=frames_rows[0:P:4, :], in_=log_frames.rearrange("(n q j) -> q n j", q=4, j=32))
-        back = f_words[EARLY:GROUPS].rearrange("g p n t -> p g (n t)")[:, :, 4 * P * FRONT :]
+        back = f_words[FULL:GROUPS].rearrange("g p n t -> p g (n t)")[:, :, 4 * P * FRONT :]
         nc.sync.dma_start(out=f_back[:].bitcast(I32), in_=back.bitcast(I32))
-        load_scales(f_back_planes, f_scales[:, :, P * FRONT :], EARLY, GROUPS)
 
         warm = bank(LAST, [P, WARM_N])
-        warm_passes(WARM_FREE, warm_codes[:])
-        warm_passes(WARM_TIED, f_first[:, 0, 0:WARM_N])
+        for i in range(WARM_PASSES):
+            nc.tensor.matmul_mx(
+                out=warm[:], lhsT=warm_codes[:, 0:P].bitcast(FP8X4), lhsT_scale=warm_plane[:, 0:P],
+                rhs=warm_codes[:].bitcast(FP8X4), rhs_scale=warm_plane[:], start=True, stop=True,
+            )
 
         est = [bank(n, [P, R]) for n in range(LAST)]
         halves = [bank(LAST, [P, HALF])]
-        for g in range(EARLY):
-            for n in range(LAST):
-                t_pass(n, g)
-            t_half(0, g)
-            for n in range(LAST):
-                a_pass(n, g)
-            a_half(0, g)
-        for g in range(EARLY, GROUPS - 1):
-            for weight_pass in (a_pass, t_pass) if g == EARLY else (t_pass, a_pass):
-                for n in range(FRONT):
+        for g in range(FULL):
+            weights = ((t_pass, t_half), (a_pass, a_half))
+            for weight_pass, weight_half in weights if g < EARLY else reversed(weights):
+                for n in range(LAST):
                     weight_pass(n, g)
+                weight_half(0, g)
+        for weight_pass in (a_pass, t_pass):
+            for n in range(FRONT):
+                weight_pass(n, FULL)
         last_group = [(weight_pass, n) for n in range(FRONT) for weight_pass in (t_pass, a_pass)]
         for weight_pass, n in last_group[:-3]:
             weight_pass(n, GROUPS - 1)
@@ -299,51 +306,41 @@ def tile_amortised_ivector_shrinkage_k3_kernel(
         for weight_pass, n in last_group[-3:]:
             weight_pass(n, GROUPS - 1)
 
-        blocks, gates = {}, {}
-        for n in range(COPIED):
-            product(n, gate(woven[n], n))
+        blocks, gates = {}, {n: gate(woven[n][:], n) for n in range(COPIED)}
+        for n in range(TURNED - 1):
+            if n >= COPIED:
+                gates[n] = gate(logits(n)[:], n)
+            if n > 1:
+                stage(n - 2, blocks[n - 2])
+            product(n, gates[n])
+            store_y(n, n + 1)
             if n > 0:
                 blocks[n - 1] = turn_blocks(n - 1)
-            round_to_pairs(n)
-            store_y(n, n + 1)
-        for n in range(COPIED, TURNED):
-            gates[n] = logits_and_gate(n)
-            stage(n - 2, blocks[n - 2])
-            if n == COPIED:
-                blocks[n - 1] = turn_blocks(n - 1)
-            nc.vector.tensor_tensor(out=pairs[:, n], in0=by_pairs(est[n][:]), in1=by_pairs(gates[n][:]), op=MULT)
-            blocks[n] = turn_blocks(n)
+            round_to_blocks(n)
+        n = TURNED - 1
+        gates[n] = gate(logits(n)[:], n)
+        stage(n - 2, blocks[n - 2])
+        nc.vector.tensor_tensor(out=block_words(n), in0=by_blocks(est[n][:]), in1=by_blocks(gates[n][:]), op=MULT)
+        blocks[n - 1] = turn_blocks(n - 1)
+        blocks[n] = turn_blocks(n)
+        product(n, gates[n])
         stage(TURNED - 2, blocks[TURNED - 2])
-        gates[TURNED] = logits_and_gate(TURNED)
+        gates[FRONT] = gate(logits(FRONT)[:], FRONT)
         stage(TURNED - 1, blocks[TURNED - 1])
-        for a in range(4):
-            for q in range(4):
-                if a != q:
-                    nc.sync.dma_start(out=landed[32 * q : 32 * q + 32, :, a, :], in_=staged[32 * a : 32 * a + 32, q])
-        for n in range(COPIED, TURNED):
-            product(n, gates[n])
-        store_y(COPIED, TURNED)
-
-        product(TURNED, gates[TURNED])
-        round_to_pairs(TURNED)
-        gates[FRONT - 1] = logits_and_gate(FRONT - 1)
-        product(FRONT - 1, gates[FRONT - 1])
-        store_y(TURNED, FRONT)
-        round_to_pairs(FRONT - 1)
-        for q in range(4):
-            nc.scalar.copy(out=landed[32 * q : 32 * q + 32, :, q, :], in_=staged[32 * q : 32 * q + 32, q])
-        gates[FRONT] = logits_and_gate(FRONT)
-        for g in range(EARLY, GROUPS):
+        store_y(TURNED - 1, TURNED)
+        for g in range(FULL, GROUPS):
             t_pass(FRONT, g)
             a_pass(FRONT, g)
         product(FRONT, gates[FRONT])
         store_y(FRONT, LAST)
-        round_to_pairs(FRONT)
+        quantize_landed(0, 2)
 
-        gates[LAST] = logits_and_gate(LAST)
+        z_last = logits(LAST)
+        half_gates = [gate(z_last[:, HALF * k : HALF * (k + 1)], LAST) for k in range(2)]
+        round_to_pairs(FRONT)
         halves.append(bank(FRONT, [P, HALF]))
         for k in range(2):
-            for g in range(EARLY if k == 0 else 0, GROUPS):
+            for g in range(FULL if k == 0 else 0, GROUPS):
                 t_half(k, g)
                 a_half(k, g)
 
@@ -352,32 +349,27 @@ def tile_amortised_ivector_shrinkage_k3_kernel(
             dst = pairs[:, LAST, :, P // 2 * k : P // 2 * (k + 1), :]
             for h in parts:
                 nc.vector.tensor_tensor(
-                    out=dst[:, h], in0=by_pairs(halves[k][:])[:, h], in1=by_pairs(gates[LAST][:, cols])[:, h], op=MULT
+                    out=dst[:, h], in0=by_pairs(halves[k][:])[:, h], in1=by_pairs(half_gates[k][:])[:, h], op=MULT
                 )
-            nc.vector.tensor_tensor(out=y[:, LAST, cols], in0=halves[k][:], in1=gates[LAST][:, cols], op=MULT)
+            nc.vector.tensor_tensor(out=y[:, LAST, cols], in0=halves[k][:], in1=half_gates[k][:], op=MULT)
 
         half_products(0, [slice(0, 2)])
-        quantize_y(0, TURNED, landed[:].rearrange("p n a w -> p (n a w)"))
-        store_words(0, TURNED, nc.sync)
+        quantize_landed(2, 4)
+        store_words(0, 4, nc.sync)
 
-        joined_pair = keep.tile([P, 2, P, 2], F32, align_bytes=256)
-        joined = {n: keep.tile([P, P, 2], F32, align_bytes=256, name="joined%d" % n) for n in (FRONT, LAST)}
+        joined = {n: keep.tile([P, P, 2], F32, align_bytes=256, name="joined%d" % n) for n in range(TURNED, TILES)}
         turned = {n: bank(n - 2, [P, 2, P]) for n in range(TURNED, TILES)}
         half_products(1, [slice(0, 1), slice(1, 2)])
         store_y(LAST, TILES)
+        quantize_landed(4, TURNED)
         for n in range(TURNED, TILES):
             for h in range(2):
                 words = pairs[:, n, h].rearrange("u p e -> u (p e)").bitcast(F32)
                 nc.tensor.transpose(turned[n][:, h, :], words, identity[:])
-        join(turned[TURNED][:], joined_pair[:, 0], nc.scalar.copy)
-        join(turned[TURNED + 1][:], joined_pair[:, 1], nc.vector.tensor_copy)
-        for n in (FRONT, LAST):
+        for n in range(TURNED, TILES):
             join(turned[n][:], joined[n][:], nc.scalar.copy)
-        quantize_y(TURNED, FRONT, joined_pair[:].rearrange("p n u h -> p (n u h)"))
-        store_words(TURNED, FRONT, nc.sync)
-        for n in (FRONT, LAST):
             quantize_y(n, n + 1, joined[n][:].rearrange("p u h -> p (u h)"))
-        store_words(FRONT, TILES, nc.scalar)
+            store_words(n if n == LAST else 4, n + 1, nc.scalar if n == LAST else nc.sync)
         scale_rows = out_2[0].rearrange("(q r) u -> r q u", r=4)
         for r, queue in enumerate((nc.sync, nc.sync, nc.scalar, nc.sync)):
             queue.dma_start(out=scale_rows[r].bitcast(I32), in_=y_plane[r:P:32, :].bitcast(I32))

@@ -30,7 +30,8 @@ PACKED = 4
 FIRST_TILES = 4
 VECTOR_COLS = 320
 WARM_N = 256
-WARM_PASSES = 10
+WARM_FREE = 7
+WARM_TIED = 2
 
 
 def tile_amortised_ivector_shrinkage_k3_kernel(
@@ -78,9 +79,9 @@ def tile_amortised_ivector_shrinkage_k3_kernel(
         def clear(planes):
             nc.vector.memset(planes[:].rearrange("p g n -> p (g n)").bitcast(I32), 0)
 
-        def load_scales(planes, scales, g0, g1, first=0):
+        def load_scales(planes, scales, g0, g1, which=range(4), first=0):
             rows = scales.rearrange("g (q r) n -> r q g n", r=4)
-            for r in range(4):
+            for r in which:
                 dst = planes[first + r : P : 32, :, :]
                 nc.sync.dma_start(out=dst.bitcast(I32), in_=rows[r][:, g0:g1, :].bitcast(I32))
 
@@ -236,9 +237,11 @@ def tile_amortised_ivector_shrinkage_k3_kernel(
         make_identity(nc, identity[:], nomemset=True)
 
         load_t(0, 1)
-        load_scales(t_early_planes, t_scales, 0, EARLY)
+        load_scales(t_early_planes, t_scales, 0, EARLY, range(1))
         load_f(0, 0, FIRST_TILES)
+        load_scales(t_early_planes, t_scales, 0, EARLY, range(1, 2))
         load_scales(f_first_planes, f_scales, 0, EARLY)
+        load_scales(t_early_planes, t_scales, 0, EARLY, range(2, 4))
         load_f(0, FIRST_TILES, TILES)
         load_a(0)
         for q in range(4):
@@ -270,9 +273,11 @@ def tile_amortised_ivector_shrinkage_k3_kernel(
         nc.sync.dma_start(out=f_back[:].bitcast(I32), in_=back.bitcast(I32))
 
         warm = bank(LAST, [P, WARM_N])
-        for i in range(WARM_PASSES):
+        free = (warm_codes[:, 0:P], warm_plane[:, 0:P])
+        tied = (f_full[0][:, 0:P], f_first_planes[:, 0, 0:P])
+        for held, held_plane in [free] * WARM_FREE + [tied] * WARM_TIED:
             nc.tensor.matmul_mx(
-                out=warm[:], lhsT=warm_codes[:, 0:P].bitcast(FP8X4), lhsT_scale=warm_plane[:, 0:P],
+                out=warm[:], lhsT=held.bitcast(FP8X4), lhsT_scale=held_plane,
                 rhs=warm_codes[:].bitcast(FP8X4), rhs_scale=warm_plane[:], start=True, stop=True,
             )
 
@@ -334,9 +339,10 @@ def tile_amortised_ivector_shrinkage_k3_kernel(
         product(FRONT, gates[FRONT])
         store_y(FRONT, LAST)
         quantize_landed(0, 2)
+        quantize_landed(2, 4)
+        store_words(0, 4, nc.sync)
 
-        z_last = logits(LAST)
-        half_gates = [gate(z_last[:, HALF * k : HALF * (k + 1)], LAST) for k in range(2)]
+        gates[LAST] = gate(logits(LAST)[:], LAST)
         round_to_pairs(FRONT)
         halves.append(bank(FRONT, [P, HALF]))
         for k in range(2):
@@ -349,13 +355,11 @@ def tile_amortised_ivector_shrinkage_k3_kernel(
             dst = pairs[:, LAST, :, P // 2 * k : P // 2 * (k + 1), :]
             for h in parts:
                 nc.vector.tensor_tensor(
-                    out=dst[:, h], in0=by_pairs(halves[k][:])[:, h], in1=by_pairs(half_gates[k][:])[:, h], op=MULT
+                    out=dst[:, h], in0=by_pairs(halves[k][:])[:, h], in1=by_pairs(gates[LAST][:, cols])[:, h], op=MULT
                 )
-            nc.vector.tensor_tensor(out=y[:, LAST, cols], in0=halves[k][:], in1=half_gates[k][:], op=MULT)
+            nc.vector.tensor_tensor(out=y[:, LAST, cols], in0=halves[k][:], in1=gates[LAST][:, cols], op=MULT)
 
         half_products(0, [slice(0, 2)])
-        quantize_landed(2, 4)
-        store_words(0, 4, nc.sync)
 
         joined = {n: keep.tile([P, P, 2], F32, align_bytes=256, name="joined%d" % n) for n in range(TURNED, TILES)}
         turned = {n: bank(n - 2, [P, 2, P]) for n in range(TURNED, TILES)}

@@ -26,12 +26,14 @@ FULL = 3
 FRONT = 6
 COPIED = 2
 TURNED = 6
+SETTLED = 4
 PACKED = 4
 FIRST_TILES = 4
 VECTOR_COLS = 320
 WARM_N = 256
 WARM_FREE = 7
-WARM_TIED = 2
+WARM_CODES = 3
+WARM_PLANE = 2
 
 
 def tile_amortised_ivector_shrinkage_k3_kernel(
@@ -161,15 +163,15 @@ def tile_amortised_ivector_shrinkage_k3_kernel(
             mx_pass(z[:], n, g, v_codes[:, g, :].bitcast(FP8X4), v_planes[:, g, :], g == 0, g == GROUPS - 1)
 
         def gate(z, n):
-            sig = ring.tile(list(z.shape), F32, align_bytes=256, name="sig")
-            nc.scalar.activation(out=sig[:], in_=z, func=SIGMOID, bias=frames_cols[:, 4 * n : 4 * n + 1])
+            sig = ring.tile([P, R], F32, align_bytes=256, name="sig")
+            nc.scalar.activation(out=sig[:], in_=z[:], func=SIGMOID, bias=frames_cols[:, 4 * n : 4 * n + 1])
             return sig
 
-        def logits(n):
+        def logits_and_gate(n):
             z = bank(n % COPIED, [P, R])
             for g in range(GROUPS):
                 z_pass(z, n, g)
-            return z
+            return gate(z, n)
 
         def product(n, sig):
             src = est_sb[:, n, :] if n < COPIED else est[n][:]
@@ -181,9 +183,6 @@ def tile_amortised_ivector_shrinkage_k3_kernel(
 
         def by_pairs(ap):
             return ap.rearrange("u (p h e) -> u h p e", h=2, e=2)
-
-        def round_to_pairs(n):
-            nc.scalar.copy(out=pairs[:, n], in_=by_pairs(y[:, n, :]))
 
         def by_blocks(ap):
             return ap.rearrange("u (i b e) -> u b i e", b=8, e=2)
@@ -211,9 +210,6 @@ def tile_amortised_ivector_shrinkage_k3_kernel(
 
         def quantize_landed(n0, n1):
             quantize_y(n0, n1, landed[:, n0:n1].rearrange("p n a w -> p (n a w)"))
-
-        def join(turned, dst, copy):
-            copy(out=dst, in_=turned.rearrange("p h u -> p u h"))
 
         def quantize_y(n0, n1, words):
             cols = slice(P * n0, P * n1)
@@ -274,8 +270,9 @@ def tile_amortised_ivector_shrinkage_k3_kernel(
 
         warm = bank(LAST, [P, WARM_N])
         free = (warm_codes[:, 0:P], warm_plane[:, 0:P])
-        tied = (f_full[0][:, 0:P], f_first_planes[:, 0, 0:P])
-        for held, held_plane in [free] * WARM_FREE + [tied] * WARM_TIED:
+        with_codes = (f_full[0][:, 0:P], warm_plane[:, 0:P])
+        with_plane = (f_full[0][:, 0:P], f_first_planes[:, 0, 0:P])
+        for held, held_plane in [free] * WARM_FREE + [with_codes] * WARM_CODES + [with_plane] * WARM_PLANE:
             nc.tensor.matmul_mx(
                 out=warm[:], lhsT=held.bitcast(FP8X4), lhsT_scale=held_plane,
                 rhs=warm_codes[:].bitcast(FP8X4), rhs_scale=warm_plane[:], start=True, stop=True,
@@ -311,10 +308,10 @@ def tile_amortised_ivector_shrinkage_k3_kernel(
         for weight_pass, n in last_group[-3:]:
             weight_pass(n, GROUPS - 1)
 
-        blocks, gates = {}, {n: gate(woven[n][:], n) for n in range(COPIED)}
+        blocks, gates = {}, {n: gate(woven[n], n) for n in range(COPIED)}
         for n in range(TURNED - 1):
             if n >= COPIED:
-                gates[n] = gate(logits(n)[:], n)
+                gates[n] = logits_and_gate(n)
             if n > 1:
                 stage(n - 2, blocks[n - 2])
             product(n, gates[n])
@@ -323,28 +320,28 @@ def tile_amortised_ivector_shrinkage_k3_kernel(
                 blocks[n - 1] = turn_blocks(n - 1)
             round_to_blocks(n)
         n = TURNED - 1
-        gates[n] = gate(logits(n)[:], n)
+        gates[n] = logits_and_gate(n)
         stage(n - 2, blocks[n - 2])
         nc.vector.tensor_tensor(out=block_words(n), in0=by_blocks(est[n][:]), in1=by_blocks(gates[n][:]), op=MULT)
         blocks[n - 1] = turn_blocks(n - 1)
         blocks[n] = turn_blocks(n)
         product(n, gates[n])
-        stage(TURNED - 2, blocks[TURNED - 2])
-        gates[FRONT] = gate(logits(FRONT)[:], FRONT)
-        stage(TURNED - 1, blocks[TURNED - 1])
-        store_y(TURNED - 1, TURNED)
+        stage(n - 1, blocks[n - 1])
+        gates[FRONT] = logits_and_gate(FRONT)
+        stage(n, blocks[n])
+        store_y(n, n + 1)
         for g in range(FULL, GROUPS):
             t_pass(FRONT, g)
             a_pass(FRONT, g)
+        quantize_landed(0, 2)
         product(FRONT, gates[FRONT])
         store_y(FRONT, LAST)
-        quantize_landed(0, 2)
-        quantize_landed(2, 4)
-        store_words(0, 4, nc.sync)
+        quantize_landed(2, SETTLED)
+        store_words(0, SETTLED, nc.sync)
 
-        gates[LAST] = gate(logits(LAST)[:], LAST)
-        round_to_pairs(FRONT)
-        halves.append(bank(FRONT, [P, HALF]))
+        gates[LAST] = logits_and_gate(LAST)
+        nc.scalar.copy(out=pairs[:, FRONT], in_=by_pairs(y[:, FRONT, :]))
+        halves.append(bank(COPIED, [P, HALF]))
         for k in range(2):
             for g in range(FULL if k == 0 else 0, GROUPS):
                 t_half(k, g)
@@ -365,15 +362,17 @@ def tile_amortised_ivector_shrinkage_k3_kernel(
         turned = {n: bank(n - 2, [P, 2, P]) for n in range(TURNED, TILES)}
         half_products(1, [slice(0, 1), slice(1, 2)])
         store_y(LAST, TILES)
-        quantize_landed(4, TURNED)
+        quantize_landed(SETTLED, TURNED)
         for n in range(TURNED, TILES):
             for h in range(2):
                 words = pairs[:, n, h].rearrange("u p e -> u (p e)").bitcast(F32)
                 nc.tensor.transpose(turned[n][:, h, :], words, identity[:])
         for n in range(TURNED, TILES):
-            join(turned[n][:], joined[n][:], nc.scalar.copy)
+            nc.scalar.copy(out=joined[n][:], in_=turned[n][:].rearrange("p h u -> p u h"))
             quantize_y(n, n + 1, joined[n][:].rearrange("p u h -> p (u h)"))
-            store_words(n if n == LAST else 4, n + 1, nc.scalar if n == LAST else nc.sync)
+            if n == FRONT:
+                store_words(SETTLED, LAST, nc.sync)
+        store_words(LAST, TILES, nc.scalar)
         scale_rows = out_2[0].rearrange("(q r) u -> r q u", r=4)
         for r, queue in enumerate((nc.sync, nc.sync, nc.scalar, nc.sync)):
             queue.dma_start(out=scale_rows[r].bitcast(I32), in_=y_plane[r:P:32, :].bitcast(I32))

@@ -21,19 +21,19 @@ GROUPS = K // 512
 TILES = U // P
 LAST = TILES - 1
 HALF = R // 2
-EARLY = 2
+STAGED = 2
 FULL = 3
-FRONT = 6
+FRONT = 5
+HELD = (3, 2, 1)
 COPIED = 2
 TURNED = 6
 SETTLED = 4
 PACKED = 4
-FIRST_TILES = 4
+FIRST_TILES = 2
 VECTOR_COLS = 320
-WARM_N = 256
-WARM_FREE = 7
-WARM_CODES = 3
-WARM_PLANE = 2
+WARM_N = 128
+WARM_FREE = 11
+WARM_CODES = 1
 
 
 def tile_amortised_ivector_shrinkage_k3_kernel(
@@ -52,10 +52,10 @@ def tile_amortised_ivector_shrinkage_k3_kernel(
         t_codes = keep.tile([P, GROUPS, 2 * R], U8, align_bytes=256)
         a_codes = keep.tile([P, GROUPS, R], U32, align_bytes=256)
         v_codes = keep.tile([P, GROUPS, R], U32, align_bytes=256)
-        f_first_planes = keep.tile([P, EARLY, U], U8, align_bytes=256)
-        t_early_planes = keep.tile([P, EARLY, R], U8, align_bytes=256)
-        f_late_planes = keep.tile([P, GROUPS - EARLY, U], U8, align_bytes=256)
-        t_late_planes = keep.tile([P, GROUPS - EARLY, R], U8, align_bytes=256)
+        f_staged = [keep.tile([P, 2, U], U8, align_bytes=256, name="f_staged%d" % g) for g in range(STAGED)]
+        t_staged = [keep.tile([P, 2, R], U8, align_bytes=256, name="t_staged%d" % g) for g in range(STAGED)]
+        f_late_planes = keep.tile([P, GROUPS - STAGED, U], U8, align_bytes=256)
+        t_late_planes = keep.tile([P, GROUPS - STAGED, R], U8, align_bytes=256)
         a_packed_planes = keep.tile([P, 1, R], U8, align_bytes=256)
         a_last_plane = keep.tile([P, 1, R], U8, align_bytes=256)
         v_planes = keep.tile([P, GROUPS, R], U8, align_bytes=256)
@@ -78,19 +78,27 @@ def tile_amortised_ivector_shrinkage_k3_kernel(
         def bank(b, shape):
             return psum.tile(shape, F32, name="bank%d" % b, tag="bank%d" % b)
 
-        def clear(planes):
-            nc.vector.memset(planes[:].rearrange("p g n -> p (g n)").bitcast(I32), 0)
+        def load_staged(staged_plane, scales, g, half, queue):
+            rows = scales[g, 8 * half : 8 * half + 8, :].rearrange("(s r) n -> r s n", r=4)
+            dst = staged_plane[64 * half : 64 * half + 4, :, :]
+            queue.dma_start(out=dst.bitcast(I32), in_=rows.bitcast(I32))
 
-        def load_scales(planes, scales, g0, g1, which=range(4), first=0):
+        def lift(staged_plane, half, c0, c1):
+            nc.vector.tensor_copy(
+                out=staged_plane[64 * half + 32 : 64 * half + 36, 0, c0:c1].bitcast(I32),
+                in_=staged_plane[64 * half : 64 * half + 4, 1, c0:c1].bitcast(I32),
+            )
+
+        def load_scales(planes, scales, g0, g1, first=0):
             rows = scales.rearrange("g (q r) n -> r q g n", r=4)
-            for r in which:
+            for r in range(4):
                 dst = planes[first + r : P : 32, :, :]
                 nc.sync.dma_start(out=dst.bitcast(I32), in_=rows[r][:, g0:g1, :].bitcast(I32))
 
-        def load_f(g, n0, n1):
+        def load_f(g, n0, n1, queue=nc.sync):
             src = f_words[g].rearrange("p n t -> p (n t)")[:, 4 * P * n0 : 4 * P * n1]
             dst = f_full[g][:, P * n0 : P * n1] if g < FULL else f_front[:, g - FULL, P * n0 : P * n1]
-            nc.sync.dma_start(out=dst.bitcast(I32), in_=src.bitcast(I32))
+            queue.dma_start(out=dst.bitcast(I32), in_=src.bitcast(I32))
 
         def load_t(g0, g1):
             src = t_words[g0:g1].rearrange("g p n -> p g n")
@@ -111,7 +119,7 @@ def tile_amortised_ivector_shrinkage_k3_kernel(
                 held = f_front[:, g - FULL, P * n : P * (n + 1)]
             else:
                 held = f_back[:, g - FULL, P * (n - FRONT) : P * (n - FRONT + 1)]
-            held_plane = f_first_planes[:, g, :] if g < EARLY else f_late_planes[:, g - EARLY, :]
+            held_plane = f_staged[g][:, 0, :] if g < STAGED else f_late_planes[:, g - STAGED, :]
             nc.tensor.matmul_mx(
                 out=acc,
                 lhsT=held.bitcast(FP8X4),
@@ -123,7 +131,7 @@ def tile_amortised_ivector_shrinkage_k3_kernel(
             )
 
         def t_part(acc, n, g, start, c0, c1):
-            plane = t_early_planes[:, g, c0:c1] if g < EARLY else t_late_planes[:, g - EARLY, c0:c1]
+            plane = t_staged[g][:, 0, c0:c1] if g < STAGED else t_late_planes[:, g - STAGED, c0:c1]
             mx_pass(acc, n, g, t_codes[:, g, 2 * c0 : 2 * c1].bitcast(FP4X4), plane, start, False)
 
         def a_part(acc, n, g, c0, c1):
@@ -219,25 +227,17 @@ def tile_amortised_ivector_shrinkage_k3_kernel(
             dst = out_1[0].rearrange("p u t -> p (u t)")[:, 4 * P * n0 : 4 * P * n1]
             queue.dma_start(out=dst.bitcast(I32), in_=y_codes[:, P * n0 : P * n1].bitcast(I32))
 
-        clear(t_early_planes)
-        nc.vector.memset(warm_in[:].bitcast(I32), 0x3F803F80)
-        clear(f_first_planes)
+        nc.gpsimd.memset(warm_in[:].bitcast(I32), 0x3F803F80)
         nc.vector.quantize_mx(out=warm_codes[:].bitcast(FP8X4), scales=warm_plane[:], in_=warm_in[:])
-        clear(a_packed_planes)
-        clear(f_late_planes)
-        clear(t_late_planes)
-        clear(a_last_plane)
         nc.vector.memset(frames_rows[:], 0.0)
-        nc.vector.memset(identity[:], 0.0)
-        nc.scalar.activation(out=warm_act[:], in_=warm_in[:, 0:1], func=SIGMOID)
-        make_identity(nc, identity[:], nomemset=True)
 
+        for half, queue in enumerate((nc.sync, nc.scalar)):
+            load_staged(t_staged[0], t_scales, 0, half, queue)
+        for half, queue in enumerate((nc.sync, nc.scalar)):
+            load_staged(f_staged[0], f_scales, 0, half, queue)
         load_t(0, 1)
-        load_scales(t_early_planes, t_scales, 0, EARLY, range(1))
-        load_f(0, 0, FIRST_TILES)
-        load_scales(t_early_planes, t_scales, 0, EARLY, range(1, 2))
-        load_scales(f_first_planes, f_scales, 0, EARLY)
-        load_scales(t_early_planes, t_scales, 0, EARLY, range(2, 4))
+        load_f(0, 0, FIRST_TILES, nc.scalar)
+        nc.scalar.activation(out=warm_act[:], in_=warm_in[:, 0:1], func=SIGMOID)
         load_f(0, FIRST_TILES, TILES)
         load_a(0)
         for q in range(4):
@@ -245,20 +245,24 @@ def tile_amortised_ivector_shrinkage_k3_kernel(
                 out=a_packed_planes[32 * q : 32 * q + 4 * PACKED, 0, :].bitcast(I32),
                 in_=a_scales[0:PACKED, 4 * q : 4 * q + 4, :].bitcast(I32),
             )
-        load_t(1, 2)
         load_f(1, 0, TILES)
         load_a(1)
-        load_scales(f_late_planes, f_scales, EARLY, GROUPS)
+        for half in range(2):
+            load_staged(f_staged[1], f_scales, 1, half, nc.sync)
+        for half in range(2):
+            load_staged(t_staged[1], t_scales, 1, half, nc.sync)
+        load_t(1, 2)
+        load_scales(f_late_planes, f_scales, STAGED, GROUPS)
+        load_v(0)
         load_f(2, 0, TILES)
         load_a(2)
-        load_scales(t_late_planes, t_scales, EARLY, GROUPS)
+        load_scales(t_late_planes, t_scales, STAGED, GROUPS)
         load_t(2, 3)
+        load_v(1)
         load_f(3, 0, FRONT)
         load_a(3)
-        load_v(0)
-        load_t(3, GROUPS)
-        load_v(1)
         load_v(2)
+        load_t(3, GROUPS)
         load_f(4, 0, FRONT)
         load_scales(a_last_plane, a_scales, PACKED, GROUPS, first=4)
         load_a(4)
@@ -268,11 +272,22 @@ def tile_amortised_ivector_shrinkage_k3_kernel(
         back = f_words[FULL:GROUPS].rearrange("g p n t -> p g (n t)")[:, :, 4 * P * FRONT :]
         nc.sync.dma_start(out=f_back[:].bitcast(I32), in_=back.bitcast(I32))
 
+        for half in range(2):
+            lift(t_staged[0], half, 0, R)
+        for c0, c1 in ((0, P * FIRST_TILES), (P * FIRST_TILES, U)):
+            for half in range(2):
+                lift(f_staged[0], half, c0, c1)
+        nc.vector.memset(identity[:], 0.0)
+        make_identity(nc, identity[:], nomemset=True)
+        for half in range(2):
+            lift(f_staged[1], half, 0, U)
+        for half in range(2):
+            lift(t_staged[1], half, 0, R)
+
         warm = bank(LAST, [P, WARM_N])
         free = (warm_codes[:, 0:P], warm_plane[:, 0:P])
         with_codes = (f_full[0][:, 0:P], warm_plane[:, 0:P])
-        with_plane = (f_full[0][:, 0:P], f_first_planes[:, 0, 0:P])
-        for held, held_plane in [free] * WARM_FREE + [with_codes] * WARM_CODES + [with_plane] * WARM_PLANE:
+        for held, held_plane in [free] * WARM_FREE + [with_codes] * WARM_CODES:
             nc.tensor.matmul_mx(
                 out=warm[:], lhsT=held.bitcast(FP8X4), lhsT_scale=held_plane,
                 rhs=warm_codes[:].bitcast(FP8X4), rhs_scale=warm_plane[:], start=True, stop=True,
@@ -282,22 +297,27 @@ def tile_amortised_ivector_shrinkage_k3_kernel(
         halves = [bank(LAST, [P, HALF])]
         for g in range(FULL):
             weights = ((t_pass, t_half), (a_pass, a_half))
-            for weight_pass, weight_half in weights if g < EARLY else reversed(weights):
+            for weight_pass, weight_half in weights if g == 0 else reversed(weights):
                 for n in range(LAST):
                     weight_pass(n, g)
                 weight_half(0, g)
-        for weight_pass in (a_pass, t_pass):
-            for n in range(FRONT):
-                weight_pass(n, FULL)
-        last_group = [(weight_pass, n) for n in range(FRONT) for weight_pass in (t_pass, a_pass)]
-        for weight_pass, n in last_group[:-3]:
-            weight_pass(n, GROUPS - 1)
+        later = [(weight_pass, n, FULL) for weight_pass in (a_pass, t_pass) for n in range(FRONT)]
+        later += [(weight_pass, n, GROUPS - 1) for n in range(FRONT) for weight_pass in (t_pass, a_pass)]
+        for n in range(FRONT, TURNED):
+            later += [(weight_pass, n, g) for g in range(FULL, GROUPS) for weight_pass in (t_pass, a_pass)]
+
+        def take_later(count):
+            for weight_pass, n, g in later[:count]:
+                weight_pass(n, g)
+            later[:count] = []
+
+        take_later(len(later) - sum(HELD))
 
         for g in range(GROUPS):
-            if g == GROUPS - 2:
+            if g == GROUPS - 1:
                 for n in range(COPIED):
                     nc.scalar.copy(out=est_sb[:, n, :], in_=est[n][:])
-            quantize_v(g, interleave_v(g, R if g == GROUPS - 2 else VECTOR_COLS))
+            quantize_v(g, interleave_v(g, R if g == GROUPS - 1 else VECTOR_COLS))
         nc.vector.transpose(frames_cols[:], frames_rows[:])
 
         woven = [bank(n, [P, R]) for n in range(COPIED)]
@@ -305,13 +325,14 @@ def tile_amortised_ivector_shrinkage_k3_kernel(
             for n in range(COPIED):
                 for g in groups:
                     z_pass(woven[n], n, g)
-        for weight_pass, n in last_group[-3:]:
-            weight_pass(n, GROUPS - 1)
+        take_later(HELD[0])
 
         blocks, gates = {}, {n: gate(woven[n], n) for n in range(COPIED)}
         for n in range(TURNED - 1):
             if n >= COPIED:
                 gates[n] = logits_and_gate(n)
+                if n <= len(HELD):
+                    take_later(HELD[n - 1])
             if n > 1:
                 stage(n - 2, blocks[n - 2])
             product(n, gates[n])
@@ -327,20 +348,20 @@ def tile_amortised_ivector_shrinkage_k3_kernel(
         blocks[n] = turn_blocks(n)
         product(n, gates[n])
         stage(n - 1, blocks[n - 1])
-        gates[FRONT] = logits_and_gate(FRONT)
+        gates[TURNED] = logits_and_gate(TURNED)
         stage(n, blocks[n])
         store_y(n, n + 1)
         for g in range(FULL, GROUPS):
-            t_pass(FRONT, g)
-            a_pass(FRONT, g)
+            t_pass(TURNED, g)
+            a_pass(TURNED, g)
         quantize_landed(0, 2)
-        product(FRONT, gates[FRONT])
-        store_y(FRONT, LAST)
+        product(TURNED, gates[TURNED])
+        store_y(TURNED, LAST)
         quantize_landed(2, SETTLED)
         store_words(0, SETTLED, nc.sync)
 
         gates[LAST] = logits_and_gate(LAST)
-        nc.scalar.copy(out=pairs[:, FRONT], in_=by_pairs(y[:, FRONT, :]))
+        nc.scalar.copy(out=pairs[:, TURNED], in_=by_pairs(y[:, TURNED, :]))
         halves.append(bank(COPIED, [P, HALF]))
         for k in range(2):
             for g in range(FULL if k == 0 else 0, GROUPS):
@@ -370,7 +391,7 @@ def tile_amortised_ivector_shrinkage_k3_kernel(
         for n in range(TURNED, TILES):
             nc.scalar.copy(out=joined[n][:], in_=turned[n][:].rearrange("p h u -> p u h"))
             quantize_y(n, n + 1, joined[n][:].rearrange("p u h -> p (u h)"))
-            if n == FRONT:
+            if n == TURNED:
                 store_words(SETTLED, LAST, nc.sync)
         store_words(LAST, TILES, nc.scalar)
         scale_rows = out_2[0].rearrange("(q r) u -> r q u", r=4)

@@ -21,10 +21,9 @@ GROUPS = K // 512
 TILES = U // P
 LAST = TILES - 1
 HALF = R // 2
-STAGED = 2
 FULL = 3
-FRONT = 5
-HELD = (3, 2, 1)
+FRONT = 6
+HELD = (3,)
 COPIED = 2
 TURNED = 6
 SETTLED = 4
@@ -52,10 +51,11 @@ def tile_amortised_ivector_shrinkage_k3_kernel(
         t_codes = keep.tile([P, GROUPS, 2 * R], U8, align_bytes=256)
         a_codes = keep.tile([P, GROUPS, R], U32, align_bytes=256)
         v_codes = keep.tile([P, GROUPS, R], U32, align_bytes=256)
-        f_staged = [keep.tile([P, 2, U], U8, align_bytes=256, name="f_staged%d" % g) for g in range(STAGED)]
-        t_staged = [keep.tile([P, 2, R], U8, align_bytes=256, name="t_staged%d" % g) for g in range(STAGED)]
-        f_late_planes = keep.tile([P, GROUPS - STAGED, U], U8, align_bytes=256)
-        t_late_planes = keep.tile([P, GROUPS - STAGED, R], U8, align_bytes=256)
+        f_staged = keep.tile([P, 2, U], U8, align_bytes=256)
+        t_staged = keep.tile([P, 2, R], U8, align_bytes=256)
+        f_second_plane = keep.tile([P, 1, U], U8, align_bytes=256)
+        f_late_planes = keep.tile([P, GROUPS - 2, U], U8, align_bytes=256)
+        t_late_planes = keep.tile([P, GROUPS - 1, R], U8, align_bytes=256)
         a_packed_planes = keep.tile([P, 1, R], U8, align_bytes=256)
         a_last_plane = keep.tile([P, 1, R], U8, align_bytes=256)
         v_planes = keep.tile([P, GROUPS, R], U8, align_bytes=256)
@@ -119,7 +119,7 @@ def tile_amortised_ivector_shrinkage_k3_kernel(
                 held = f_front[:, g - FULL, P * n : P * (n + 1)]
             else:
                 held = f_back[:, g - FULL, P * (n - FRONT) : P * (n - FRONT + 1)]
-            held_plane = f_staged[g][:, 0, :] if g < STAGED else f_late_planes[:, g - STAGED, :]
+            held_plane = (f_staged, f_second_plane)[g][:, 0, :] if g < 2 else f_late_planes[:, g - 2, :]
             nc.tensor.matmul_mx(
                 out=acc,
                 lhsT=held.bitcast(FP8X4),
@@ -131,7 +131,7 @@ def tile_amortised_ivector_shrinkage_k3_kernel(
             )
 
         def t_part(acc, n, g, start, c0, c1):
-            plane = t_staged[g][:, 0, c0:c1] if g < STAGED else t_late_planes[:, g - STAGED, c0:c1]
+            plane = t_staged[:, 0, c0:c1] if g == 0 else t_late_planes[:, g - 1, c0:c1]
             mx_pass(acc, n, g, t_codes[:, g, 2 * c0 : 2 * c1].bitcast(FP4X4), plane, start, False)
 
         def a_part(acc, n, g, c0, c1):
@@ -150,14 +150,13 @@ def tile_amortised_ivector_shrinkage_k3_kernel(
         def a_half(k, g):
             a_part(halves[k][:], LAST, g, HALF * k, HALF * (k + 1))
 
-        def interleave_v(g, vector_cols):
+        def interleave_v(g):
             grouped = ring.tile([P, R, 4], BF16, align_bytes=256, name="v_grouped")
             src = v_rows[g][:].rearrange("p t (c i) -> p c t i", i=4)
             dst = grouped[:].rearrange("p (c i) t -> p c t i", i=4)
-            split = vector_cols // 4
+            split = VECTOR_COLS // 4
             nc.vector.tensor_copy(out=dst[:, :split], in_=src[:, :split])
-            if vector_cols < R:
-                nc.scalar.copy(out=dst[:, split:], in_=src[:, split:])
+            nc.scalar.copy(out=dst[:, split:], in_=src[:, split:])
             return grouped
 
         def quantize_v(g, grouped):
@@ -232,13 +231,14 @@ def tile_amortised_ivector_shrinkage_k3_kernel(
         nc.vector.memset(frames_rows[:], 0.0)
 
         for half, queue in enumerate((nc.sync, nc.scalar)):
-            load_staged(t_staged[0], t_scales, 0, half, queue)
+            load_staged(t_staged, t_scales, 0, half, queue)
         for half, queue in enumerate((nc.sync, nc.scalar)):
-            load_staged(f_staged[0], f_scales, 0, half, queue)
+            load_staged(f_staged, f_scales, 0, half, queue)
         load_t(0, 1)
         load_f(0, 0, FIRST_TILES, nc.scalar)
         nc.scalar.activation(out=warm_act[:], in_=warm_in[:, 0:1], func=SIGMOID)
-        load_f(0, FIRST_TILES, TILES)
+        load_f(0, FIRST_TILES, 2 * FIRST_TILES)
+        load_f(0, 2 * FIRST_TILES, TILES)
         load_a(0)
         for q in range(4):
             nc.sync.dma_start(
@@ -246,21 +246,18 @@ def tile_amortised_ivector_shrinkage_k3_kernel(
                 in_=a_scales[0:PACKED, 4 * q : 4 * q + 4, :].bitcast(I32),
             )
         load_f(1, 0, TILES)
+        load_scales(f_second_plane, f_scales, 1, 2)
         load_a(1)
-        for half in range(2):
-            load_staged(f_staged[1], f_scales, 1, half, nc.sync)
-        for half in range(2):
-            load_staged(t_staged[1], t_scales, 1, half, nc.sync)
         load_t(1, 2)
-        load_scales(f_late_planes, f_scales, STAGED, GROUPS)
-        load_v(0)
+        load_scales(t_late_planes, t_scales, 1, GROUPS)
         load_f(2, 0, TILES)
         load_a(2)
-        load_scales(t_late_planes, t_scales, STAGED, GROUPS)
+        load_scales(f_late_planes, f_scales, 2, GROUPS)
         load_t(2, 3)
-        load_v(1)
+        load_v(0)
         load_f(3, 0, FRONT)
         load_a(3)
+        load_v(1)
         load_v(2)
         load_t(3, GROUPS)
         load_f(4, 0, FRONT)
@@ -273,16 +270,12 @@ def tile_amortised_ivector_shrinkage_k3_kernel(
         nc.sync.dma_start(out=f_back[:].bitcast(I32), in_=back.bitcast(I32))
 
         for half in range(2):
-            lift(t_staged[0], half, 0, R)
+            lift(t_staged, half, 0, R)
         for c0, c1 in ((0, P * FIRST_TILES), (P * FIRST_TILES, U)):
             for half in range(2):
-                lift(f_staged[0], half, c0, c1)
+                lift(f_staged, half, c0, c1)
         nc.vector.memset(identity[:], 0.0)
         make_identity(nc, identity[:], nomemset=True)
-        for half in range(2):
-            lift(f_staged[1], half, 0, U)
-        for half in range(2):
-            lift(t_staged[1], half, 0, R)
 
         warm = bank(LAST, [P, WARM_N])
         free = (warm_codes[:, 0:P], warm_plane[:, 0:P])
@@ -313,11 +306,13 @@ def tile_amortised_ivector_shrinkage_k3_kernel(
 
         take_later(len(later) - sum(HELD))
 
-        for g in range(GROUPS):
-            if g == GROUPS - 1:
-                for n in range(COPIED):
-                    nc.scalar.copy(out=est_sb[:, n, :], in_=est[n][:])
-            quantize_v(g, interleave_v(g, R if g == GROUPS - 1 else VECTOR_COLS))
+        for g in range(GROUPS - 2):
+            quantize_v(g, interleave_v(g))
+        for n in range(COPIED):
+            nc.scalar.copy(out=est_sb[:, n, :], in_=est[n][:])
+        last_groups = [(g, interleave_v(g)) for g in range(GROUPS - 2, GROUPS)]
+        for g, grouped in last_groups:
+            quantize_v(g, grouped)
         nc.vector.transpose(frames_cols[:], frames_rows[:])
 
         woven = [bank(n, [P, R]) for n in range(COPIED)]

@@ -23,8 +23,8 @@ LAST = TILES - 1
 HALF = R // 2
 FULL = 3
 FRONT = 6
-HELD = (3,)
-COPIED = 2
+HELD = 4
+COPIED = 3
 TURNED = 6
 SETTLED = 4
 PACKED = 4
@@ -150,13 +150,14 @@ def tile_amortised_ivector_shrinkage_k3_kernel(
         def a_half(k, g):
             a_part(halves[k][:], LAST, g, HALF * k, HALF * (k + 1))
 
-        def interleave_v(g):
+        def interleave_v(g, vector_cols):
             grouped = ring.tile([P, R, 4], BF16, align_bytes=256, name="v_grouped")
             src = v_rows[g][:].rearrange("p t (c i) -> p c t i", i=4)
             dst = grouped[:].rearrange("p (c i) t -> p c t i", i=4)
-            split = VECTOR_COLS // 4
+            split = vector_cols // 4
             nc.vector.tensor_copy(out=dst[:, :split], in_=src[:, :split])
-            nc.scalar.copy(out=dst[:, split:], in_=src[:, split:])
+            if vector_cols < R:
+                nc.scalar.copy(out=dst[:, split:], in_=src[:, split:])
             return grouped
 
         def quantize_v(g, grouped):
@@ -197,8 +198,7 @@ def tile_amortised_ivector_shrinkage_k3_kernel(
         def block_words(n):
             return pairs[:, n].rearrange("u h p e -> u (h p e)").rearrange("u (b i e) -> u b i e", b=8, e=2)
 
-        def round_to_blocks(n):
-            copy = nc.scalar.copy if n < COPIED else nc.vector.tensor_copy
+        def round_to_blocks(n, copy):
             copy(out=block_words(n), in_=by_blocks(y[:, n, :]))
 
         def turn_blocks(n):
@@ -245,21 +245,23 @@ def tile_amortised_ivector_shrinkage_k3_kernel(
                 out=a_packed_planes[32 * q : 32 * q + 4 * PACKED, 0, :].bitcast(I32),
                 in_=a_scales[0:PACKED, 4 * q : 4 * q + 4, :].bitcast(I32),
             )
-        load_f(1, 0, TILES)
+        load_f(1, 0, TILES // 2)
         load_scales(f_second_plane, f_scales, 1, 2)
         load_a(1)
+        load_f(1, TILES // 2, TILES)
         load_t(1, 2)
         load_scales(t_late_planes, t_scales, 1, GROUPS)
-        load_f(2, 0, TILES)
-        load_a(2)
+        load_f(2, 0, TILES // 2)
         load_scales(f_late_planes, f_scales, 2, GROUPS)
+        load_a(2)
+        load_f(2, TILES // 2, TILES)
         load_t(2, 3)
         load_v(0)
         load_f(3, 0, FRONT)
         load_a(3)
         load_v(1)
-        load_v(2)
         load_t(3, GROUPS)
+        load_v(2)
         load_f(4, 0, FRONT)
         load_scales(a_last_plane, a_scales, PACKED, GROUPS, first=4)
         load_a(4)
@@ -295,7 +297,8 @@ def tile_amortised_ivector_shrinkage_k3_kernel(
                     weight_pass(n, g)
                 weight_half(0, g)
         later = [(weight_pass, n, FULL) for weight_pass in (a_pass, t_pass) for n in range(FRONT)]
-        later += [(weight_pass, n, GROUPS - 1) for n in range(FRONT) for weight_pass in (t_pass, a_pass)]
+        later += [(weight_pass, n, GROUPS - 1) for weight_pass in (t_pass, a_pass) for n in range(COPIED)]
+        later += [(weight_pass, n, GROUPS - 1) for n in range(COPIED, FRONT) for weight_pass in (t_pass, a_pass)]
         for n in range(FRONT, TURNED):
             later += [(weight_pass, n, g) for g in range(FULL, GROUPS) for weight_pass in (t_pass, a_pass)]
 
@@ -304,13 +307,13 @@ def tile_amortised_ivector_shrinkage_k3_kernel(
                 weight_pass(n, g)
             later[:count] = []
 
-        take_later(len(later) - sum(HELD))
+        take_later(len(later) - HELD)
 
         for g in range(GROUPS - 2):
-            quantize_v(g, interleave_v(g))
+            quantize_v(g, interleave_v(g, VECTOR_COLS))
         for n in range(COPIED):
             nc.scalar.copy(out=est_sb[:, n, :], in_=est[n][:])
-        last_groups = [(g, interleave_v(g)) for g in range(GROUPS - 2, GROUPS)]
+        last_groups = [(GROUPS - 2, interleave_v(GROUPS - 2, R)), (GROUPS - 1, interleave_v(GROUPS - 1, VECTOR_COLS))]
         for g, grouped in last_groups:
             quantize_v(g, grouped)
         nc.vector.transpose(frames_cols[:], frames_rows[:])
@@ -320,21 +323,25 @@ def tile_amortised_ivector_shrinkage_k3_kernel(
             for n in range(COPIED):
                 for g in groups:
                     z_pass(woven[n], n, g)
-        take_later(HELD[0])
+        take_later(HELD)
 
         blocks, gates = {}, {n: gate(woven[n], n) for n in range(COPIED)}
-        for n in range(TURNED - 1):
-            if n >= COPIED:
-                gates[n] = logits_and_gate(n)
-                if n <= len(HELD):
-                    take_later(HELD[n - 1])
-            if n > 1:
-                stage(n - 2, blocks[n - 2])
+        for n in range(COPIED):
             product(n, gates[n])
             store_y(n, n + 1)
-            if n > 0:
-                blocks[n - 1] = turn_blocks(n - 1)
-            round_to_blocks(n)
+        for n in range(COPIED - 1):
+            round_to_blocks(n, nc.scalar.copy)
+        blocks[0] = turn_blocks(0)
+        round_to_blocks(COPIED - 1, nc.vector.tensor_copy)
+        blocks[1] = turn_blocks(1)
+        for n in range(COPIED, TURNED - 1):
+            gates[n] = logits_and_gate(n)
+            for m in range(0 if n == COPIED else n - 2, n - 1):
+                stage(m, blocks[m])
+            product(n, gates[n])
+            store_y(n, n + 1)
+            blocks[n - 1] = turn_blocks(n - 1)
+            round_to_blocks(n, nc.vector.tensor_copy)
         n = TURNED - 1
         gates[n] = logits_and_gate(n)
         stage(n - 2, blocks[n - 2])

@@ -23,16 +23,16 @@ LAST = TILES - 1
 HALF = R // 2
 FULL = 3
 FRONT = 6
-HELD = 4
+HELD = 3
 COPIED = 3
 TURNED = 6
 SETTLED = 4
 PACKED = 4
-FIRST_TILES = 2
+FIRST_TILES = 1
 VECTOR_COLS = 320
 WARM_N = 128
-WARM_FREE = 11
-WARM_CODES = 1
+WARM_WORDS = 32
+WARM_FREE = 9
 
 
 def tile_amortised_ivector_shrinkage_k3_kernel(
@@ -63,7 +63,7 @@ def tile_amortised_ivector_shrinkage_k3_kernel(
         frames_rows = keep.tile([P, 32], BF16, align_bytes=64)
         frames_cols = keep.tile([P, 32], BF16, align_bytes=64)
         identity = keep.tile([P, P], F32, align_bytes=256)
-        warm_in = keep.tile([P, 4 * WARM_N], BF16, align_bytes=256)
+        warm_in = keep.tile([P, 4 * WARM_WORDS], BF16, align_bytes=256)
         warm_codes = keep.tile([P, WARM_N], U32, align_bytes=256)
         warm_plane = keep.tile([P, WARM_N], U8, align_bytes=256)
         warm_act = keep.tile([P, 1], F32)
@@ -227,7 +227,11 @@ def tile_amortised_ivector_shrinkage_k3_kernel(
             queue.dma_start(out=dst.bitcast(I32), in_=y_codes[:, P * n0 : P * n1].bitcast(I32))
 
         nc.gpsimd.memset(warm_in[:].bitcast(I32), 0x3F803F80)
-        nc.vector.quantize_mx(out=warm_codes[:].bitcast(FP8X4), scales=warm_plane[:], in_=warm_in[:])
+        nc.vector.memset(warm_codes[:, WARM_WORDS:], 0)
+        nc.vector.memset(warm_plane[:, WARM_WORDS:].bitcast(I32), 0)
+        nc.vector.quantize_mx(
+            out=warm_codes[:, :WARM_WORDS].bitcast(FP8X4), scales=warm_plane[:, :WARM_WORDS], in_=warm_in[:]
+        )
         nc.vector.memset(frames_rows[:], 0.0)
 
         for half, queue in enumerate((nc.sync, nc.scalar)):
@@ -237,22 +241,22 @@ def tile_amortised_ivector_shrinkage_k3_kernel(
         load_t(0, 1)
         load_f(0, 0, FIRST_TILES, nc.scalar)
         nc.scalar.activation(out=warm_act[:], in_=warm_in[:, 0:1], func=SIGMOID)
-        load_f(0, FIRST_TILES, 2 * FIRST_TILES)
-        load_f(0, 2 * FIRST_TILES, TILES)
-        load_a(0)
+        load_f(0, FIRST_TILES, TILES // 2)
+        load_f(0, TILES // 2, TILES)
         for q in range(4):
             nc.sync.dma_start(
                 out=a_packed_planes[32 * q : 32 * q + 4 * PACKED, 0, :].bitcast(I32),
                 in_=a_scales[0:PACKED, 4 * q : 4 * q + 4, :].bitcast(I32),
             )
+        load_a(0)
         load_f(1, 0, TILES // 2)
         load_scales(f_second_plane, f_scales, 1, 2)
         load_a(1)
         load_f(1, TILES // 2, TILES)
         load_t(1, 2)
         load_scales(t_late_planes, t_scales, 1, GROUPS)
-        load_f(2, 0, TILES // 2)
         load_scales(f_late_planes, f_scales, 2, GROUPS)
+        load_f(2, 0, TILES // 2)
         load_a(2)
         load_f(2, TILES // 2, TILES)
         load_t(2, 3)
@@ -280,12 +284,12 @@ def tile_amortised_ivector_shrinkage_k3_kernel(
         make_identity(nc, identity[:], nomemset=True)
 
         warm = bank(LAST, [P, WARM_N])
-        free = (warm_codes[:, 0:P], warm_plane[:, 0:P])
-        with_codes = (f_full[0][:, 0:P], warm_plane[:, 0:P])
-        for held, held_plane in [free] * WARM_FREE + [with_codes] * WARM_CODES:
+        free = (warm_plane[:], warm_plane[:])
+        with_planes = (f_staged[:, 0, 0:P], t_staged[:, 0, 0:WARM_N])
+        for held_plane, moving_plane in [free] * WARM_FREE + [with_planes]:
             nc.tensor.matmul_mx(
-                out=warm[:], lhsT=held.bitcast(FP8X4), lhsT_scale=held_plane,
-                rhs=warm_codes[:].bitcast(FP8X4), rhs_scale=warm_plane[:], start=True, stop=True,
+                out=warm[:], lhsT=warm_codes[:].bitcast(FP8X4), lhsT_scale=held_plane,
+                rhs=warm_codes[:].bitcast(FP8X4), rhs_scale=moving_plane, start=True, stop=True,
             )
 
         est = [bank(n, [P, R]) for n in range(LAST)]

@@ -17,6 +17,9 @@ SIGMOID = mybir.ActivationFunctionType.Sigmoid
 MULT = mybir.AluOpType.mult
 
 P = 128
+REGION = 32768
+WIDTH = {F32: 4, U32: 4, BF16: 2, U8: 1}
+V_ROW = 8
 GROUPS = K // 512
 TILES = U // P
 LAST = TILES - 1
@@ -45,35 +48,45 @@ def tile_amortised_ivector_shrinkage_k3_kernel(
         psum = ctx.enter_context(tc.psum_pool(name="psum", bufs=1))
         ctx.enter_context(tc.manual_schedule())
 
-        f_full = [keep.tile([P, U], U32, align_bytes=256, name="f_full%d" % g) for g in range(FULL)]
-        f_front = keep.tile([P, GROUPS - FULL, P * FRONT], U32, align_bytes=256)
-        f_back = keep.tile([P, GROUPS - FULL, U - P * FRONT], U32, align_bytes=256)
-        t_codes = keep.tile([P, GROUPS, 2 * R], U8, align_bytes=256)
-        a_codes = keep.tile([P, GROUPS, R], U32, align_bytes=256)
-        v_codes = keep.tile([P, GROUPS, R], U32, align_bytes=256)
-        f_staged = keep.tile([P, 2, U], U8, align_bytes=256)
-        t_staged = keep.tile([P, 2, R], U8, align_bytes=256)
-        f_second_plane = keep.tile([P, 1, U], U8, align_bytes=256)
-        f_late_planes = keep.tile([P, GROUPS - 2, U], U8, align_bytes=256)
-        t_late_planes = keep.tile([P, GROUPS - 1, R], U8, align_bytes=256)
-        a_packed_planes = keep.tile([P, 1, R], U8, align_bytes=256)
-        a_last_plane = keep.tile([P, 1, R], U8, align_bytes=256)
-        v_planes = keep.tile([P, GROUPS, R], U8, align_bytes=256)
-        v_rows = [keep.tile([P, 4, R], BF16, align_bytes=256, name="v_rows%d" % g) for g in range(GROUPS)]
-        frames_rows = keep.tile([P, 32], BF16, align_bytes=64)
-        frames_cols = keep.tile([P, 32], BF16, align_bytes=64)
-        identity = keep.tile([P, P], F32, align_bytes=256)
-        warm_in = keep.tile([P, 4 * WARM_WORDS], BF16, align_bytes=256)
-        warm_codes = keep.tile([P, WARM_N], U32, align_bytes=256)
-        warm_plane = keep.tile([P, WARM_N], U8, align_bytes=256)
-        warm_act = keep.tile([P, 1], F32)
-        est_sb = keep.tile([P, COPIED, R], F32, align_bytes=256)
-        pairs = keep.tile([P, TILES, 2, P, 2], BF16, align_bytes=256)
-        y = keep.tile([P, TILES, R], F32, align_bytes=256)
-        staged = keep.tile([P, TURNED // 2, 4, 2, 64], F32, align_bytes=256)
-        landed = keep.tile([P, TURNED, 4, 64], F32, align_bytes=256)
-        y_codes = keep.tile([P, U], U32, align_bytes=256)
-        y_plane = keep.tile([P, U], U8, align_bytes=256)
+        ends = [REGION * i for i in range(7)]
+
+        def placed(region, shape, dtype, name):
+            size = WIDTH[dtype]
+            for extent in shape[1:]:
+                size = size * extent
+            start = ends[region]
+            ends[region] = start + -(-size // 256) * 256
+            return keep.tile(shape, dtype, align_bytes=256, offset=start, name=name)
+
+        f_full = [placed(0, [P, U], U32, "f_full%d" % g) for g in range(FULL)]
+        f_front = placed(0, [P, GROUPS - FULL, P * FRONT], U32, "f_front")
+        f_back = placed(0, [P, GROUPS - FULL, U - P * FRONT], U32, "f_back")
+        t_codes = placed(2, [P, GROUPS, 2 * R], U8, "t_codes")
+        a_codes = placed(2, [P, GROUPS, R], U32, "a_codes")
+        v_codes = placed(2, [P, GROUPS, R], U32, "v_codes")
+        f_staged = placed(4, [P, 2, U], U8, "f_staged")
+        t_staged = placed(6, [P, 2, R], U8, "t_staged")
+        f_second_plane = placed(4, [P, 1, U], U8, "f_second_plane")
+        f_late_planes = placed(4, [P, GROUPS - 2, U], U8, "f_late_planes")
+        t_late_planes = placed(6, [P, GROUPS - 1, R], U8, "t_late_planes")
+        a_packed_planes = placed(6, [P, 1, R], U8, "a_packed_planes")
+        a_last_plane = placed(6, [P, 1, R], U8, "a_last_plane")
+        v_planes = placed(6, [P, GROUPS, R], U8, "v_planes")
+        v_rows = [placed(1, [P, 4, R], BF16, "v_rows%d" % g) for g in range(GROUPS)]
+        frames_rows = placed(1, [P, 32], BF16, "frames_rows")
+        frames_cols = placed(1, [P, 32], BF16, "frames_cols")
+        identity = placed(1, [P, P], F32, "identity")
+        warm_in = placed(1, [P, 4 * WARM_WORDS], BF16, "warm_in")
+        warm_codes = placed(2, [P, WARM_N], U32, "warm_codes")
+        warm_plane = placed(6, [P, WARM_N], U8, "warm_plane")
+        warm_act = placed(1, [P, 1], F32, "warm_act")
+        est_sb = placed(1, [P, COPIED, R], F32, "est_sb")
+        pairs = placed(3, [P, TILES, 2, P, 2], BF16, "pairs")
+        y = placed(3, [P, TILES, R], F32, "y")
+        staged = placed(5, [P, TURNED // 2, 4, 2, 64], F32, "staged")
+        landed = placed(5, [P, TURNED, 4, 64], F32, "landed")
+        y_codes = placed(5, [P, U], U32, "y_codes")
+        y_plane = placed(5, [P, U], U8, "y_plane")
 
         def bank(b, shape):
             return psum.tile(shape, F32, name="bank%d" % b, tag="bank%d" % b)
@@ -163,12 +176,12 @@ def tile_amortised_ivector_shrinkage_k3_kernel(
         def quantize_v(g, grouped):
             nc.vector.quantize_mx(
                 out=v_codes[:, g, :].bitcast(FP8X4),
-                scales=v_planes[:, g, :],
+                scales=v_planes[V_ROW:P, g, :],
                 in_=grouped[:].rearrange("p n t -> p (n t)"),
             )
 
         def z_pass(z, n, g):
-            mx_pass(z[:], n, g, v_codes[:, g, :].bitcast(FP8X4), v_planes[:, g, :], g == 0, g == GROUPS - 1)
+            mx_pass(z[:], n, g, v_codes[:, g, :].bitcast(FP8X4), v_planes[V_ROW:P, g, :], g == 0, g == GROUPS - 1)
 
         def gate(z, n):
             sig = ring.tile([P, R], F32, align_bytes=256, name="sig")
@@ -385,7 +398,7 @@ def tile_amortised_ivector_shrinkage_k3_kernel(
 
         half_products(0, [slice(0, 2)])
 
-        joined = {n: keep.tile([P, P, 2], F32, align_bytes=256, name="joined%d" % n) for n in range(TURNED, TILES)}
+        joined = {n: placed(5, [P, P, 2], F32, "joined%d" % n) for n in range(TURNED, TILES)}
         turned = {n: bank(n - 2, [P, 2, P]) for n in range(TURNED, TILES)}
         half_products(1, [slice(0, 1), slice(1, 2)])
         store_y(LAST, TILES)

from contextlib import ExitStack

import concourse.mybir as mybir
from concourse.masks import make_identity

U, K, R = 1024, 2560, 512
FLOPS = 3 * 2 * U * K * R

F32 = mybir.dt.float32
BF16 = mybir.dt.bfloat16
I32 = mybir.dt.int32
U32 = mybir.dt.uint32
U8 = mybir.dt.uint8
FP8X4 = mybir.dt.float8_e4m3fn_x4
FP4X4 = mybir.dt.float4_e2m1fn_x4
SIGMOID = mybir.ActivationFunctionType.Sigmoid
MULT = mybir.AluOpType.mult

P = 128
REGION = 32768
WIDTH = {F32: 4, U32: 4, BF16: 2, U8: 1}
V_ROW = 8
GROUPS = K // 512
TILES = U // P
LAST = TILES - 1
HALF = R // 2
FULL = 3
FRONT = 6
HELD = 3
COPIED = 3
TURNED = 6
SETTLED = 4
PACKED = 4
FIRST_TILES = 1
VECTOR_COLS = 320
WARM_N = 128
WARM_WORDS = 32
WARM_FREE = 9


def tile_amortised_ivector_shrinkage_k3_kernel(
    tc, f_words, f_scales, t_words, t_scales, a_words, a_scales, v, log_frames, out_0, out_1, out_2
):
    nc = tc.nc
    with ExitStack() as ctx:
        keep = ctx.enter_context(tc.tile_pool(name="keep", bufs=1))
        ring = ctx.enter_context(tc.tile_pool(name="ring", bufs=3))
        psum = ctx.enter_context(tc.psum_pool(name="psum", bufs=1))
        ctx.enter_context(tc.manual_schedule())

        ends = [REGION * i for i in range(7)]

        def placed(region, shape, dtype, name):
            size = WIDTH[dtype]
            for extent in shape[1:]:
                size = size * extent
            start = ends[region]
            ends[region] = start + -(-size // 256) * 256
            return keep.tile(shape, dtype, align_bytes=256, offset=start, name=name)

        f_full = [placed(0, [P, U], U32, "f_full%d" % g) for g in range(FULL)]
        f_front = placed(0, [P, GROUPS - FULL, P * FRONT], U32, "f_front")
        f_back = placed(0, [P, GROUPS - FULL, U - P * FRONT], U32, "f_back")
        t_codes = placed(2, [P, GROUPS, 2 * R], U8, "t_codes")
        a_codes = placed(2, [P, GROUPS, R], U32, "a_codes")
        v_codes = placed(2, [P, GROUPS, R], U32, "v_codes")
        f_staged = placed(4, [P, 2, U], U8, "f_staged")
        t_staged = placed(6, [P, 2, R], U8, "t_staged")
        f_second_plane = placed(4, [P, 1, U], U8, "f_second_plane")
        f_late_planes = placed(4, [P, GROUPS - 2, U], U8, "f_late_planes")
        t_late_planes = placed(6, [P, GROUPS - 1, R], U8, "t_late_planes")
        a_packed_planes = placed(6, [P, 1, R], U8, "a_packed_planes")
        a_last_plane = placed(6, [P, 1, R], U8, "a_last_plane")
        v_planes = placed(6, [P, GROUPS, R], U8, "v_planes")
        v_rows = [placed(1, [P, 4, R], BF16, "v_rows%d" % g) for g in range(GROUPS)]
        frames_rows = placed(1, [P, 32], BF16, "frames_rows")
        frames_cols = placed(1, [P, 32], BF16, "frames_cols")
        identity = placed(1, [P, P], F32, "identity")
        warm_in = placed(1, [P, 4 * WARM_WORDS], BF16, "warm_in")
        warm_codes = placed(2, [P, WARM_N], U32, "warm_codes")
        warm_plane = placed(6, [P, WARM_N], U8, "warm_plane")
        warm_act = placed(1, [P, 1], F32, "warm_act")
        est_sb = placed(1, [P, COPIED, R], F32, "est_sb")
        pairs = placed(3, [P, TILES, 2, P, 2], BF16, "pairs")
        y = placed(3, [P, TILES, R], F32, "y")
        staged = placed(5, [P, TURNED // 2, 4, 2, 64], F32, "staged")
        landed = placed(5, [P, TURNED, 4, 64], F32, "landed")
        y_codes = placed(5, [P, U], U32, "y_codes")
        y_plane = placed(5, [P, U], U8, "y_plane")

        def bank(b, shape):
            return psum.tile(shape, F32, name="bank%d" % b, tag="bank%d" % b)

        def load_staged(staged_plane, scales, g, half, queue):
            rows = scales[g, 8 * half : 8 * half + 8, :].rearrange("(s r) n -> r s n", r=4)
            dst = staged_plane[64 * half : 64 * half + 4, :, :]
            queue.dma_start(out=dst.bitcast(I32), in_=rows.bitcast(I32))

        def lift(staged_plane, half, c0, c1):
            nc.vector.tensor_copy(
                out=staged_plane[64 * half + 32 : 64 * half + 36, 0, c0:c1].bitcast(I32),
                in_=staged_plane[64 * half : 64 * half + 4, 1, c0:c1].bitcast(I32),
            )

        def load_scales(planes, scales, g0, g1, first=0):
            rows = scales.rearrange("g (q r) n -> r q g n", r=4)
            for r in range(4):
                dst = planes[first + r : P : 32, :, :]
                nc.sync.dma_start(out=dst.bitcast(I32), in_=rows[r][:, g0:g1, :].bitcast(I32))

        def load_f(g, n0, n1, queue=nc.sync):
            src = f_words[g].rearrange("p n t -> p (n t)")[:, 4 * P * n0 : 4 * P * n1]
            dst = f_full[g][:, P * n0 : P * n1] if g < FULL else f_front[:, g - FULL, P * n0 : P * n1]
            queue.dma_start(out=dst.bitcast(I32), in_=src.bitcast(I32))

        def load_t(g0, g1):
            src = t_words[g0:g1].rearrange("g p n -> p g n")
            nc.sync.dma_start(out=t_codes[:, g0:g1, :].bitcast(I32), in_=src.bitcast(I32))

        def load_a(g):
            src = a_words[g].rearrange("p n t -> p (n t)")
            nc.sync.dma_start(out=a_codes[:, g, :].bitcast(I32), in_=src.bitcast(I32))

        def load_v(g):
            src = v[512 * g : 512 * (g + 1), :].rearrange("(p t) n -> p t n", t=4)
            nc.sync.dma_start(out=v_rows[g][:], in_=src)

        def mx_pass(acc, n, g, codes, plane, start, stop):
            if g < FULL:
                held = f_full[g][:, P * n : P * (n + 1)]
            elif n < FRONT:
                held = f_front[:, g - FULL, P * n : P * (n + 1)]
            else:
                held = f_back[:, g - FULL, P * (n - FRONT) : P * (n - FRONT + 1)]
            held_plane = (f_staged, f_second_plane)[g][:, 0, :] if g < 2 else f_late_planes[:, g - 2, :]
            nc.tensor.matmul_mx(
                out=acc,
                lhsT=held.bitcast(FP8X4),
                lhsT_scale=held_plane[:, P * n : P * (n + 1)],
                rhs=codes,
                rhs_scale=plane,
                start=start,
                stop=stop,
            )

        def t_part(acc, n, g, start, c0, c1):
            plane = t_staged[:, 0, c0:c1] if g == 0 else t_late_planes[:, g - 1, c0:c1]
            mx_pass(acc, n, g, t_codes[:, g, 2 * c0 : 2 * c1].bitcast(FP4X4), plane, start, False)

        def a_part(acc, n, g, c0, c1):
            plane = a_packed_planes[4 * g : P, 0, c0:c1] if g < PACKED else a_last_plane[4:P, 0, c0:c1]
            mx_pass(acc, n, g, a_codes[:, g, c0:c1].bitcast(FP8X4), plane, False, g == GROUPS - 1)

        def t_pass(n, g):
            t_part(est[n][:], n, g, g == 0, 0, R)

        def a_pass(n, g):
            a_part(est[n][:], n, g, 0, R)

        def t_half(k, g):
            t_part(halves[k][:], LAST, g, g == 0, HALF * k, HALF * (k + 1))

        def a_half(k, g):
            a_part(halves[k][:], LAST, g, HALF * k, HALF * (k + 1))

        def interleave_v(g, vector_cols):
            grouped = ring.tile([P, R, 4], BF16, align_bytes=256, name="v_grouped")
            src = v_rows[g][:].rearrange("p t (c i) -> p c t i", i=4)
            dst = grouped[:].rearrange("p (c i) t -> p c t i", i=4)
            split = vector_cols // 4
            nc.vector.tensor_copy(out=dst[:, :split], in_=src[:, :split])
            if vector_cols < R:
                nc.scalar.copy(out=dst[:, split:], in_=src[:, split:])
            return grouped

        def quantize_v(g, grouped):
            nc.vector.quantize_mx(
                out=v_codes[:, g, :].bitcast(FP8X4),
                scales=v_planes[V_ROW:P, g, :],
                in_=grouped[:].rearrange("p n t -> p (n t)"),
            )

        def z_pass(z, n, g):
            mx_pass(z[:], n, g, v_codes[:, g, :].bitcast(FP8X4), v_planes[V_ROW:P, g, :], g == 0, g == GROUPS - 1)

        def gate(z, n):
            sig = ring.tile([P, R], F32, align_bytes=256, name="sig")
            nc.scalar.activation(out=sig[:], in_=z[:], func=SIGMOID, bias=frames_cols[:, 4 * n : 4 * n + 1])
            return sig

        def logits_and_gate(n):
            z = bank(n % COPIED, [P, R])
            for g in range(GROUPS):
                z_pass(z, n, g)
            return gate(z, n)

        def product(n, sig):
            src = est_sb[:, n, :] if n < COPIED else est[n][:]
            nc.vector.tensor_tensor(out=y[:, n, :], in0=src, in1=sig[:], op=MULT)

        def store_y(n0, n1):
            rows = out_0[P * n0 : P * n1, :].rearrange("(n p) r -> p n r", p=P)
            nc.sync.dma_start(out=rows, in_=y[:, n0:n1, :])

        def by_pairs(ap):
            return ap.rearrange("u (p h e) -> u h p e", h=2, e=2)

        def by_blocks(ap):
            return ap.rearrange("u (i b e) -> u b i e", b=8, e=2)

        def block_words(n):
            return pairs[:, n].rearrange("u h p e -> u (h p e)").rearrange("u (b i e) -> u b i e", b=8, e=2)

        def round_to_blocks(n, copy):
            copy(out=block_words(n), in_=by_blocks(y[:, n, :]))

        def turn_blocks(n):
            blocks = ring.tile([P, 2 * P], F32, align_bytes=256, name="blocks")
            nc.vector.transpose(blocks[:], pairs[:, n].rearrange("u h p e -> u (h p e)").bitcast(F32))
            return blocks

        def stage(n, blocks):
            nc.scalar.copy(
                out=staged[:, n // 2, :, n % 2, :].rearrange("p q (j h) -> p q j h", h=2),
                in_=blocks[:].rearrange("p (q h j) -> p q j h", h=2, q=4),
            )
            if n % 2 == 1:
                for a in (0, 2, 1, 3):
                    nc.sync.dma_start(out=landed[:, n - 1 : n + 1, a, :], in_=staged[32 * a : 32 * a + 32, n // 2])

        def quantize_landed(n0, n1):
            quantize_y(n0, n1, landed[:, n0:n1].rearrange("p n a w -> p (n a w)"))

        def quantize_y(n0, n1, words):
            cols = slice(P * n0, P * n1)
            nc.vector.quantize_mx(out=y_codes[:, cols].bitcast(FP8X4), scales=y_plane[:, cols], in_=words.bitcast(BF16))

        def store_words(n0, n1, queue):
            dst = out_1[0].rearrange("p u t -> p (u t)")[:, 4 * P * n0 : 4 * P * n1]
            queue.dma_start(out=dst.bitcast(I32), in_=y_codes[:, P * n0 : P * n1].bitcast(I32))

        nc.gpsimd.memset(warm_in[:].bitcast(I32), 0x3F803F80)
        nc.vector.memset(warm_codes[:, WARM_WORDS:], 0)
        nc.vector.memset(warm_plane[:, WARM_WORDS:].bitcast(I32), 0)
        nc.vector.quantize_mx(
            out=warm_codes[:, :WARM_WORDS].bitcast(FP8X4), scales=warm_plane[:, :WARM_WORDS], in_=warm_in[:]
        )
        nc.vector.memset(frames_rows[:], 0.0)

        for half, queue in enumerate((nc.sync, nc.scalar)):
            load_staged(t_staged, t_scales, 0, half, queue)
        for half, queue in enumerate((nc.sync, nc.scalar)):
            load_staged(f_staged, f_scales, 0, half, queue)
        load_t(0, 1)
        load_f(0, 0, FIRST_TILES, nc.scalar)
        nc.scalar.activation(out=warm_act[:], in_=warm_in[:, 0:1], func=SIGMOID)
        load_f(0, FIRST_TILES, TILES // 2)
        load_f(0, TILES // 2, TILES)
        for q in range(4):
            nc.sync.dma_start(
                out=a_packed_planes[32 * q : 32 * q + 4 * PACKED, 0, :].bitcast(I32),
                in_=a_scales[0:PACKED, 4 * q : 4 * q + 4, :].bitcast(I32),
            )
        load_a(0)
        load_f(1, 0, TILES // 2)
        load_scales(f_second_plane, f_scales, 1, 2)
        load_a(1)
        load_f(1, TILES // 2, TILES)
        load_t(1, 2)
        load_scales(t_late_planes, t_scales, 1, GROUPS)
        load_scales(f_late_planes, f_scales, 2, GROUPS)
        load_f(2, 0, TILES // 2)
        load_a(2)
        load_f(2, TILES // 2, TILES)
        load_t(2, 3)
        load_v(0)
        load_f(3, 0, FRONT)
        load_a(3)
        load_v(1)
        load_t(3, GROUPS)
        load_v(2)
        load_f(4, 0, FRONT)
        load_scales(a_last_plane, a_scales, PACKED, GROUPS, first=4)
        load_a(4)
        load_v(3)
        load_v(4)
        nc.sync.dma_start(out=frames_rows[0:P:4, :], in_=log_frames.rearrange("(n q j) -> q n j", q=4, j=32))
        back = f_words[FULL:GROUPS].rearrange("g p n t -> p g (n t)")[:, :, 4 * P * FRONT :]
        nc.sync.dma_start(out=f_back[:].bitcast(I32), in_=back.bitcast(I32))

        for half in range(2):
            lift(t_staged, half, 0, R)
        for c0, c1 in ((0, P * FIRST_TILES), (P * FIRST_TILES, U)):
            for half in range(2):
                lift(f_staged, half, c0, c1)
        nc.vector.memset(identity[:], 0.0)
        make_identity(nc, identity[:], nomemset=True)

        warm = bank(LAST, [P, WARM_N])
        free = (warm_plane[:], warm_plane[:])
        with_planes = (f_staged[:, 0, 0:P], t_staged[:, 0, 0:WARM_N])
        for held_plane, moving_plane in [free] * WARM_FREE + [with_planes]:
            nc.tensor.matmul_mx(
                out=warm[:], lhsT=warm_codes[:].bitcast(FP8X4), lhsT_scale=held_plane,
                rhs=warm_codes[:].bitcast(FP8X4), rhs_scale=moving_plane, start=True, stop=True,
            )

        est = [bank(n, [P, R]) for n in range(LAST)]
        halves = [bank(LAST, [P, HALF])]
        for g in range(FULL):
            weights = ((t_pass, t_half), (a_pass, a_half))
            for weight_pass, weight_half in weights if g == 0 else reversed(weights):
                for n in range(LAST):
                    weight_pass(n, g)
                weight_half(0, g)
        later = [(weight_pass, n, FULL) for weight_pass in (a_pass, t_pass) for n in range(FRONT)]
        later += [(weight_pass, n, GROUPS - 1) for weight_pass in (t_pass, a_pass) for n in range(COPIED)]
        later += [(weight_pass, n, GROUPS - 1) for n in range(COPIED, FRONT) for weight_pass in (t_pass, a_pass)]
        for n in range(FRONT, TURNED):
            later += [(weight_pass, n, g) for g in range(FULL, GROUPS) for weight_pass in (t_pass, a_pass)]

        def take_later(count):
            for weight_pass, n, g in later[:count]:
                weight_pass(n, g)
            later[:count] = []

        take_later(len(later) - HELD)

        for g in range(GROUPS - 2):
            quantize_v(g, interleave_v(g, VECTOR_COLS))
        for n in range(COPIED):
            nc.scalar.copy(out=est_sb[:, n, :], in_=est[n][:])
        last_groups = [(GROUPS - 2, interleave_v(GROUPS - 2, R)), (GROUPS - 1, interleave_v(GROUPS - 1, VECTOR_COLS))]
        for g, grouped in last_groups:
            quantize_v(g, grouped)
        nc.vector.transpose(frames_cols[:], frames_rows[:])

        woven = [bank(n, [P, R]) for n in range(COPIED)]
        for groups in (range(GROUPS - 2), (GROUPS - 2,), (GROUPS - 1,)):
            for n in range(COPIED):
                for g in groups:
                    z_pass(woven[n], n, g)
        take_later(HELD)

        blocks, gates = {}, {n: gate(woven[n], n) for n in range(COPIED)}
        for n in range(COPIED):
            product(n, gates[n])
            store_y(n, n + 1)
        for n in range(COPIED - 1):
            round_to_blocks(n, nc.scalar.copy)
        blocks[0] = turn_blocks(0)
        round_to_blocks(COPIED - 1, nc.vector.tensor_copy)
        blocks[1] = turn_blocks(1)
        for n in range(COPIED, TURNED - 1):
            gates[n] = logits_and_gate(n)
            for m in range(0 if n == COPIED else n - 2, n - 1):
                stage(m, blocks[m])
            product(n, gates[n])
            store_y(n, n + 1)
            blocks[n - 1] = turn_blocks(n - 1)
            round_to_blocks(n, nc.vector.tensor_copy)
        n = TURNED - 1
        gates[n] = logits_and_gate(n)
        stage(n - 2, blocks[n - 2])
        nc.vector.tensor_tensor(out=block_words(n), in0=by_blocks(est[n][:]), in1=by_blocks(gates[n][:]), op=MULT)
        blocks[n - 1] = turn_blocks(n - 1)
        blocks[n] = turn_blocks(n)
        product(n, gates[n])
        stage(n - 1, blocks[n - 1])
        gates[TURNED] = logits_and_gate(TURNED)
        stage(n, blocks[n])
        store_y(n, n + 1)
        for g in range(FULL, GROUPS):
            t_pass(TURNED, g)
            a_pass(TURNED, g)
        quantize_landed(0, 2)
        product(TURNED, gates[TURNED])
        store_y(TURNED, LAST)
        quantize_landed(2, SETTLED)
        store_words(0, SETTLED, nc.sync)

        gates[LAST] = logits_and_gate(LAST)
        nc.scalar.copy(out=pairs[:, TURNED], in_=by_pairs(y[:, TURNED, :]))
        halves.append(bank(COPIED, [P, HALF]))
        for k in range(2):
            for g in range(FULL if k == 0 else 0, GROUPS):
                t_half(k, g)
                a_half(k, g)

        def half_products(k, parts):
            cols = slice(HALF * k, HALF * (k + 1))
            dst = pairs[:, LAST, :, P // 2 * k : P // 2 * (k + 1), :]
            for h in parts:
                nc.vector.tensor_tensor(
                    out=dst[:, h], in0=by_pairs(halves[k][:])[:, h], in1=by_pairs(gates[LAST][:, cols])[:, h], op=MULT
                )
            nc.vector.tensor_tensor(out=y[:, LAST, cols], in0=halves[k][:], in1=gates[LAST][:, cols], op=MULT)

        half_products(0, [slice(0, 2)])

        joined = {n: placed(5, [P, P, 2], F32, "joined%d" % n) for n in range(TURNED, TILES)}
        turned = {n: bank(n - 2, [P, 2, P]) for n in range(TURNED, TILES)}
        half_products(1, [slice(0, 1), slice(1, 2)])
        store_y(LAST, TILES)
        quantize_landed(SETTLED, TURNED)
        for n in range(TURNED, TILES):
            for h in range(2):
                words = pairs[:, n, h].rearrange("u p e -> u (p e)").bitcast(F32)
                nc.tensor.transpose(turned[n][:, h, :], words, identity[:])
        for n in range(TURNED, TILES):
            nc.scalar.copy(out=joined[n][:], in_=turned[n][:].rearrange("p h u -> p u h"))
            quantize_y(n, n + 1, joined[n][:].rearrange("p u h -> p (u h)"))
            if n == TURNED:
                store_words(SETTLED, LAST, nc.sync)
        store_words(LAST, TILES, nc.scalar)
        scale_rows = out_2[0].rearrange("(q r) u -> r q u", r=4)
        for r, queue in enumerate((nc.sync, nc.sync, nc.scalar, nc.sync)):
            queue.dma_start(out=scale_rows[r].bitcast(I32), in_=y_plane[r:P:32, :].bitcast(I32))
